import numpy as np
import ml_dtypes


def mxq(x, axis, fmt="e4m3"):
    dtype, down = {"e4m3": (ml_dtypes.float8_e4m3fn, 7), "e5m2": (ml_dtypes.float8_e5m2, 14)}[fmt]
    v = np.moveaxis(np.asarray(x, np.float32).astype(ml_dtypes.bfloat16).astype(np.float64), axis, -1)
    blocks = v.reshape(v.shape[:-1] + (-1, 32))
    amax = np.abs(blocks).max(-1, keepdims=True)
    byte = np.maximum(np.where(amax > 0, np.frexp(amax)[1] - 1 + 127, 0) - down, 1)
    scale = np.exp2(byte - 127.0)
    codes = (blocks / scale).astype(np.float32).astype(dtype).astype(np.float64)
    return np.moveaxis((codes * scale).reshape(v.shape), -1, axis)


WIDE = False


def mx_kscale(k):
    if not WIDE:
        return np.ones(k)
    levels = np.array([18, -18])
    if k % 512:
        return np.exp2(np.random.permutation(np.resize(levels, k // 32))).repeat(32)
    a = np.empty((k // 512, 16))
    for p in range(k // 512):
        a[p, :8] = np.random.permutation(np.resize(levels, 8))
        for g in range(8):
            far = levels[np.abs(levels - a[p, g]) >= 10]
            a[p, g + 8] = far[np.random.randint(len(far))]
    return np.exp2(a.ravel()).repeat(32)


def f64(x):
    return np.asarray(x).astype(np.float64)


def striped(idx):
    return np.tile(np.asarray(idx).reshape(-1, 16).T, (8, 1)).astype(np.uint16)


def unstriped(offs):
    return offs[:16].T.reshape(-1).astype(np.int64)

def planes(y):
    n, m = y.shape
    v = y.astype(np.float32).astype(ml_dtypes.bfloat16).astype(np.float64).reshape(n // 32, 32, m)
    top = np.abs(v).max(1)
    byte = np.clip(np.where(top > 0, np.frexp(top)[1] - 1 + 127 - 7, 1), 1, 254)
    codes = (v * np.exp2(127.0 - byte)[:, None, :]).reshape(n, m).astype(np.float32).astype(ml_dtypes.float8_e4m3fn).view(np.uint8)
    words = codes.reshape(n // 512, 128, 4, m).transpose(0, 1, 3, 2)
    return np.ascontiguousarray(words), np.ascontiguousarray(byte.astype(np.uint8).reshape(n // 512, 16, m))


def setup_inputs():
    n = np.random.standard_normal
    uni = np.random.uniform
    hd = np.random.permutation(2048)[:512]
    rl = np.random.permutation(1024)[:512]
    idx = np.random.permutation(2048)[:512]
    f_r = mx_kscale(512)
    f_hd = np.ones(2048)
    f_hd[hd] = f_r
    f_rl = np.ones(1024)
    f_rl[rl] = f_r
    return {
        "hT": (np.round(n((512, 2048)) * 8) / 8).astype(np.float32),
        "rT": (np.round(n((512, 1024)) * 8) / 8 * f_rl[None, :]).astype(np.float32),
        "G": (n((512, 512)) / np.sqrt(512) / f_r[:, None]).astype(np.float32),
        "hoffs": striped(hd),
        "roffs": striped(rl),
        "offs": striped(idx),
    }


def reference(hT, rT, G, hoffs, roffs, offs):
    hd = unstriped(hoffs)
    rl = unstriped(roffs)
    idx = unstriped(offs)
    h_ = f64(hT)[:, hd]
    r_ = f64(rT)[:, rl]
    c = h_ * r_
    dt = mxq(c, 1, "e4m3") @ mxq(f64(G), 0, "e5m2")
    out_0 = np.zeros((512, 2048))
    out_0[:, idx] = dt
    return (out_0,) + planes(out_0)

@@ -1,0 +1,219 @@
+from contextlib import ExitStack
+
+import concourse.mybir as mybir
+from concourse.masks import make_identity
+
+F32 = mybir.dt.float32
+BF16 = mybir.dt.bfloat16
+U32 = mybir.dt.uint32
+I32 = mybir.dt.int32
+U16 = mybir.dt.uint16
+U8 = mybir.dt.uint8
+E4M3 = mybir.dt.float8_e4m3fn_x4
+E5M2 = mybir.dt.float8_e5m2_x4
+
+P = 128
+PACK = 4
+D = 512
+R = 512
+SLOTS = 512
+HEADS = 2048
+RELS = 1024
+TAILS = 2048
+CHUNK = 512
+FLOPS = 2 * D * R * SLOTS
+
+LANES = (2, 0, 1, 3)
+
+
+def tile_attend_gdistm_t_pl_kernel(tc, hT, rT, G, hoffs, roffs, offs, out_0, out_1, out_2):
+    nc = tc.nc
+    mult = mybir.AluOpType.mult
+    half = SLOTS // 2
+    chunks = TAILS // CHUNK
+
+    with ExitStack() as ctx:
+        lists = ctx.enter_context(tc.tile_pool(name="lists", bufs=1))
+        sb = ctx.enter_context(tc.tile_pool(name="sb", bufs=1))
+        ps = ctx.enter_context(tc.psum_pool(name="ps", bufs=1))
+
+        h_list = lists.tile([P, R // 16], U16, name="h_list")
+        r_list = lists.tile([P, R // 16], U16, name="r_list")
+        t_list = lists.tile([P, SLOTS // 16], U16, name="t_list")
+
+        h_rows = hT.rearrange("(p t) c -> p t c", t=PACK)
+        r_rows = rT.rearrange("(p t) c -> p t c", t=PACK)
+        g_rows = G.rearrange("(q t) i -> q t i", t=PACK)
+        out_rows = out_0.rearrange("(p t) c -> p t c", t=PACK)
+        out_words = out_1[0].rearrange("p c t -> p (c t)").bitcast(I32)
+        out_scales = out_2[0].bitcast(I32)
+
+        h_tab = [sb.tile([P, HEADS], F32, name="h_tab%d" % n) for n in range(PACK)]
+        r_tab = [sb.tile([P, RELS], F32, name="r_tab%d" % n) for n in range(PACK)]
+        g_raw = [sb.tile([P, PACK, half], F32, name="g_raw%d" % a) for a in range(2)]
+        window = [sb.tile([P, TAILS], F32, name="window%d" % n) for n in range(PACK)]
+
+        def load_tables(n):
+            nc.sync.dma_start(r_tab[n][:], r_rows[:, LANES[n], :])
+            nc.sync.dma_start(h_tab[n][:], h_rows[:, LANES[n], :])
+
+        nc.sync.dma_start(r_list[:], roffs)
+        nc.sync.dma_start(h_list[:], hoffs)
+        load_tables(0)
+        load_tables(1)
+        for a in range(2):
+            nc.sync.dma_start(g_raw[a][:], g_rows[:, :, a * half : (a + 1) * half])
+        nc.sync.dma_start(t_list[:], offs)
+        load_tables(2)
+        load_tables(3)
+
+        ident = sb.tile([P, P], F32, name="ident")
+        make_identity(nc, ident[:])
+        for n in range(PACK):
+            nc.vector.memset(window[n][:], 0.0)
+
+        r_got = [sb.tile([P, R], F32, name="r_got%d" % n) for n in range(PACK)]
+        c_rows = [sb.tile([P, R], F32, name="c_rows%d" % n) for n in range(PACK)]
+        c_codes = [sb.tile([P, P], U32, name="c_codes%d" % n, align_bytes=64) for n in range(PACK)]
+        c_scales = [sb.tile([P, P], U8, name="c_scales%d" % n, align_bytes=64) for n in range(PACK)]
+        turned = [ps.tile([P, PACK, P], F32, name="turned%d" % n) for n in range(PACK)]
+        acc = [ps.tile([P, SLOTS], F32, name="acc%d" % n) for n in range(PACK)]
+        g_codes = sb.tile([P, SLOTS], U32, name="g_codes", align_bytes=64)
+        g_scales = sb.tile([P, SLOTS], U8, name="g_scales", align_bytes=64)
+        pairs = [sb.tile([P, 2, CHUNK, 2], BF16, name="pairs%d" % k) for k in range(chunks)]
+        c_grouped = {}
+
+        def gather_r(n):
+            nc.vector.tensor_copy(r_got[n][:], r_tab[n][:].indirect(r_list[:]))
+
+        def gather_h(n):
+            nc.vector.tensor_tensor(c_rows[n][:], h_tab[n][:].indirect(h_list[:]), r_got[n][:], mult)
+
+        def turn(n):
+            for t in range(PACK):
+                nc.tensor.transpose(turned[n][:, t, :], c_rows[n][:, t:R:PACK], ident[:])
+            c_grouped[n] = sb.tile([P, P, PACK], BF16, name="c_grouped%d" % n, tag="c_grouped%d" % n, align_bytes=64)
+            nc.scalar.copy(c_grouped[n][:], turned[n][:].rearrange("q t p -> q p t"))
+
+        def multiply(n):
+            nc.vector.quantize_mx(
+                out=c_codes[n][:].bitcast(E4M3),
+                scales=c_scales[n][:],
+                in_=c_grouped[n][:].rearrange("q p t -> q (p t)"),
+            )
+            nc.tensor.matmul_mx(
+                out=acc[n][:],
+                lhsT=c_codes[n][:].bitcast(E4M3),
+                lhsT_scale=c_scales[n][:],
+                rhs=g_codes[:].bitcast(E5M2),
+                rhs_scale=g_scales[:],
+                start=True,
+                stop=True,
+            )
+
+        def fetch(n, lo, hi, tag):
+            dt = sb.tile([P, hi - lo], F32, name="dt%d_%d" % (n, lo), tag=tag, align_bytes=64)
+            nc.scalar.copy(dt[:], acc[n][:, lo:hi])
+            return dt
+
+        def scatter(n, dt, lo, hi):
+            nc.vector.tensor_copy(window[n][:].indirect(t_list[:, lo // 16 : hi // 16]), dt[:])
+
+        def store(n):
+            nc.sync.dma_start(out_rows[:, LANES[n], :], window[n][:])
+
+        def round_lane(n, k, on_vector=False):
+            dst = pairs[k][:, LANES[n] // 2, :, LANES[n] % 2]
+            src = window[n][:, k * CHUNK : (k + 1) * CHUNK]
+            if on_vector:
+                nc.vector.tensor_copy(dst, src)
+            else:
+                nc.scalar.copy(dst, src)
+
+        gather_r(0)
+        gather_h(0)
+        turn(0)
+        gather_r(1)
+        gather_h(1)
+        turn(1)
+
+        for a in range(2):
+            g_grouped = sb.tile([P, half, PACK], BF16, name="g_grouped%d" % a, align_bytes=64)
+            dst = g_grouped[:].rearrange("q (c i) t -> q c t i", i=4)
+            src = g_raw[a][:].rearrange("q t (c i) -> q c t i", i=4)
+            if a == 0:
+                nc.scalar.copy(dst, src)
+            else:
+                nc.vector.tensor_copy(dst, src)
+            nc.vector.quantize_mx(
+                out=g_codes[:, a * half : (a + 1) * half].bitcast(E5M2),
+                scales=g_scales[:, a * half : (a + 1) * half],
+                in_=g_grouped[:].rearrange("q c t -> q (c t)"),
+            )
+
+        multiply(0)
+        dt0 = fetch(0, 0, SLOTS, "dt_early")
+        multiply(1)
+        gather_r(2)
+        scatter(0, dt0, 0, SLOTS)
+        store(0)
+        gather_h(2)
+        turn(2)
+        dt1 = fetch(1, 0, SLOTS, "dt_early")
+        for k in range(chunks):
+            round_lane(0, k)
+        scatter(1, dt1, 0, SLOTS)
+        store(1)
+        gather_r(3)
+        multiply(2)
+        gather_h(3)
+        turn(3)
+        round_lane(1, 0)
+        round_lane(1, 1)
+        dt2a = fetch(2, 0, half, "dt_early")
+        scatter(2, dt2a, 0, half)
+        multiply(3)
+        dt2b = fetch(2, half, SLOTS, "c_grouped3")
+        dt3 = fetch(3, 0, SLOTS, "dt_last")
+        round_lane(1, 2)
+        round_lane(1, 3)
+        scatter(2, dt2b, half, SLOTS)
+        store(2)
+        for k in range(chunks):
+            round_lane(2, k)
+        scatter(3, dt3, 0, SLOTS)
+        store(3)
+
+        y_grouped = [sb.tile([P, CHUNK, PACK], BF16, name="y_grouped%d" % k, align_bytes=64) for k in range(chunks)]
+        y_codes = [sb.tile([P, CHUNK], U32, name="y_codes%d" % k, align_bytes=64) for k in range(chunks)]
+        y_scales = sb.tile([P, TAILS], U8, name="y_scales", align_bytes=64)
+
+        def weave(k, on_vector):
+            dst = y_grouped[k][:].rearrange("p c t -> p (c t)").bitcast(F32).rearrange("p (c u) -> p c u", u=2)
+            src = pairs[k][:].rearrange("p u c e -> p (u c e)").bitcast(F32).rearrange("p (u c) -> p c u", u=2)
+            if on_vector:
+                nc.vector.tensor_copy(dst, src)
+            else:
+                nc.scalar.copy(dst, src)
+
+        def quantize_planes(k):
+            nc.vector.quantize_mx(
+                out=y_codes[k][:].bitcast(E4M3),
+                scales=y_scales[:, k * CHUNK : (k + 1) * CHUNK],
+                in_=y_grouped[k][:].rearrange("p c t -> p (c t)"),
+            )
+            nc.sync.dma_start(out_words[:, k * CHUNK : (k + 1) * CHUNK], y_codes[k][:].bitcast(I32))
+
+        round_lane(3, 0, True)
+        round_lane(3, 1, True)
+        weave(0, True)
+        weave(1, True)
+        round_lane(3, 2)
+        weave(2, False)
+        round_lane(3, 3)
+        weave(3, False)
+        for k in range(chunks):
+            quantize_planes(k)
+        for q in range(4):
+            queue = nc.sync if q < 2 else nc.scalar
+            queue.dma_start(out_scales[4 * q : 4 * q + 4, :], y_scales[32 * q : 32 * q + 4, :].bitcast(I32))

@@ -35,6 +35,7 @@ def tile_attend_gdistm_t_pl_kernel(tc, hT, rT, G, hoffs, roffs, offs, out_0, out
     with ExitStack() as ctx:
         lists = ctx.enter_context(tc.tile_pool(name="lists", bufs=1))
         sb = ctx.enter_context(tc.tile_pool(name="sb", bufs=1))
+        reuse = ctx.enter_context(tc.tile_pool(name="reuse", bufs=1))
         ps = ctx.enter_context(tc.psum_pool(name="ps", bufs=1))
 
         h_list = lists.tile([P, R // 16], U16, name="h_list")
@@ -48,62 +49,82 @@ def tile_attend_gdistm_t_pl_kernel(tc, hT, rT, G, hoffs, roffs, offs, out_0, out
         out_words = out_1[0].rearrange("p c t -> p (c t)").bitcast(I32)
         out_scales = out_2[0].bitcast(I32)
 
-        h_tab = [sb.tile([P, HEADS], F32, name="h_tab%d" % n) for n in range(PACK)]
+        h_tab = [sb.tile([P, HEADS], F32, name="h_tab%d" % n) for n in range(PACK - 1)]
+        h_tab.append(reuse.tile([P, HEADS], F32, name="h_tab3", offset=0, align_bytes=64))
         r_tab = [sb.tile([P, RELS], F32, name="r_tab%d" % n) for n in range(PACK)]
         g_raw = [sb.tile([P, PACK, half], F32, name="g_raw%d" % a) for a in range(2)]
         window = [sb.tile([P, TAILS], F32, name="window%d" % n) for n in range(PACK)]
 
-        def load_tables(n):
+        def load_r(n):
             nc.sync.dma_start(r_tab[n][:], r_rows[:, LANES[n], :])
+
+        def load_h(n):
             nc.sync.dma_start(h_tab[n][:], h_rows[:, LANES[n], :])
 
+        load_r(0)
         nc.sync.dma_start(r_list[:], roffs)
+        load_h(0)
         nc.sync.dma_start(h_list[:], hoffs)
-        load_tables(0)
-        load_tables(1)
         for a in range(2):
             nc.sync.dma_start(g_raw[a][:], g_rows[:, :, a * half : (a + 1) * half])
         nc.sync.dma_start(t_list[:], offs)
-        load_tables(2)
-        load_tables(3)
+        load_r(1)
+        load_h(1)
+        load_r(2)
+        load_h(2)
+        load_r(3)
+        load_h(3)
 
         ident = sb.tile([P, P], F32, name="ident")
         make_identity(nc, ident[:])
         for n in range(PACK):
-            nc.vector.memset(window[n][:], 0.0)
+            (nc.vector if n < 2 else nc.gpsimd).memset(window[n][:], 0.0)
 
-        r_got = [sb.tile([P, R], F32, name="r_got%d" % n) for n in range(PACK)]
-        c_rows = [sb.tile([P, R], F32, name="c_rows%d" % n) for n in range(PACK)]
-        c_codes = [sb.tile([P, P], U32, name="c_codes%d" % n, align_bytes=64) for n in range(PACK)]
-        c_scales = [sb.tile([P, P], U8, name="c_scales%d" % n, align_bytes=64) for n in range(PACK)]
-        turned = [ps.tile([P, PACK, P], F32, name="turned%d" % n) for n in range(PACK)]
+        r_got = {}
+        c_rows = {}
+        c_scales = [sb.tile([P, P], U8, name="c_scales%d" % n, tag="c_scales%d" % n, align_bytes=64) for n in range(PACK)]
+        turned = [ps.tile([P, 2, P], F32, name="turned%d" % n) for n in range(PACK)]
         acc = [ps.tile([P, SLOTS], F32, name="acc%d" % n) for n in range(PACK)]
         g_codes = sb.tile([P, SLOTS], U32, name="g_codes", align_bytes=64)
         g_scales = sb.tile([P, SLOTS], U8, name="g_scales", align_bytes=64)
-        pairs = [sb.tile([P, 2, CHUNK, 2], BF16, name="pairs%d" % k) for k in range(chunks)]
         c_grouped = {}
+        pairs = {}
 
-        def gather_r(n):
+        def gather_r(n, tag):
+            r_got[n] = sb.tile([P, R], F32, name="r_got%d" % n, tag=tag, align_bytes=64)
             nc.vector.tensor_copy(r_got[n][:], r_tab[n][:].indirect(r_list[:]))
 
-        def gather_h(n):
+        def gather_h(n, tag):
+            c_rows[n] = sb.tile([P, R], F32, name="c_rows%d" % n, tag=tag, align_bytes=64)
             nc.vector.tensor_tensor(c_rows[n][:], h_tab[n][:].indirect(h_list[:]), r_got[n][:], mult)
 
-        def turn(n):
-            for t in range(PACK):
-                nc.tensor.transpose(turned[n][:, t, :], c_rows[n][:, t:R:PACK], ident[:])
-            c_grouped[n] = sb.tile([P, P, PACK], BF16, name="c_grouped%d" % n, tag="c_grouped%d" % n, align_bytes=64)
-            nc.scalar.copy(c_grouped[n][:], turned[n][:].rearrange("q t p -> q p t"))
+        def gather_h_first(n, tag):
+            r_got[n] = sb.tile([P, R], F32, name="h_got%d" % n, tag=tag, align_bytes=64)
+            nc.vector.tensor_copy(r_got[n][:], h_tab[n][:].indirect(h_list[:]))
 
-        def multiply(n):
+        def gather_r_second(n, tag):
+            c_rows[n] = sb.tile([P, R], F32, name="c_rows%d" % n, tag=tag, align_bytes=64)
+            nc.vector.tensor_tensor(c_rows[n][:], r_tab[n][:].indirect(r_list[:]), r_got[n][:], mult)
+
+        def turn(n):
+            c_pairs = sb.tile([P, 2, P, 2], BF16, name="c_pairs%d" % n, tag="c_pairs", align_bytes=64)
+            nc.scalar.copy(c_pairs[:], c_rows[n][:].rearrange("p (q u e) -> p u q e", u=2, e=2))
+            c_words = c_pairs[:].rearrange("p u q e -> p (u q e)").bitcast(F32)
+            for u in range(2):
+                nc.tensor.transpose(turned[n][:, u, :], c_words[:, u * P : (u + 1) * P], ident[:])
+            c_grouped[n] = sb.tile([P, P, PACK], BF16, name="c_grouped%d" % n, tag="c_grouped%d" % n, align_bytes=64)
+            dst = c_grouped[n][:].rearrange("q p t -> q (p t)").bitcast(F32).rearrange("q (p u) -> q p u", u=2)
+            nc.scalar.copy(dst, turned[n][:].rearrange("q u p -> q p u"))
+
+        def multiply(n, c_codes):
             nc.vector.quantize_mx(
-                out=c_codes[n][:].bitcast(E4M3),
+                out=c_codes[:].bitcast(E4M3),
                 scales=c_scales[n][:],
                 in_=c_grouped[n][:].rearrange("q p t -> q (p t)"),
             )
             nc.tensor.matmul_mx(
                 out=acc[n][:],
-                lhsT=c_codes[n][:].bitcast(E4M3),
+                lhsT=c_codes[:].bitcast(E4M3),
                 lhsT_scale=c_scales[n][:],
                 rhs=g_codes[:].bitcast(E5M2),
                 rhs_scale=g_scales[:],
@@ -111,13 +132,11 @@ def tile_attend_gdistm_t_pl_kernel(tc, hT, rT, G, hoffs, roffs, offs, out_0, out
                 stop=True,
             )
 
-        def fetch(n, lo, hi, tag):
-            dt = sb.tile([P, hi - lo], F32, name="dt%d_%d" % (n, lo), tag=tag, align_bytes=64)
-            nc.scalar.copy(dt[:], acc[n][:, lo:hi])
-            return dt
+        def fetch(dt, n, lo, hi):
+            nc.scalar.copy(dt, acc[n][:, lo:hi])
 
-        def scatter(n, dt, lo, hi):
-            nc.vector.tensor_copy(window[n][:].indirect(t_list[:, lo // 16 : hi // 16]), dt[:])
+        def scatter(dt, n, lo, hi):
+            nc.vector.tensor_copy(window[n][:].indirect(t_list[:, lo // 16 : hi // 16]), dt)
 
         def store(n):
             nc.sync.dma_start(out_rows[:, LANES[n], :], window[n][:])
@@ -130,12 +149,9 @@ def tile_attend_gdistm_t_pl_kernel(tc, hT, rT, G, hoffs, roffs, offs, out_0, out
             else:
                 nc.scalar.copy(dst, src)
 
-        gather_r(0)
-        gather_h(0)
+        gather_r(0, "r_got0")
+        gather_h(0, "c_rows0")
         turn(0)
-        gather_r(1)
-        gather_h(1)
-        turn(1)
 
         for a in range(2):
             g_grouped = sb.tile([P, half, PACK], BF16, name="g_grouped%d" % a, align_bytes=64)
@@ -151,58 +167,70 @@ def tile_attend_gdistm_t_pl_kernel(tc, hT, rT, G, hoffs, roffs, offs, out_0, out
                 in_=g_grouped[:].rearrange("q c t -> q (c t)"),
             )
 
-        multiply(0)
-        dt0 = fetch(0, 0, SLOTS, "dt_early")
-        multiply(1)
-        gather_r(2)
-        scatter(0, dt0, 0, SLOTS)
+        multiply(0, sb.tile([P, P], U32, name="c_codes0", align_bytes=64))
+        dt0 = sb.tile([P, SLOTS], F32, name="dt0", tag="dt0", align_bytes=64)
+        fetch(dt0[:], 0, 0, SLOTS)
+        gather_r(1, "c_grouped0")
+        scatter(dt0[:], 0, 0, SLOTS)
         store(0)
-        gather_h(2)
+        gather_h(1, "dt0")
+        turn(1)
+        gather_r(2, "c_grouped0")
+        gather_h(2, "c_rows2")
         turn(2)
-        dt1 = fetch(1, 0, SLOTS, "dt_early")
-        for k in range(chunks):
-            round_lane(0, k)
-        scatter(1, dt1, 0, SLOTS)
-        store(1)
-        gather_r(3)
-        multiply(2)
-        gather_h(3)
+        multiply(1, sb.tile([P, P], U32, name="c_codes1", tag="c_grouped0", align_bytes=64))
+        gather_h_first(3, "c_grouped1")
+        dt1a = reuse.tile([P, half], F32, name="dt1a", offset=0, align_bytes=64)
+        fetch(dt1a[:], 1, 0, half)
+        gather_r_second(3, "c_scales1")
         turn(3)
-        round_lane(1, 0)
-        round_lane(1, 1)
-        dt2a = fetch(2, 0, half, "dt_early")
-        scatter(2, dt2a, 0, half)
-        multiply(3)
-        dt2b = fetch(2, half, SLOTS, "c_grouped3")
-        dt3 = fetch(3, 0, SLOTS, "dt_last")
-        round_lane(1, 2)
-        round_lane(1, 3)
-        scatter(2, dt2b, half, SLOTS)
+        multiply(2, reuse.tile([P, P], U32, name="c_codes2", offset=4096, align_bytes=64))
+        scatter(dt1a[:], 1, 0, half)
+        multiply(3, sb.tile([P, P], U32, name="c_codes3", align_bytes=64))
+        late = sb.tile([P, half + SLOTS], F32, name="late", tag="c_pairs", align_bytes=64)
+        fetch(late[:, :half], 1, half, SLOTS)
+        fetch(late[:, half:], 2, 0, SLOTS)
+        dt3 = sb.tile([P, SLOTS], F32, name="dt3", align_bytes=64)
+        fetch(dt3[:], 3, 0, SLOTS)
+        pair_tags = ("pairs0", "dt0", "c_rows2", "c_scales1")
+        for k in range(chunks):
+            pairs[k] = sb.tile([P, 2, CHUNK, 2], BF16, name="pairs%d" % k, tag=pair_tags[k], align_bytes=64)
+            round_lane(0, k)
+        scatter(late[:, :half], 1, half, SLOTS)
+        store(1)
+        for k in range(chunks):
+            round_lane(1, k)
+        scatter(late[:, half:], 2, 0, SLOTS)
         store(2)
         for k in range(chunks):
             round_lane(2, k)
-        scatter(3, dt3, 0, SLOTS)
+        scatter(dt3[:], 3, 0, SLOTS)
         store(3)
 
-        y_grouped = [sb.tile([P, CHUNK, PACK], BF16, name="y_grouped%d" % k, align_bytes=64) for k in range(chunks)]
-        y_codes = [sb.tile([P, CHUNK], U32, name="y_codes%d" % k, align_bytes=64) for k in range(chunks)]
+        pieces = ((0, 512), (512, 1024), (1024, 1536), (1536, 1792), (1792, 2048))
+        y_grouped = [sb.tile([P, hi - lo, PACK], BF16, name="y_grouped%d" % lo, align_bytes=64) for lo, hi in pieces]
+        y_codes = [sb.tile([P, hi - lo], U32, name="y_codes%d" % lo, align_bytes=64) for lo, hi in pieces]
         y_scales = sb.tile([P, TAILS], U8, name="y_scales", align_bytes=64)
 
-        def weave(k, on_vector):
-            dst = y_grouped[k][:].rearrange("p c t -> p (c t)").bitcast(F32).rearrange("p (c u) -> p c u", u=2)
+        def weave(i, on_vector):
+            lo, hi = pieces[i]
+            k = lo // CHUNK
+            dst = y_grouped[i][:].rearrange("p c t -> p (c t)").bitcast(F32).rearrange("p (c u) -> p c u", u=2)
             src = pairs[k][:].rearrange("p u c e -> p (u c e)").bitcast(F32).rearrange("p (u c) -> p c u", u=2)
+            src = src[:, lo - k * CHUNK : hi - k * CHUNK, :]
             if on_vector:
                 nc.vector.tensor_copy(dst, src)
             else:
                 nc.scalar.copy(dst, src)
 
-        def quantize_planes(k):
+        def quantize_planes(i):
+            lo, hi = pieces[i]
             nc.vector.quantize_mx(
-                out=y_codes[k][:].bitcast(E4M3),
-                scales=y_scales[:, k * CHUNK : (k + 1) * CHUNK],
-                in_=y_grouped[k][:].rearrange("p c t -> p (c t)"),
+                out=y_codes[i][:].bitcast(E4M3),
+                scales=y_scales[:, lo:hi],
+                in_=y_grouped[i][:].rearrange("p c t -> p (c t)"),
             )
-            nc.sync.dma_start(out_words[:, k * CHUNK : (k + 1) * CHUNK], y_codes[k][:].bitcast(I32))
+            nc.sync.dma_start(out_words[:, lo:hi], y_codes[i][:].bitcast(I32))
 
         round_lane(3, 0, True)
         round_lane(3, 1, True)
@@ -212,8 +240,9 @@ def tile_attend_gdistm_t_pl_kernel(tc, hT, rT, G, hoffs, roffs, offs, out_0, out
         weave(2, False)
         round_lane(3, 3)
         weave(3, False)
-        for k in range(chunks):
-            quantize_planes(k)
+        weave(4, False)
+        for i in range(len(pieces)):
+            quantize_planes(i)
         for q in range(4):
             queue = nc.sync if q < 2 else nc.scalar
             queue.dma_start(out_scales[4 * q : 4 * q + 4, :], y_scales[32 * q : 32 * q + 4, :].bitcast(I32))

@@ -35,7 +35,8 @@ def tile_attend_gdistm_t_pl_kernel(tc, hT, rT, G, hoffs, roffs, offs, out_0, out
     with ExitStack() as ctx:
         lists = ctx.enter_context(tc.tile_pool(name="lists", bufs=1))
         sb = ctx.enter_context(tc.tile_pool(name="sb", bufs=1))
-        reuse = ctx.enter_context(tc.tile_pool(name="reuse", bufs=1))
+        after_h1 = ctx.enter_context(tc.tile_pool(name="after_h1", bufs=1))
+        after_h3 = ctx.enter_context(tc.tile_pool(name="after_h3", bufs=1))
         ps = ctx.enter_context(tc.psum_pool(name="ps", bufs=1))
 
         h_list = lists.tile([P, R // 16], U16, name="h_list")
@@ -49,70 +50,58 @@ def tile_attend_gdistm_t_pl_kernel(tc, hT, rT, G, hoffs, roffs, offs, out_0, out
         out_words = out_1[0].rearrange("p c t -> p (c t)").bitcast(I32)
         out_scales = out_2[0].bitcast(I32)
 
-        h_tab = [sb.tile([P, HEADS], F32, name="h_tab%d" % n) for n in range(PACK - 1)]
-        h_tab.append(reuse.tile([P, HEADS], F32, name="h_tab3", offset=0, align_bytes=64))
-        r_tab = [sb.tile([P, RELS], F32, name="r_tab%d" % n) for n in range(PACK)]
-        g_raw = [sb.tile([P, PACK, half], F32, name="g_raw%d" % a) for a in range(2)]
-        window = [sb.tile([P, TAILS], F32, name="window%d" % n) for n in range(PACK)]
+        def own(shape, dtype, name, tag=None):
+            return sb.tile(shape, dtype, name=name, tag=tag or name, align_bytes=64)
 
-        def load_r(n):
-            nc.sync.dma_start(r_tab[n][:], r_rows[:, LANES[n], :])
+        def placed(pool, shape, dtype, name, offset):
+            return pool.tile(shape, dtype, name=name, offset=offset, align_bytes=64)
 
-        def load_h(n):
-            nc.sync.dma_start(h_tab[n][:], h_rows[:, LANES[n], :])
+        h_tab = [
+            own([P, HEADS], F32, "h_tab0"),
+            placed(after_h1, [P, HEADS], F32, "h_tab1", 0),
+            own([P, HEADS], F32, "h_tab2"),
+            placed(after_h3, [P, HEADS], F32, "h_tab3", 0),
+        ]
+        r_tab = [own([P, RELS], F32, "r_tab%d" % n) for n in range(PACK)]
+        g_raw = [own([P, PACK, half], F32, "g_raw%d" % a) for a in range(2)]
+        window = [own([P, TAILS], F32, "window%d" % n) for n in range(PACK - 1)]
+        window.append(window[0])
 
-        load_r(0)
+        nc.sync.dma_start(r_tab[0][:], r_rows[:, LANES[0], :])
         nc.sync.dma_start(r_list[:], roffs)
-        load_h(0)
+        nc.sync.dma_start(h_tab[0][:], h_rows[:, LANES[0], :])
         nc.sync.dma_start(h_list[:], hoffs)
         for a in range(2):
             nc.sync.dma_start(g_raw[a][:], g_rows[:, :, a * half : (a + 1) * half])
         nc.sync.dma_start(t_list[:], offs)
-        load_r(1)
-        load_h(1)
-        load_r(2)
-        load_h(2)
-        load_r(3)
-        load_h(3)
+        for n in range(1, PACK):
+            nc.sync.dma_start(r_tab[n][:], r_rows[:, LANES[n], :])
+            nc.sync.dma_start(h_tab[n][:], h_rows[:, LANES[n], :])
 
-        ident = sb.tile([P, P], F32, name="ident")
+        ident = own([P, P], F32, "ident")
         make_identity(nc, ident[:])
-        for n in range(PACK):
-            (nc.vector if n < 2 else nc.gpsimd).memset(window[n][:], 0.0)
 
-        r_got = {}
-        c_rows = {}
-        c_scales = [sb.tile([P, P], U8, name="c_scales%d" % n, tag="c_scales%d" % n, align_bytes=64) for n in range(PACK)]
+        c_scales = [own([P, P], U8, "c_scales%d" % n) for n in range(PACK)]
         turned = [ps.tile([P, 2, P], F32, name="turned%d" % n) for n in range(PACK)]
         acc = [ps.tile([P, SLOTS], F32, name="acc%d" % n) for n in range(PACK)]
-        g_codes = sb.tile([P, SLOTS], U32, name="g_codes", align_bytes=64)
-        g_scales = sb.tile([P, SLOTS], U8, name="g_scales", align_bytes=64)
-        c_grouped = {}
+        g_codes = own([P, SLOTS], U32, "g_codes")
+        g_scales = own([P, SLOTS], U8, "g_scales")
+        c_grouped = [own([P, P, PACK], BF16, "c_grouped%d" % n) for n in range(PACK)]
         pairs = {}
 
-        def gather_r(n, tag):
-            r_got[n] = sb.tile([P, R], F32, name="r_got%d" % n, tag=tag, align_bytes=64)
-            nc.vector.tensor_copy(r_got[n][:], r_tab[n][:].indirect(r_list[:]))
+        def gather_r(n, r_got):
+            nc.vector.tensor_copy(r_got, r_tab[n][:].indirect(r_list[:]))
 
-        def gather_h(n, tag):
-            c_rows[n] = sb.tile([P, R], F32, name="c_rows%d" % n, tag=tag, align_bytes=64)
-            nc.vector.tensor_tensor(c_rows[n][:], h_tab[n][:].indirect(h_list[:]), r_got[n][:], mult)
+        def gather_h(n, r_got, c_rows):
+            nc.vector.tensor_tensor(c_rows, h_tab[n][:].indirect(h_list[:]), r_got, mult)
 
-        def gather_h_first(n, tag):
-            r_got[n] = sb.tile([P, R], F32, name="h_got%d" % n, tag=tag, align_bytes=64)
-            nc.vector.tensor_copy(r_got[n][:], h_tab[n][:].indirect(h_list[:]))
+        def round_c(c_rows, c_pairs):
+            nc.scalar.copy(c_pairs[:], c_rows.rearrange("p (q u e) -> p u q e", u=2, e=2))
 
-        def gather_r_second(n, tag):
-            c_rows[n] = sb.tile([P, R], F32, name="c_rows%d" % n, tag=tag, align_bytes=64)
-            nc.vector.tensor_tensor(c_rows[n][:], r_tab[n][:].indirect(r_list[:]), r_got[n][:], mult)
-
-        def turn(n):
-            c_pairs = sb.tile([P, 2, P, 2], BF16, name="c_pairs%d" % n, tag="c_pairs", align_bytes=64)
-            nc.scalar.copy(c_pairs[:], c_rows[n][:].rearrange("p (q u e) -> p u q e", u=2, e=2))
+        def turn(n, c_pairs):
             c_words = c_pairs[:].rearrange("p u q e -> p (u q e)").bitcast(F32)
             for u in range(2):
                 nc.tensor.transpose(turned[n][:, u, :], c_words[:, u * P : (u + 1) * P], ident[:])
-            c_grouped[n] = sb.tile([P, P, PACK], BF16, name="c_grouped%d" % n, tag="c_grouped%d" % n, align_bytes=64)
             dst = c_grouped[n][:].rearrange("q p t -> q (p t)").bitcast(F32).rearrange("q (p u) -> q p u", u=2)
             nc.scalar.copy(dst, turned[n][:].rearrange("q u p -> q p u"))
 
@@ -149,53 +138,77 @@ def tile_attend_gdistm_t_pl_kernel(tc, hT, rT, G, hoffs, roffs, offs, out_0, out
             else:
                 nc.scalar.copy(dst, src)
 
-        gather_r(0, "r_got0")
-        gather_h(0, "c_rows0")
-        turn(0)
+        pair_shape = [P, 2, CHUNK, 2]
+        c_pair_shape = [P, 2, P, 2]
+
+        nc.vector.memset(window[0][:], 0.0)
+        nc.vector.memset(window[1][:], 0.0)
+        r_got0 = own([P, R], F32, "r_got0")
+        gather_r(0, r_got0[:])
+        nc.vector.memset(window[2][:], 0.0)
+        c_rows0 = own([P, R], F32, "c_rows0")
+        gather_h(0, r_got0[:], c_rows0[:])
+        c_pairs0 = own(c_pair_shape, BF16, "c_pairs0")
+        round_c(c_rows0[:], c_pairs0)
+        turn(0, c_pairs0)
 
         for a in range(2):
-            g_grouped = sb.tile([P, half, PACK], BF16, name="g_grouped%d" % a, align_bytes=64)
+            g_grouped = own([P, half, PACK], BF16, "g_grouped%d" % a)
             dst = g_grouped[:].rearrange("q (c i) t -> q c t i", i=4)
             src = g_raw[a][:].rearrange("q t (c i) -> q c t i", i=4)
-            if a == 0:
-                nc.scalar.copy(dst, src)
-            else:
-                nc.vector.tensor_copy(dst, src)
+            nc.vector.tensor_copy(dst, src)
             nc.vector.quantize_mx(
                 out=g_codes[:, a * half : (a + 1) * half].bitcast(E5M2),
                 scales=g_scales[:, a * half : (a + 1) * half],
                 in_=g_grouped[:].rearrange("q c t -> q (c t)"),
             )
 
-        multiply(0, sb.tile([P, P], U32, name="c_codes0", align_bytes=64))
-        dt0 = sb.tile([P, SLOTS], F32, name="dt0", tag="dt0", align_bytes=64)
+        multiply(0, own([P, P], U32, "c_codes0"))
+        r_got1 = own([P, R], F32, "r_got1", "c_grouped0")
+        gather_r(1, r_got1[:])
+        c_rows1 = own([P, R], F32, "c_rows1")
+        gather_h(1, r_got1[:], c_rows1[:])
+        dt0 = placed(after_h1, [P, SLOTS], F32, "dt0", 0)
         fetch(dt0[:], 0, 0, SLOTS)
-        gather_r(1, "c_grouped0")
+        c_pairs1 = placed(after_h1, c_pair_shape, BF16, "c_pairs1", 7168)
+        round_c(c_rows1[:], c_pairs1)
+        r_got2 = own([P, R], F32, "r_got2", "r_tab1")
+        gather_r(2, r_got2[:])
         scatter(dt0[:], 0, 0, SLOTS)
         store(0)
-        gather_h(1, "dt0")
-        turn(1)
-        gather_r(2, "c_grouped0")
-        gather_h(2, "c_rows2")
-        turn(2)
-        multiply(1, sb.tile([P, P], U32, name="c_codes1", tag="c_grouped0", align_bytes=64))
-        gather_h_first(3, "c_grouped1")
-        dt1a = reuse.tile([P, half], F32, name="dt1a", offset=0, align_bytes=64)
+        turn(1, c_pairs1)
+
+        mid = placed(after_h1, [P, 2 * R], F32, "mid", 3584)
+        gather_h(2, r_got2[:], mid[:, :R])
+        multiply(1, own([P, P], U32, "c_codes1"))
+        pairs[0] = placed(after_h1, pair_shape, BF16, "pairs0", 7680)
+        round_lane(0, 0)
+        c_pairs2 = own(c_pair_shape, BF16, "c_pairs2")
+        round_c(mid[:, :R], c_pairs2)
+        gather_r(3, mid[:, R:])
+        pairs[1] = own(pair_shape, BF16, "pairs1", "h_tab2")
+        round_lane(0, 1)
+        turn(2, c_pairs2)
+        pairs[2] = own(pair_shape, BF16, "pairs2", "c_pairs2")
+        round_lane(0, 2)
+
+        c_rows3 = own([P, R], F32, "c_rows3")
+        gather_h(3, mid[:, R:], c_rows3[:])
+        multiply(2, placed(after_h3, [P, P], U32, "c_codes2", 1024))
+        dt1a = placed(after_h3, [P, half], F32, "dt1a", 0)
         fetch(dt1a[:], 1, 0, half)
-        gather_r_second(3, "c_scales1")
-        turn(3)
-        multiply(2, reuse.tile([P, P], U32, name="c_codes2", offset=4096, align_bytes=64))
+        c_pairs3 = placed(after_h3, c_pair_shape, BF16, "c_pairs3", 7168)
+        round_c(c_rows3[:], c_pairs3)
         scatter(dt1a[:], 1, 0, half)
-        multiply(3, sb.tile([P, P], U32, name="c_codes3", align_bytes=64))
-        late = sb.tile([P, half + SLOTS], F32, name="late", tag="c_pairs", align_bytes=64)
+        turn(3, c_pairs3)
+        multiply(3, own([P, P], U32, "c_codes3"))
+        late = placed(after_h3, [P, half + SLOTS], F32, "late", 4608)
         fetch(late[:, :half], 1, half, SLOTS)
         fetch(late[:, half:], 2, 0, SLOTS)
-        dt3 = sb.tile([P, SLOTS], F32, name="dt3", align_bytes=64)
+        pairs[3] = placed(after_h3, pair_shape, BF16, "pairs3", 7680)
+        round_lane(0, 3)
+        dt3 = own([P, SLOTS], F32, "dt3")
         fetch(dt3[:], 3, 0, SLOTS)
-        pair_tags = ("pairs0", "dt0", "c_rows2", "c_scales1")
-        for k in range(chunks):
-            pairs[k] = sb.tile([P, 2, CHUNK, 2], BF16, name="pairs%d" % k, tag=pair_tags[k], align_bytes=64)
-            round_lane(0, k)
         scatter(late[:, :half], 1, half, SLOTS)
         store(1)
         for k in range(chunks):
@@ -208,9 +221,9 @@ def tile_attend_gdistm_t_pl_kernel(tc, hT, rT, G, hoffs, roffs, offs, out_0, out
         store(3)
 
         pieces = ((0, 512), (512, 1024), (1024, 1536), (1536, 1792), (1792, 2048))
-        y_grouped = [sb.tile([P, hi - lo, PACK], BF16, name="y_grouped%d" % lo, align_bytes=64) for lo, hi in pieces]
-        y_codes = [sb.tile([P, hi - lo], U32, name="y_codes%d" % lo, align_bytes=64) for lo, hi in pieces]
-        y_scales = sb.tile([P, TAILS], U8, name="y_scales", align_bytes=64)
+        y_grouped = [own([P, hi - lo, PACK], BF16, "y_grouped%d" % lo) for lo, hi in pieces]
+        y_codes = own([P, TAILS], U32, "y_codes")
+        y_scales = own([P, TAILS], U8, "y_scales")
 
         def weave(i, on_vector):
             lo, hi = pieces[i]
@@ -223,26 +236,19 @@ def tile_attend_gdistm_t_pl_kernel(tc, hT, rT, G, hoffs, roffs, offs, out_0, out
             else:
                 nc.scalar.copy(dst, src)
 
-        def quantize_planes(i):
-            lo, hi = pieces[i]
+        round_lane(3, 0, True)
+        round_lane(3, 1, True)
+        round_lane(3, 2)
+        round_lane(3, 3)
+        for i in range(len(pieces)):
+            weave(i, i < 2)
+        for i, (lo, hi) in enumerate(pieces):
             nc.vector.quantize_mx(
-                out=y_codes[i][:].bitcast(E4M3),
+                out=y_codes[:, lo:hi].bitcast(E4M3),
                 scales=y_scales[:, lo:hi],
                 in_=y_grouped[i][:].rearrange("p c t -> p (c t)"),
             )
-            nc.sync.dma_start(out_words[:, lo:hi], y_codes[i][:].bitcast(I32))
-
-        round_lane(3, 0, True)
-        round_lane(3, 1, True)
-        weave(0, True)
-        weave(1, True)
-        round_lane(3, 2)
-        weave(2, False)
-        round_lane(3, 3)
-        weave(3, False)
-        weave(4, False)
-        for i in range(len(pieces)):
-            quantize_planes(i)
+            nc.sync.dma_start(out_words[:, lo:hi], y_codes[:, lo:hi].bitcast(I32))
         for q in range(4):
             queue = nc.sync if q < 2 else nc.scalar
             queue.dma_start(out_scales[4 * q : 4 * q + 4, :], y_scales[32 * q : 32 * q + 4, :].bitcast(I32))

@@ -35,8 +35,7 @@ def tile_attend_gdistm_t_pl_kernel(tc, hT, rT, G, hoffs, roffs, offs, out_0, out
     with ExitStack() as ctx:
         lists = ctx.enter_context(tc.tile_pool(name="lists", bufs=1))
         sb = ctx.enter_context(tc.tile_pool(name="sb", bufs=1))
-        after_h1 = ctx.enter_context(tc.tile_pool(name="after_h1", bufs=1))
-        after_h3 = ctx.enter_context(tc.tile_pool(name="after_h3", bufs=1))
+        reuse = ctx.enter_context(tc.tile_pool(name="reuse", bufs=1))
         ps = ctx.enter_context(tc.psum_pool(name="ps", bufs=1))
 
         h_list = lists.tile([P, R // 16], U16, name="h_list")
@@ -53,14 +52,14 @@ def tile_attend_gdistm_t_pl_kernel(tc, hT, rT, G, hoffs, roffs, offs, out_0, out
         def own(shape, dtype, name, tag=None):
             return sb.tile(shape, dtype, name=name, tag=tag or name, align_bytes=64)
 
-        def placed(pool, shape, dtype, name, offset):
-            return pool.tile(shape, dtype, name=name, offset=offset, align_bytes=64)
+        def placed(shape, dtype, name, offset):
+            return reuse.tile(shape, dtype, name=name, offset=offset, align_bytes=64)
 
         h_tab = [
             own([P, HEADS], F32, "h_tab0"),
-            placed(after_h1, [P, HEADS], F32, "h_tab1", 0),
+            placed([P, HEADS], F32, "h_tab1", 16384),
             own([P, HEADS], F32, "h_tab2"),
-            placed(after_h3, [P, HEADS], F32, "h_tab3", 0),
+            placed([P, HEADS], F32, "h_tab3", 0),
         ]
         r_tab = [own([P, RELS], F32, "r_tab%d" % n) for n in range(PACK)]
         g_raw = [own([P, PACK, half], F32, "g_raw%d" % a) for a in range(2)]
@@ -73,20 +72,24 @@ def tile_attend_gdistm_t_pl_kernel(tc, hT, rT, G, hoffs, roffs, offs, out_0, out
         nc.sync.dma_start(h_list[:], hoffs)
         for a in range(2):
             nc.sync.dma_start(g_raw[a][:], g_rows[:, :, a * half : (a + 1) * half])
-        nc.sync.dma_start(t_list[:], offs)
-        for n in range(1, PACK):
+        for n in (1, 2):
             nc.sync.dma_start(r_tab[n][:], r_rows[:, LANES[n], :])
-            nc.sync.dma_start(h_tab[n][:], h_rows[:, LANES[n], :])
+        nc.sync.dma_start(t_list[:], offs)
+        nc.sync.dma_start(h_tab[2][:, : HEADS // 2], h_rows[:, LANES[2], : HEADS // 2])
+        nc.sync.dma_start(h_tab[1][:], h_rows[:, LANES[1], :])
+        nc.sync.dma_start(h_tab[2][:, HEADS // 2 :], h_rows[:, LANES[2], HEADS // 2 :])
+        nc.sync.dma_start(h_tab[3][:], h_rows[:, LANES[3], :])
+        nc.sync.dma_start(r_tab[3][:], r_rows[:, LANES[3], :])
 
-        ident = own([P, P], F32, "ident")
+        ident = placed([P, P], F32, "ident", 26624)
         make_identity(nc, ident[:])
 
         c_scales = [own([P, P], U8, "c_scales%d" % n) for n in range(PACK)]
         turned = [ps.tile([P, 2, P], F32, name="turned%d" % n) for n in range(PACK)]
-        acc = [ps.tile([P, SLOTS], F32, name="acc%d" % n) for n in range(PACK)]
+        acc = [ps.tile([P, SLOTS], F32, name="acc%d" % n, tag="acc%d" % min(n, 2)) for n in range(PACK)]
         g_codes = own([P, SLOTS], U32, "g_codes")
         g_scales = own([P, SLOTS], U8, "g_scales")
-        c_grouped = [own([P, P, PACK], BF16, "c_grouped%d" % n) for n in range(PACK)]
+        c_grouped = {n: [own([P, P * PACK], BF16, "c_grouped%d" % n)[:]] for n in range(PACK - 1)}
         pairs = {}
 
         def gather_r(n, r_got):
@@ -96,21 +99,29 @@ def tile_attend_gdistm_t_pl_kernel(tc, hT, rT, G, hoffs, roffs, offs, out_0, out
             nc.vector.tensor_tensor(c_rows, h_tab[n][:].indirect(h_list[:]), r_got, mult)
 
         def round_c(c_rows, c_pairs):
-            nc.scalar.copy(c_pairs[:], c_rows.rearrange("p (q u e) -> p u q e", u=2, e=2))
+            nc.scalar.copy(c_pairs.rearrange("p (u q e) -> p u q e", u=2, e=2), c_rows.rearrange("p (q u e) -> p u q e", u=2, e=2))
 
-        def turn(n, c_pairs):
-            c_words = c_pairs[:].rearrange("p u q e -> p (u q e)").bitcast(F32)
+        def round_c_half(c_rows, c_half, u):
+            nc.scalar.copy(c_half.rearrange("p (q e) -> p q e", e=2), c_rows.rearrange("p (q u e) -> p u q e", u=2, e=2)[:, u])
+
+        def halves(c_pairs):
+            return [c_pairs[:, u * 2 * P : (u + 1) * 2 * P] for u in range(2)]
+
+        def turn(n, c_halves):
             for u in range(2):
-                nc.tensor.transpose(turned[n][:, u, :], c_words[:, u * P : (u + 1) * P], ident[:])
-            dst = c_grouped[n][:].rearrange("q p t -> q (p t)").bitcast(F32).rearrange("q (p u) -> q p u", u=2)
-            nc.scalar.copy(dst, turned[n][:].rearrange("q u p -> q p u"))
+                nc.tensor.transpose(turned[n][:, u, :], c_halves[u].bitcast(F32), ident[:])
+
+        def group(n):
+            width = P // len(c_grouped[n])
+            for a, part in enumerate(c_grouped[n]):
+                dst = part.bitcast(F32).rearrange("q (p u) -> q p u", u=2)
+                nc.scalar.copy(dst, turned[n][:, :, a * width : (a + 1) * width].rearrange("q u p -> q p u"))
 
         def multiply(n, c_codes):
-            nc.vector.quantize_mx(
-                out=c_codes[:].bitcast(E4M3),
-                scales=c_scales[n][:],
-                in_=c_grouped[n][:].rearrange("q p t -> q (p t)"),
-            )
+            width = P // len(c_grouped[n])
+            for a, part in enumerate(c_grouped[n]):
+                cols = slice(a * width, (a + 1) * width)
+                nc.vector.quantize_mx(out=c_codes[:, cols].bitcast(E4M3), scales=c_scales[n][:, cols], in_=part)
             nc.tensor.matmul_mx(
                 out=acc[n][:],
                 lhsT=c_codes[:].bitcast(E4M3),
@@ -130,16 +141,16 @@ def tile_attend_gdistm_t_pl_kernel(tc, hT, rT, G, hoffs, roffs, offs, out_0, out
         def store(n):
             nc.sync.dma_start(out_rows[:, LANES[n], :], window[n][:])
 
-        def round_lane(n, k, on_vector=False):
-            dst = pairs[k][:, LANES[n] // 2, :, LANES[n] % 2]
-            src = window[n][:, k * CHUNK : (k + 1) * CHUNK]
+        def round_lane(n, k, on_vector=False, lo=0, hi=CHUNK):
+            dst = pairs[k][:, LANES[n] // 2, lo:hi, LANES[n] % 2]
+            src = window[n][:, k * CHUNK + lo : k * CHUNK + hi]
             if on_vector:
                 nc.vector.tensor_copy(dst, src)
             else:
                 nc.scalar.copy(dst, src)
 
         pair_shape = [P, 2, CHUNK, 2]
-        c_pair_shape = [P, 2, P, 2]
+        c_pair_shape = [P, R]
 
         nc.vector.memset(window[0][:], 0.0)
         nc.vector.memset(window[1][:], 0.0)
@@ -149,8 +160,9 @@ def tile_attend_gdistm_t_pl_kernel(tc, hT, rT, G, hoffs, roffs, offs, out_0, out
         c_rows0 = own([P, R], F32, "c_rows0")
         gather_h(0, r_got0[:], c_rows0[:])
         c_pairs0 = own(c_pair_shape, BF16, "c_pairs0")
-        round_c(c_rows0[:], c_pairs0)
-        turn(0, c_pairs0)
+        round_c(c_rows0[:], c_pairs0[:])
+        turn(0, halves(c_pairs0))
+        group(0)
 
         for a in range(2):
             g_grouped = own([P, half, PACK], BF16, "g_grouped%d" % a)
@@ -164,56 +176,64 @@ def tile_attend_gdistm_t_pl_kernel(tc, hT, rT, G, hoffs, roffs, offs, out_0, out
             )
 
         multiply(0, own([P, P], U32, "c_codes0"))
-        r_got1 = own([P, R], F32, "r_got1", "c_grouped0")
-        gather_r(1, r_got1[:])
-        c_rows1 = own([P, R], F32, "c_rows1")
-        gather_h(1, r_got1[:], c_rows1[:])
-        dt0 = placed(after_h1, [P, SLOTS], F32, "dt0", 0)
-        fetch(dt0[:], 0, 0, SLOTS)
-        c_pairs1 = placed(after_h1, c_pair_shape, BF16, "c_pairs1", 7168)
-        round_c(c_rows1[:], c_pairs1)
-        r_got2 = own([P, R], F32, "r_got2", "r_tab1")
-        gather_r(2, r_got2[:])
-        scatter(dt0[:], 0, 0, SLOTS)
-        store(0)
-        turn(1, c_pairs1)
+        r_got12 = own([P, 2 * R], F32, "r_got12", "c_grouped0")
+        gather_r(1, r_got12[:, :R])
+        dt0a = own([P, half], F32, "dt0a", "r_tab1")
+        fetch(dt0a[:], 0, 0, half)
+        gather_r(2, r_got12[:, R:])
+        scatter(dt0a[:], 0, 0, half)
 
-        mid = placed(after_h1, [P, 2 * R], F32, "mid", 3584)
-        gather_h(2, r_got2[:], mid[:, :R])
-        multiply(1, own([P, P], U32, "c_codes1"))
-        pairs[0] = placed(after_h1, pair_shape, BF16, "pairs0", 7680)
-        round_lane(0, 0)
+        c_rows1 = own([P, R], F32, "c_rows1", "r_tab2")
+        gather_h(1, r_got12[:, :R], c_rows1[:])
+        dt0b = placed([P, half], F32, "dt0b", 16384)
+        fetch(dt0b[:], 0, half, SLOTS)
+        c_pairs1 = placed(c_pair_shape, BF16, "c_pairs1", 17408)
+        round_c(c_rows1[:], c_pairs1[:])
+        c_rows2 = own([P, R], F32, "c_rows2")
+        gather_h(2, r_got12[:, R:], c_rows2[:])
+        scatter(dt0b[:], 0, half, SLOTS)
+        store(0)
+        turn(1, halves(c_pairs1))
         c_pairs2 = own(c_pair_shape, BF16, "c_pairs2")
-        round_c(mid[:, :R], c_pairs2)
-        gather_r(3, mid[:, R:])
-        pairs[1] = own(pair_shape, BF16, "pairs1", "h_tab2")
-        round_lane(0, 1)
-        turn(2, c_pairs2)
-        pairs[2] = own(pair_shape, BF16, "pairs2", "c_pairs2")
+        round_c(c_rows2[:], c_pairs2[:])
+        group(1)
+        turn(2, halves(c_pairs2))
+        multiply(1, placed([P, P], U32, "c_codes1", 8192))
+        group(2)
+        pairs[0] = own(pair_shape, BF16, "pairs0", "c_pairs2")
+        round_lane(0, 0)
+        pairs[2] = own(pair_shape, BF16, "pairs2", "c_grouped1")
         round_lane(0, 2)
 
+        h_got3 = placed([P, R], F32, "h_got3", 17920)
+        nc.vector.tensor_copy(h_got3[:], h_tab[3][:].indirect(h_list[:]))
+        multiply(2, placed([P, P], U32, "c_codes2", 0))
+        dt1 = placed([P, SLOTS], F32, "dt1", 1024)
+        fetch(dt1[:], 1, 0, SLOTS)
+        pairs[1] = placed(pair_shape, BF16, "pairs1", 6144)
+        round_lane(0, 1)
         c_rows3 = own([P, R], F32, "c_rows3")
-        gather_h(3, mid[:, R:], c_rows3[:])
-        multiply(2, placed(after_h3, [P, P], U32, "c_codes2", 1024))
-        dt1a = placed(after_h3, [P, half], F32, "dt1a", 0)
-        fetch(dt1a[:], 1, 0, half)
-        c_pairs3 = placed(after_h3, c_pair_shape, BF16, "c_pairs3", 7168)
-        round_c(c_rows3[:], c_pairs3)
-        scatter(dt1a[:], 1, 0, half)
-        turn(3, c_pairs3)
+        nc.vector.tensor_tensor(c_rows3[:], r_tab[3][:].indirect(r_list[:]), h_got3[:], mult)
+        scatter(dt1[:], 1, 0, SLOTS)
+        c_first3 = own([P, 2 * P], BF16, "c_first3")
+        scratch = [pairs[k][:].rearrange("p u c e -> p (u c e)")[:, : 2 * P] for k in range(3)]
+        c_halves3 = [c_first3[:], scratch[1]]
+        for u in range(2):
+            round_c_half(c_rows3[:], c_halves3[u], u)
+        turn(3, c_halves3)
+        c_grouped[3] = [scratch[0], scratch[2]]
+        group(3)
+        dt2 = placed([P, SLOTS], F32, "dt2", 24832)
+        fetch(dt2[:], 2, 0, SLOTS)
         multiply(3, own([P, P], U32, "c_codes3"))
-        late = placed(after_h3, [P, half + SLOTS], F32, "late", 4608)
-        fetch(late[:, :half], 1, half, SLOTS)
-        fetch(late[:, half:], 2, 0, SLOTS)
-        pairs[3] = placed(after_h3, pair_shape, BF16, "pairs3", 7680)
+        pairs[3] = placed(pair_shape, BF16, "pairs3", 26880)
         round_lane(0, 3)
         dt3 = own([P, SLOTS], F32, "dt3")
         fetch(dt3[:], 3, 0, SLOTS)
-        scatter(late[:, :half], 1, half, SLOTS)
         store(1)
-        for k in range(chunks):
+        for k in (1, 0, 2, 3):
             round_lane(1, k)
-        scatter(late[:, half:], 2, 0, SLOTS)
+        scatter(dt2[:], 2, 0, SLOTS)
         store(2)
         for k in range(chunks):
             round_lane(2, k)
@@ -238,7 +258,8 @@ def tile_attend_gdistm_t_pl_kernel(tc, hT, rT, G, hoffs, roffs, offs, out_0, out
 
         round_lane(3, 0, True)
         round_lane(3, 1, True)
-        round_lane(3, 2)
+        round_lane(3, 2, False, CHUNK // 2, CHUNK)
+        round_lane(3, 2, True, 0, CHUNK // 2)
         round_lane(3, 3)
         for i in range(len(pieces)):
             weave(i, i < 2)

@@ -62,7 +62,7 @@ def tile_attend_gdistm_t_pl_kernel(tc, hT, rT, G, hoffs, roffs, offs, out_0, out
             placed([P, HEADS], F32, "h_tab3", 0),
         ]
         r_tab = [own([P, RELS], F32, "r_tab%d" % n) for n in range(PACK)]
-        g_raw = [own([P, PACK, half], F32, "g_raw%d" % a) for a in range(2)]
+        g_raw = [own([P, 2, SLOTS], F32, "g_raw%d" % u) for u in range(2)]
         window = [own([P, TAILS], F32, "window%d" % n) for n in range(PACK - 1)]
         window.append(window[0])
 
@@ -70,8 +70,8 @@ def tile_attend_gdistm_t_pl_kernel(tc, hT, rT, G, hoffs, roffs, offs, out_0, out
         nc.sync.dma_start(r_list[:], roffs)
         nc.sync.dma_start(h_tab[0][:], h_rows[:, LANES[0], :])
         nc.sync.dma_start(h_list[:], hoffs)
-        for a in range(2):
-            nc.sync.dma_start(g_raw[a][:], g_rows[:, :, a * half : (a + 1) * half])
+        for u in range(2):
+            nc.sync.dma_start(g_raw[u][:], g_rows[:, 2 * u : 2 * u + 2, :])
         for n in (1, 2):
             nc.sync.dma_start(r_tab[n][:], r_rows[:, LANES[n], :])
         nc.sync.dma_start(t_list[:], offs)
@@ -156,7 +156,7 @@ def tile_attend_gdistm_t_pl_kernel(tc, hT, rT, G, hoffs, roffs, offs, out_0, out
         nc.vector.memset(window[1][:], 0.0)
         r_got0 = own([P, R], F32, "r_got0")
         gather_r(0, r_got0[:])
-        nc.vector.memset(window[2][:], 0.0)
+        nc.gpsimd.memset(window[2][:], 0.0)
         c_rows0 = own([P, R], F32, "c_rows0")
         gather_h(0, r_got0[:], c_rows0[:])
         c_pairs0 = own(c_pair_shape, BF16, "c_pairs0")
@@ -164,15 +164,16 @@ def tile_attend_gdistm_t_pl_kernel(tc, hT, rT, G, hoffs, roffs, offs, out_0, out
         turn(0, halves(c_pairs0))
         group(0)
 
+        g_grouped = [own([P, half, PACK], BF16, "g_grouped%d" % a) for a in range(2)]
+        for u in range(2):
+            for a in range(2):
+                src = g_raw[u][:, :, a * half : (a + 1) * half].rearrange("q e c -> q c e")
+                nc.vector.tensor_copy(g_grouped[a][:, :, 2 * u : 2 * u + 2], src)
         for a in range(2):
-            g_grouped = own([P, half, PACK], BF16, "g_grouped%d" % a)
-            dst = g_grouped[:].rearrange("q (c i) t -> q c t i", i=4)
-            src = g_raw[a][:].rearrange("q t (c i) -> q c t i", i=4)
-            nc.vector.tensor_copy(dst, src)
             nc.vector.quantize_mx(
                 out=g_codes[:, a * half : (a + 1) * half].bitcast(E5M2),
                 scales=g_scales[:, a * half : (a + 1) * half],
-                in_=g_grouped[:].rearrange("q c t -> q (c t)"),
+                in_=g_grouped[a][:].rearrange("q c t -> q (c t)"),
             )
 
         multiply(0, own([P, P], U32, "c_codes0"))
@@ -243,7 +244,7 @@ def tile_attend_gdistm_t_pl_kernel(tc, hT, rT, G, hoffs, roffs, offs, out_0, out
         pieces = ((0, 512), (512, 1024), (1024, 1536), (1536, 1792), (1792, 2048))
         y_grouped = [own([P, hi - lo, PACK], BF16, "y_grouped%d" % lo) for lo, hi in pieces]
         y_codes = own([P, TAILS], U32, "y_codes")
-        y_scales = own([P, TAILS], U8, "y_scales")
+        y_scales = own([P, CHUNK], U8, "y_scales")
 
         def weave(i, on_vector):
             lo, hi = pieces[i]
@@ -264,12 +265,16 @@ def tile_attend_gdistm_t_pl_kernel(tc, hT, rT, G, hoffs, roffs, offs, out_0, out
         for i in range(len(pieces)):
             weave(i, i < 2)
         for i, (lo, hi) in enumerate(pieces):
-            nc.vector.quantize_mx(
-                out=y_codes[:, lo:hi].bitcast(E4M3),
-                scales=y_scales[:, lo:hi],
-                in_=y_grouped[i][:].rearrange("p c t -> p (c t)"),
-            )
+            for a in range(lo, hi, CHUNK // 2):
+                b = a + CHUNK // 2
+                k = a // CHUNK
+                nc.vector.quantize_mx(
+                    out=y_codes[:, a:b].bitcast(E4M3),
+                    scales=y_scales[4 * k :, a - k * CHUNK : b - k * CHUNK],
+                    in_=y_grouped[i][:, a - lo : b - lo, :].rearrange("p c t -> p (c t)"),
+                )
             nc.sync.dma_start(out_words[:, lo:hi], y_codes[:, lo:hi].bitcast(I32))
+        scale_rows = out_scales.rearrange("f (k c) -> k f c", k=chunks)
         for q in range(4):
             queue = nc.sync if q < 2 else nc.scalar
-            queue.dma_start(out_scales[4 * q : 4 * q + 4, :], y_scales[32 * q : 32 * q + 4, :].bitcast(I32))
+            queue.dma_start(scale_rows[:, 4 * q : 4 * q + 4, :], y_scales[32 * q : 32 * q + 16, :].bitcast(I32))

@@ -62,7 +62,7 @@ def tile_attend_gdistm_t_pl_kernel(tc, hT, rT, G, hoffs, roffs, offs, out_0, out
             placed([P, HEADS], F32, "h_tab3", 0),
         ]
         r_tab = [own([P, RELS], F32, "r_tab%d" % n) for n in range(PACK)]
-        g_raw = [own([P, 2, SLOTS], F32, "g_raw%d" % u) for u in range(2)]
+        g_raw = own([P, PACK, SLOTS], F32, "g_raw")
         window = [own([P, TAILS], F32, "window%d" % n) for n in range(PACK - 1)]
         window.append(window[0])
 
@@ -70,8 +70,7 @@ def tile_attend_gdistm_t_pl_kernel(tc, hT, rT, G, hoffs, roffs, offs, out_0, out
         nc.sync.dma_start(r_list[:], roffs)
         nc.sync.dma_start(h_tab[0][:], h_rows[:, LANES[0], :])
         nc.sync.dma_start(h_list[:], hoffs)
-        for u in range(2):
-            nc.sync.dma_start(g_raw[u][:], g_rows[:, 2 * u : 2 * u + 2, :])
+        nc.sync.dma_start(g_raw[:], g_rows)
         for n in (1, 2):
             nc.sync.dma_start(r_tab[n][:], r_rows[:, LANES[n], :])
         nc.sync.dma_start(t_list[:], offs)
@@ -118,10 +117,16 @@ def tile_attend_gdistm_t_pl_kernel(tc, hT, rT, G, hoffs, roffs, offs, out_0, out
                 nc.scalar.copy(dst, turned[n][:, :, a * width : (a + 1) * width].rearrange("q u p -> q p u"))
 
         def multiply(n, c_codes):
+            quantize_c(n, c_codes)
+            product(n, c_codes)
+
+        def quantize_c(n, c_codes):
             width = P // len(c_grouped[n])
             for a, part in enumerate(c_grouped[n]):
                 cols = slice(a * width, (a + 1) * width)
                 nc.vector.quantize_mx(out=c_codes[:, cols].bitcast(E4M3), scales=c_scales[n][:, cols], in_=part)
+
+        def product(n, c_codes):
             nc.tensor.matmul_mx(
                 out=acc[n][:],
                 lhsT=c_codes[:].bitcast(E4M3),
@@ -158,25 +163,43 @@ def tile_attend_gdistm_t_pl_kernel(tc, hT, rT, G, hoffs, roffs, offs, out_0, out
         gather_r(0, r_got0[:])
         nc.gpsimd.memset(window[2][:], 0.0)
         c_rows0 = own([P, R], F32, "c_rows0")
-        gather_h(0, r_got0[:], c_rows0[:])
         c_pairs0 = own(c_pair_shape, BF16, "c_pairs0")
-        round_c(c_rows0[:], c_pairs0[:])
-        turn(0, halves(c_pairs0))
-        group(0)
-
-        g_grouped = [own([P, half, PACK], BF16, "g_grouped%d" % a) for a in range(2)]
-        for u in range(2):
-            for a in range(2):
-                src = g_raw[u][:, :, a * half : (a + 1) * half].rearrange("q e c -> q c e")
-                nc.vector.tensor_copy(g_grouped[a][:, :, 2 * u : 2 * u + 2], src)
         for a in range(2):
+            part = slice(a * R // 2, (a + 1) * R // 2)
+            nc.vector.tensor_tensor(c_rows0[:, part], h_tab[0][:].indirect(h_list[:, a * R // 32 : (a + 1) * R // 32]), r_got0[:, part], mult)
+            dst = c_pairs0[:].rearrange("p (u q e) -> p u q e", u=2, e=2)[:, :, a * P // 2 : (a + 1) * P // 2, :]
+            nc.scalar.copy(dst, c_rows0[:, part].rearrange("p (q u e) -> p u q e", u=2, e=2))
+
+        g_parts = ((0, 256), (256, 384), (384, 512))
+        g_grouped = [own([P, hi - lo, PACK], BF16, "g_grouped%d" % lo, "h_tab0" if lo == 384 else None) for lo, hi in g_parts]
+
+        def group_g(i):
+            lo, hi = g_parts[i]
+            dst = g_grouped[i][:].rearrange("q (c i) t -> q c t i", i=4)
+            src = g_raw[:, :, lo:hi].rearrange("q t (c i) -> q c t i", i=4)
+            if i < 2:
+                nc.vector.tensor_copy(dst, src)
+            else:
+                nc.scalar.copy(dst, src)
+
+        def quantize_g(i):
+            lo, hi = g_parts[i]
             nc.vector.quantize_mx(
-                out=g_codes[:, a * half : (a + 1) * half].bitcast(E5M2),
-                scales=g_scales[:, a * half : (a + 1) * half],
-                in_=g_grouped[a][:].rearrange("q c t -> q (c t)"),
+                out=g_codes[:, lo:hi].bitcast(E5M2),
+                scales=g_scales[:, lo:hi],
+                in_=g_grouped[i][:].rearrange("q c t -> q (c t)"),
             )
 
-        multiply(0, own([P, P], U32, "c_codes0"))
+        turn(0, halves(c_pairs0))
+        for i in range(3):
+            group_g(i)
+        group(0)
+        quantize_g(0)
+        c_codes0 = own([P, P], U32, "c_codes0")
+        quantize_c(0, c_codes0)
+        quantize_g(1)
+        quantize_g(2)
+        product(0, c_codes0)
         r_got12 = own([P, 2 * R], F32, "r_got12", "c_grouped0")
         gather_r(1, r_got12[:, :R])
         dt0a = own([P, half], F32, "dt0a", "r_tab1")
@@ -241,7 +264,8 @@ def tile_attend_gdistm_t_pl_kernel(tc, hT, rT, G, hoffs, roffs, offs, out_0, out
         scatter(dt3[:], 3, 0, SLOTS)
         store(3)
 
-        pieces = ((0, 512), (512, 1024), (1024, 1536), (1536, 1792), (1792, 2048))
+        pieces = ((0, 512), (512, 1024), (1024, 1280), (1280, 1536), (1536, 1792), (1792, 2048))
+        stores = ((0, 512), (512, 1024), (1024, 1536), (1536, 1792), (1792, 2048))
         y_grouped = [own([P, hi - lo, PACK], BF16, "y_grouped%d" % lo) for lo, hi in pieces]
         y_codes = own([P, TAILS], U32, "y_codes")
         y_scales = own([P, CHUNK], U8, "y_scales")
@@ -257,13 +281,13 @@ def tile_attend_gdistm_t_pl_kernel(tc, hT, rT, G, hoffs, roffs, offs, out_0, out
             else:
                 nc.scalar.copy(dst, src)
 
+        round_lane(3, 1, False, CHUNK // 2, CHUNK)
         round_lane(3, 0, True)
-        round_lane(3, 1, True)
-        round_lane(3, 2, False, CHUNK // 2, CHUNK)
-        round_lane(3, 2, True, 0, CHUNK // 2)
+        round_lane(3, 1, True, 0, CHUNK // 2)
+        round_lane(3, 2)
         round_lane(3, 3)
         for i in range(len(pieces)):
-            weave(i, i < 2)
+            weave(i, i < 3)
         for i, (lo, hi) in enumerate(pieces):
             for a in range(lo, hi, CHUNK // 2):
                 b = a + CHUNK // 2
@@ -273,7 +297,9 @@ def tile_attend_gdistm_t_pl_kernel(tc, hT, rT, G, hoffs, roffs, offs, out_0, out
                     scales=y_scales[4 * k :, a - k * CHUNK : b - k * CHUNK],
                     in_=y_grouped[i][:, a - lo : b - lo, :].rearrange("p c t -> p (c t)"),
                 )
-            nc.sync.dma_start(out_words[:, lo:hi], y_codes[:, lo:hi].bitcast(I32))
+            for first, last in stores:
+                if last == hi:
+                    nc.sync.dma_start(out_words[:, first:last], y_codes[:, first:last].bitcast(I32))
         scale_rows = out_scales.rearrange("f (k c) -> k f c", k=chunks)
         for q in range(4):
             queue = nc.sync if q < 2 else nc.scalar

@@ -157,11 +157,10 @@ def tile_attend_gdistm_t_pl_kernel(tc, hT, rT, G, hoffs, roffs, offs, out_0, out
         pair_shape = [P, 2, CHUNK, 2]
         c_pair_shape = [P, R]
 
-        nc.vector.memset(window[0][:], 0.0)
-        nc.vector.memset(window[1][:], 0.0)
+        for n in range(PACK - 1):
+            nc.vector.memset(window[n][:], 0.0)
         r_got0 = own([P, R], F32, "r_got0")
         gather_r(0, r_got0[:])
-        nc.gpsimd.memset(window[2][:], 0.0)
         c_rows0 = own([P, R], F32, "c_rows0")
         c_pairs0 = own(c_pair_shape, BF16, "c_pairs0")
         for a in range(2):
@@ -286,9 +285,9 @@ def tile_attend_gdistm_t_pl_kernel(tc, hT, rT, G, hoffs, roffs, offs, out_0, out
         round_lane(3, 1, True, 0, CHUNK // 2)
         round_lane(3, 2)
         round_lane(3, 3)
-        for i in range(len(pieces)):
-            weave(i, i < 3)
-        for i, (lo, hi) in enumerate(pieces):
+
+        def quantize_planes(i):
+            lo, hi = pieces[i]
             for a in range(lo, hi, CHUNK // 2):
                 b = a + CHUNK // 2
                 k = a // CHUNK
@@ -300,6 +299,14 @@ def tile_attend_gdistm_t_pl_kernel(tc, hT, rT, G, hoffs, roffs, offs, out_0, out
             for first, last in stores:
                 if last == hi:
                     nc.sync.dma_start(out_words[:, first:last], y_codes[:, first:last].bitcast(I32))
+
+        weave(0, True)
+        weave(1, True)
+        quantize_planes(0)
+        for i in range(2, len(pieces)):
+            weave(i, i < 3)
+        for i in range(1, len(pieces)):
+            quantize_planes(i)
         scale_rows = out_scales.rearrange("f (k c) -> k f c", k=chunks)
         for q in range(4):
             queue = nc.sync if q < 2 else nc.scalar

@@ -21,6 +21,7 @@ HEADS = 2048
 RELS = 1024
 TAILS = 2048
 CHUNK = 512
+PIECE = 256
 FLOPS = 2 * D * R * SLOTS
 
 LANES = (2, 0, 1, 3)
@@ -29,6 +30,7 @@ LANES = (2, 0, 1, 3)
 def tile_attend_gdistm_t_pl_kernel(tc, hT, rT, G, hoffs, roffs, offs, out_0, out_1, out_2):
     nc = tc.nc
     mult = mybir.AluOpType.mult
+    add = mybir.AluOpType.add
     half = SLOTS // 2
     chunks = TAILS // CHUNK
 
@@ -61,7 +63,8 @@ def tile_attend_gdistm_t_pl_kernel(tc, hT, rT, G, hoffs, roffs, offs, out_0, out
             own([P, HEADS], F32, "h_tab2"),
             placed([P, HEADS], F32, "h_tab3", 0),
         ]
-        r_tab = [own([P, RELS], F32, "r_tab%d" % n) for n in range(PACK)]
+        r_tab = [own([P, RELS], F32, "r_tab%d" % n) for n in range(PACK - 1)]
+        r_tab.append(placed([P, RELS], F32, "r_tab3", 32768))
         g_raw = own([P, PACK, SLOTS], F32, "g_raw")
         window = [own([P, TAILS], F32, "window%d" % n) for n in range(PACK - 1)]
         window.append(window[0])
@@ -146,15 +149,25 @@ def tile_attend_gdistm_t_pl_kernel(tc, hT, rT, G, hoffs, roffs, offs, out_0, out
         def store(n):
             nc.sync.dma_start(out_rows[:, LANES[n], :], window[n][:])
 
-        def round_lane(n, k, on_vector=False, lo=0, hi=CHUNK):
-            dst = pairs[k][:, LANES[n] // 2, lo:hi, LANES[n] % 2]
-            src = window[n][:, k * CHUNK + lo : k * CHUNK + hi]
-            if on_vector:
-                nc.vector.tensor_copy(dst, src)
-            else:
-                nc.scalar.copy(dst, src)
+        spans = ((768, 1280), (1280, 1792), (1792, 2048))
 
-        pair_shape = [P, 2, CHUNK, 2]
+        def round_lane(n, k, lo=0, hi=None):
+            first, last = spans[k]
+            hi = last - first if hi is None else hi
+            nc.scalar.copy(pairs[k][:, LANES[n] // 2, lo:hi, LANES[n] % 2], window[n][:, first + lo : first + hi])
+
+        def pair_shape(k):
+            return [P, 2, spans[k][1] - spans[k][0], 2]
+
+        def pool_round(dst, src):
+            nc.gpsimd.tensor_scalar(dst, src, 1.0, -0.0, mult, add)
+
+        def prefill(n, i, hi=PIECE):
+            pool_round(y_grouped[i][:, :hi, LANES[n]], window[n][:, i * PIECE : i * PIECE + hi])
+
+        def stage(n):
+            pool_round(staged[:, :, LANES[n]], window[n][:, 3 * PIECE - P : 3 * PIECE])
+
         c_pair_shape = [P, R]
 
         for n in range(PACK - 1):
@@ -223,89 +236,104 @@ def tile_attend_gdistm_t_pl_kernel(tc, hT, rT, G, hoffs, roffs, offs, out_0, out
         turn(2, halves(c_pairs2))
         multiply(1, placed([P, P], U32, "c_codes1", 8192))
         group(2)
-        pairs[0] = own(pair_shape, BF16, "pairs0", "c_pairs2")
+        pairs[0] = own(pair_shape(0), BF16, "pairs0", "c_pairs2")
         round_lane(0, 0)
-        pairs[2] = own(pair_shape, BF16, "pairs2", "c_grouped1")
-        round_lane(0, 2)
+        pairs[1] = own(pair_shape(1), BF16, "pairs1", "c_grouped1")
+        round_lane(0, 1)
 
         h_got3 = placed([P, R], F32, "h_got3", 17920)
         nc.vector.tensor_copy(h_got3[:], h_tab[3][:].indirect(h_list[:]))
         multiply(2, placed([P, P], U32, "c_codes2", 0))
         dt1 = placed([P, SLOTS], F32, "dt1", 1024)
         fetch(dt1[:], 1, 0, SLOTS)
-        pairs[1] = placed(pair_shape, BF16, "pairs1", 6144)
-        round_lane(0, 1)
+        pairs[2] = placed(pair_shape(2), BF16, "pairs2", 7168)
+        round_lane(0, 2)
         c_rows3 = own([P, R], F32, "c_rows3")
         nc.vector.tensor_tensor(c_rows3[:], r_tab[3][:].indirect(r_list[:]), h_got3[:], mult)
         scatter(dt1[:], 1, 0, SLOTS)
+        y_grouped = [placed([P, PIECE, PACK], BF16, "y_grouped%d" % i, at) for i, at in enumerate((32768, 34816, 17920))]
+        y_grouped.extend(own([P, PIECE, PACK], BF16, "y_grouped%d" % i) for i in range(3, TAILS // PIECE))
+        staged = own([P, P, 2], BF16, "staged")
+        for i in range(3):
+            prefill(0, i)
         c_first3 = own([P, 2 * P], BF16, "c_first3")
         scratch = [pairs[k][:].rearrange("p u c e -> p (u c e)")[:, : 2 * P] for k in range(3)]
-        c_halves3 = [c_first3[:], scratch[1]]
+        c_halves3 = [c_first3[:], scratch[2]]
         for u in range(2):
             round_c_half(c_rows3[:], c_halves3[u], u)
         turn(3, c_halves3)
-        c_grouped[3] = [scratch[0], scratch[2]]
+        c_grouped[3] = [scratch[0], scratch[1]]
         group(3)
         dt2 = placed([P, SLOTS], F32, "dt2", 24832)
         fetch(dt2[:], 2, 0, SLOTS)
         multiply(3, own([P, P], U32, "c_codes3"))
-        pairs[3] = placed(pair_shape, BF16, "pairs3", 26880)
-        round_lane(0, 3)
         dt3 = own([P, SLOTS], F32, "dt3")
         fetch(dt3[:], 3, 0, SLOTS)
         store(1)
-        for k in (1, 0, 2, 3):
+        for k in (2, 0, 1):
             round_lane(1, k)
+        stage(1)
+        for i in range(3):
+            prefill(1, i, PIECE if i < 2 else P)
         scatter(dt2[:], 2, 0, SLOTS)
         store(2)
-        for k in range(chunks):
+        for k in range(3):
             round_lane(2, k)
+        for i in range(3):
+            prefill(2, i, PIECE if i < 2 else P)
+        stage(2)
         scatter(dt3[:], 3, 0, SLOTS)
         store(3)
 
-        pieces = ((0, 512), (512, 1024), (1024, 1280), (1280, 1536), (1536, 1792), (1792, 2048))
-        stores = ((0, 512), (512, 1024), (1024, 1536), (1536, 1792), (1792, 2048))
-        y_grouped = [own([P, hi - lo, PACK], BF16, "y_grouped%d" % lo) for lo, hi in pieces]
         y_codes = own([P, TAILS], U32, "y_codes")
         y_scales = own([P, CHUNK], U8, "y_scales")
+        stores = ((0, 512), (512, 1024), (1024, 1536), (1536, 1792), (1792, 2048))
+
+        def words(i):
+            return y_grouped[i][:].rearrange("p c t -> p (c t)").bitcast(F32).rearrange("p (c u) -> p c u", u=2)
+
+        def home(i):
+            k = max(k for k in range(3) if spans[k][0] <= i * PIECE)
+            return k, i * PIECE - spans[k][0]
 
         def weave(i, on_vector):
-            lo, hi = pieces[i]
-            k = lo // CHUNK
-            dst = y_grouped[i][:].rearrange("p c t -> p (c t)").bitcast(F32).rearrange("p (c u) -> p c u", u=2)
+            k, lo = home(i)
             src = pairs[k][:].rearrange("p u c e -> p (u c e)").bitcast(F32).rearrange("p (u c) -> p c u", u=2)
-            src = src[:, lo - k * CHUNK : hi - k * CHUNK, :]
             if on_vector:
-                nc.vector.tensor_copy(dst, src)
+                nc.vector.tensor_copy(words(i), src[:, lo : lo + PIECE, :])
             else:
-                nc.scalar.copy(dst, src)
+                nc.scalar.copy(words(i), src[:, lo : lo + PIECE, :])
 
-        round_lane(3, 1, False, CHUNK // 2, CHUNK)
-        round_lane(3, 0, True)
-        round_lane(3, 1, True, 0, CHUNK // 2)
-        round_lane(3, 2)
-        round_lane(3, 3)
+        def finish(i):
+            nc.vector.tensor_copy(y_grouped[i][:, :, LANES[3]], window[3][:, i * PIECE : (i + 1) * PIECE])
 
         def quantize_planes(i):
-            lo, hi = pieces[i]
-            for a in range(lo, hi, CHUNK // 2):
-                b = a + CHUNK // 2
-                k = a // CHUNK
-                nc.vector.quantize_mx(
-                    out=y_codes[:, a:b].bitcast(E4M3),
-                    scales=y_scales[4 * k :, a - k * CHUNK : b - k * CHUNK],
-                    in_=y_grouped[i][:, a - lo : b - lo, :].rearrange("p c t -> p (c t)"),
-                )
+            a, b = i * PIECE, (i + 1) * PIECE
+            k = a // CHUNK
+            nc.vector.quantize_mx(
+                out=y_codes[:, a:b].bitcast(E4M3),
+                scales=y_scales[4 * k :, a - k * CHUNK : b - k * CHUNK],
+                in_=y_grouped[i][:].rearrange("p c t -> p (c t)"),
+            )
             for first, last in stores:
-                if last == hi:
+                if last == b:
                     nc.sync.dma_start(out_words[:, first:last], y_codes[:, first:last].bitcast(I32))
 
-        weave(0, True)
-        weave(1, True)
+        nc.vector.tensor_copy(words(2)[:, P:, 0], staged[:].rearrange("p c e -> p (c e)").bitcast(F32))
+        for i in range(3, TAILS // PIECE):
+            k, lo = home(i)
+            round_lane(3, k, lo, lo + PIECE)
+        finish(0)
+        finish(1)
         quantize_planes(0)
-        for i in range(2, len(pieces)):
-            weave(i, i < 3)
-        for i in range(1, len(pieces)):
+        finish(2)
+        quantize_planes(1)
+        weave(3, True)
+        quantize_planes(2)
+        weave(4, True)
+        for i in range(5, TAILS // PIECE):
+            weave(i, False)
+        for i in range(3, TAILS // PIECE):
             quantize_planes(i)
         scale_rows = out_scales.rearrange("f (k c) -> k f c", k=chunks)
         for q in range(4):

@@ -63,16 +63,19 @@ def tile_attend_gdistm_t_pl_kernel(tc, hT, rT, G, hoffs, roffs, offs, out_0, out
             own([P, HEADS], F32, "h_tab2"),
             placed([P, HEADS], F32, "h_tab3", 0),
         ]
-        r_tab = [own([P, RELS], F32, "r_tab%d" % n) for n in range(PACK - 1)]
-        r_tab.append(placed([P, RELS], F32, "r_tab3", 32768))
+        r_tab = [
+            own([P, RELS], F32, "r_tab0"),
+            own([P, RELS], F32, "r_tab1"),
+            placed([P, RELS], F32, "r_tab2", 40960),
+            placed([P, RELS], F32, "r_tab3", 32768),
+        ]
         g_raw = own([P, PACK, SLOTS], F32, "g_raw")
-        window = [own([P, TAILS], F32, "window%d" % n) for n in range(PACK - 1)]
-        window.append(window[0])
+        window = [own([P, TAILS], F32, "window%d" % n) for n in range(2)]
 
         nc.sync.dma_start(r_tab[0][:], r_rows[:, LANES[0], :])
         nc.sync.dma_start(r_list[:], roffs)
-        nc.sync.dma_start(h_tab[0][:], h_rows[:, LANES[0], :])
         nc.sync.dma_start(h_list[:], hoffs)
+        nc.sync.dma_start(h_tab[0][:], h_rows[:, LANES[0], :])
         nc.sync.dma_start(g_raw[:], g_rows)
         for n in (1, 2):
             nc.sync.dma_start(r_tab[n][:], r_rows[:, LANES[n], :])
@@ -170,7 +173,7 @@ def tile_attend_gdistm_t_pl_kernel(tc, hT, rT, G, hoffs, roffs, offs, out_0, out
 
         c_pair_shape = [P, R]
 
-        for n in range(PACK - 1):
+        for n in range(2):
             nc.vector.memset(window[n][:], 0.0)
         r_got0 = own([P, R], F32, "r_got0")
         gather_r(0, r_got0[:])
@@ -219,7 +222,9 @@ def tile_attend_gdistm_t_pl_kernel(tc, hT, rT, G, hoffs, roffs, offs, out_0, out
         gather_r(2, r_got12[:, R:])
         scatter(dt0a[:], 0, 0, half)
 
-        c_rows1 = own([P, R], F32, "c_rows1", "r_tab2")
+        window.extend((placed([P, TAILS], F32, "window2", 43008), window[0]))
+        nc.gpsimd.memset(window[2][:], 0.0)
+        c_rows1 = placed([P, R], F32, "c_rows1", 40960)
         gather_h(1, r_got12[:, :R], c_rows1[:])
         dt0b = placed([P, half], F32, "dt0b", 16384)
         fetch(dt0b[:], 0, half, SLOTS)
@@ -236,8 +241,6 @@ def tile_attend_gdistm_t_pl_kernel(tc, hT, rT, G, hoffs, roffs, offs, out_0, out
         turn(2, halves(c_pairs2))
         multiply(1, placed([P, P], U32, "c_codes1", 8192))
         group(2)
-        pairs[0] = own(pair_shape(0), BF16, "pairs0", "c_pairs2")
-        round_lane(0, 0)
         pairs[1] = own(pair_shape(1), BF16, "pairs1", "c_grouped1")
         round_lane(0, 1)
 
@@ -246,12 +249,13 @@ def tile_attend_gdistm_t_pl_kernel(tc, hT, rT, G, hoffs, roffs, offs, out_0, out
         multiply(2, placed([P, P], U32, "c_codes2", 0))
         dt1 = placed([P, SLOTS], F32, "dt1", 1024)
         fetch(dt1[:], 1, 0, SLOTS)
-        pairs[2] = placed(pair_shape(2), BF16, "pairs2", 7168)
-        round_lane(0, 2)
+        pairs[0] = placed(pair_shape(0), BF16, "pairs0", 4096)
+        round_lane(0, 0)
         c_rows3 = own([P, R], F32, "c_rows3")
         nc.vector.tensor_tensor(c_rows3[:], r_tab[3][:].indirect(r_list[:]), h_got3[:], mult)
         scatter(dt1[:], 1, 0, SLOTS)
-        y_grouped = [placed([P, PIECE, PACK], BF16, "y_grouped%d" % i, at) for i, at in enumerate((32768, 34816, 17920))]
+        y_grouped = [placed([P, PIECE, PACK], BF16, "y_grouped%d" % i, at) for i, at in enumerate((31744, 35840, 17920))]
+        pairs[2] = placed(pair_shape(2), BF16, "pairs2", 33792)
         y_grouped.extend(own([P, PIECE, PACK], BF16, "y_grouped%d" % i) for i in range(3, TAILS // PIECE))
         staged = own([P, P, 2], BF16, "staged")
         for i in range(3):
@@ -261,6 +265,7 @@ def tile_attend_gdistm_t_pl_kernel(tc, hT, rT, G, hoffs, roffs, offs, out_0, out
         c_halves3 = [c_first3[:], scratch[2]]
         for u in range(2):
             round_c_half(c_rows3[:], c_halves3[u], u)
+        round_lane(0, 2)
         turn(3, c_halves3)
         c_grouped[3] = [scratch[0], scratch[1]]
         group(3)

@@ -94,7 +94,7 @@ def tile_attend_gdistm_t_pl_kernel(tc, hT, rT, G, hoffs, roffs, offs, out_0, out
         acc = [ps.tile([P, SLOTS], F32, name="acc%d" % n, tag="acc%d" % min(n, 2)) for n in range(PACK)]
         g_codes = own([P, SLOTS], U32, "g_codes")
         g_scales = own([P, SLOTS], U8, "g_scales")
-        c_grouped = {n: [own([P, P * PACK], BF16, "c_grouped%d" % n)[:]] for n in range(PACK - 1)}
+        c_grouped = {n: [own([P, P * PACK], BF16, "c_grouped%d" % n, "c_grouped%d" % min(n, 1))[:]] for n in range(PACK - 1)}
         pairs = {}
 
         def gather_r(n, r_got):
@@ -104,7 +104,8 @@ def tile_attend_gdistm_t_pl_kernel(tc, hT, rT, G, hoffs, roffs, offs, out_0, out
             nc.vector.tensor_tensor(c_rows, h_tab[n][:].indirect(h_list[:]), r_got, mult)
 
         def round_c(c_rows, c_pairs):
-            nc.scalar.copy(c_pairs.rearrange("p (u q e) -> p u q e", u=2, e=2), c_rows.rearrange("p (q u e) -> p u q e", u=2, e=2))
+            for u, c_half in enumerate(halves(c_pairs)):
+                round_c_half(c_rows, c_half, u)
 
         def round_c_half(c_rows, c_half, u):
             nc.scalar.copy(c_half.rearrange("p (q e) -> p q e", e=2), c_rows.rearrange("p (q u e) -> p u q e", u=2, e=2)[:, u])
@@ -183,7 +184,12 @@ def tile_attend_gdistm_t_pl_kernel(tc, hT, rT, G, hoffs, roffs, offs, out_0, out
             part = slice(a * R // 2, (a + 1) * R // 2)
             nc.vector.tensor_tensor(c_rows0[:, part], h_tab[0][:].indirect(h_list[:, a * R // 32 : (a + 1) * R // 32]), r_got0[:, part], mult)
             dst = c_pairs0[:].rearrange("p (u q e) -> p u q e", u=2, e=2)[:, :, a * P // 2 : (a + 1) * P // 2, :]
-            nc.scalar.copy(dst, c_rows0[:, part].rearrange("p (q u e) -> p u q e", u=2, e=2))
+            src = c_rows0[:, part].rearrange("p (q u e) -> p u q e", u=2, e=2)
+            if a == 0:
+                nc.scalar.copy(dst, src)
+            else:
+                for u in range(2):
+                    nc.scalar.copy(dst[:, u], src[:, u])
 
         g_parts = ((0, 256), (256, 384), (384, 512))
         g_grouped = [own([P, hi - lo, PACK], BF16, "g_grouped%d" % lo, "h_tab0" if lo == 384 else None) for lo, hi in g_parts]
@@ -241,12 +247,12 @@ def tile_attend_gdistm_t_pl_kernel(tc, hT, rT, G, hoffs, roffs, offs, out_0, out
         turn(2, halves(c_pairs2))
         multiply(1, placed([P, P], U32, "c_codes1", 8192))
         group(2)
-        pairs[1] = own(pair_shape(1), BF16, "pairs1", "c_grouped1")
-        round_lane(0, 1)
+        pairs[2] = own(pair_shape(2), BF16, "pairs2", "c_pairs2")
+        round_lane(0, 2)
 
         h_got3 = placed([P, R], F32, "h_got3", 17920)
         nc.vector.tensor_copy(h_got3[:], h_tab[3][:].indirect(h_list[:]))
-        multiply(2, placed([P, P], U32, "c_codes2", 0))
+        multiply(2, own([P, P], U32, "c_codes2"))
         dt1 = placed([P, SLOTS], F32, "dt1", 1024)
         fetch(dt1[:], 1, 0, SLOTS)
         pairs[0] = placed(pair_shape(0), BF16, "pairs0", 4096)
@@ -254,8 +260,8 @@ def tile_attend_gdistm_t_pl_kernel(tc, hT, rT, G, hoffs, roffs, offs, out_0, out
         c_rows3 = own([P, R], F32, "c_rows3")
         nc.vector.tensor_tensor(c_rows3[:], r_tab[3][:].indirect(r_list[:]), h_got3[:], mult)
         scatter(dt1[:], 1, 0, SLOTS)
-        y_grouped = [placed([P, PIECE, PACK], BF16, "y_grouped%d" % i, at) for i, at in enumerate((31744, 35840, 17920))]
-        pairs[2] = placed(pair_shape(2), BF16, "pairs2", 33792)
+        y_grouped = [placed([P, PIECE, PACK], BF16, "y_grouped%d" % i, at) for i, at in enumerate((30976, 18944, 16896))]
+        pairs[1] = placed(pair_shape(1), BF16, "pairs1", 33024)
         y_grouped.extend(own([P, PIECE, PACK], BF16, "y_grouped%d" % i) for i in range(3, TAILS // PIECE))
         staged = own([P, P, 2], BF16, "staged")
         for i in range(3):
@@ -265,7 +271,7 @@ def tile_attend_gdistm_t_pl_kernel(tc, hT, rT, G, hoffs, roffs, offs, out_0, out
         c_halves3 = [c_first3[:], scratch[2]]
         for u in range(2):
             round_c_half(c_rows3[:], c_halves3[u], u)
-        round_lane(0, 2)
+        round_lane(0, 1)
         turn(3, c_halves3)
         c_grouped[3] = [scratch[0], scratch[1]]
         group(3)

@@ -67,7 +67,7 @@ def tile_attend_gdistm_t_pl_kernel(tc, hT, rT, G, hoffs, roffs, offs, out_0, out
             own([P, RELS], F32, "r_tab0"),
             own([P, RELS], F32, "r_tab1"),
             placed([P, RELS], F32, "r_tab2", 40960),
-            placed([P, RELS], F32, "r_tab3", 32768),
+            placed([P, RELS], F32, "r_tab3", 53248),
         ]
         g_raw = own([P, PACK, SLOTS], F32, "g_raw")
         window = [own([P, TAILS], F32, "window%d" % n) for n in range(2)]
@@ -94,7 +94,7 @@ def tile_attend_gdistm_t_pl_kernel(tc, hT, rT, G, hoffs, roffs, offs, out_0, out
         acc = [ps.tile([P, SLOTS], F32, name="acc%d" % n, tag="acc%d" % min(n, 2)) for n in range(PACK)]
         g_codes = own([P, SLOTS], U32, "g_codes")
         g_scales = own([P, SLOTS], U8, "g_scales")
-        c_grouped = {n: [own([P, P * PACK], BF16, "c_grouped%d" % n, "c_grouped%d" % min(n, 1))[:]] for n in range(PACK - 1)}
+        c_grouped = {n: [own([P, P * PACK], BF16, "c_grouped%d" % n, "c_grouped%d" % n)[:]] for n in range(PACK - 1)}
         pairs = {}
 
         def gather_r(n, r_got):
@@ -158,10 +158,11 @@ def tile_attend_gdistm_t_pl_kernel(tc, hT, rT, G, hoffs, roffs, offs, out_0, out
         def round_lane(n, k, lo=0, hi=None):
             first, last = spans[k]
             hi = last - first if hi is None else hi
-            nc.scalar.copy(pairs[k][:, LANES[n] // 2, lo:hi, LANES[n] % 2], window[n][:, first + lo : first + hi])
+            dst = pairs[k].rearrange("p (u c e) -> p u c e", u=2, e=2)[:, LANES[n] // 2, lo:hi, LANES[n] % 2]
+            nc.scalar.copy(dst, window[n][:, first + lo : first + hi])
 
         def pair_shape(k):
-            return [P, 2, spans[k][1] - spans[k][0], 2]
+            return [P, PACK * (spans[k][1] - spans[k][0])]
 
         def pool_round(dst, src):
             nc.gpsimd.tensor_scalar(dst, src, 1.0, -0.0, mult, add)
@@ -247,36 +248,34 @@ def tile_attend_gdistm_t_pl_kernel(tc, hT, rT, G, hoffs, roffs, offs, out_0, out
         turn(2, halves(c_pairs2))
         multiply(1, placed([P, P], U32, "c_codes1", 8192))
         group(2)
-        pairs[2] = own(pair_shape(2), BF16, "pairs2", "c_pairs2")
-        round_lane(0, 2)
+        pairs[1] = own(pair_shape(1), BF16, "pairs1", "c_pairs2")[:]
+        round_lane(0, 1)
 
         h_got3 = placed([P, R], F32, "h_got3", 17920)
         nc.vector.tensor_copy(h_got3[:], h_tab[3][:].indirect(h_list[:]))
-        multiply(2, own([P, P], U32, "c_codes2"))
+        multiply(2, placed([P, P], U32, "c_codes2", 0))
         dt1 = placed([P, SLOTS], F32, "dt1", 1024)
         fetch(dt1[:], 1, 0, SLOTS)
-        pairs[0] = placed(pair_shape(0), BF16, "pairs0", 4096)
-        round_lane(0, 0)
+        pairs[2] = placed(pair_shape(2), BF16, "pairs2", 4096)[:]
+        round_lane(0, 2)
         c_rows3 = own([P, R], F32, "c_rows3")
         nc.vector.tensor_tensor(c_rows3[:], r_tab[3][:].indirect(r_list[:]), h_got3[:], mult)
         scatter(dt1[:], 1, 0, SLOTS)
-        y_grouped = [placed([P, PIECE, PACK], BF16, "y_grouped%d" % i, at) for i, at in enumerate((30976, 18944, 16896))]
-        pairs[1] = placed(pair_shape(1), BF16, "pairs1", 33024)
+        y_grouped = [placed([P, PIECE, PACK], BF16, "y_grouped%d" % i, at) for i, at in enumerate((53248, 55296, 17920))]
         y_grouped.extend(own([P, PIECE, PACK], BF16, "y_grouped%d" % i) for i in range(3, TAILS // PIECE))
         staged = own([P, P, 2], BF16, "staged")
         for i in range(3):
             prefill(0, i)
-        c_first3 = own([P, 2 * P], BF16, "c_first3")
-        scratch = [pairs[k][:].rearrange("p u c e -> p (u c e)")[:, : 2 * P] for k in range(3)]
-        c_halves3 = [c_first3[:], scratch[2]]
+        c_halves3 = [own([P, 2 * P], BF16, "c_first3")[:], pairs[2][:, : 2 * P]]
         for u in range(2):
             round_c_half(c_rows3[:], c_halves3[u], u)
-        round_lane(0, 1)
         turn(3, c_halves3)
-        c_grouped[3] = [scratch[0], scratch[1]]
+        pairs[0] = placed(pair_shape(0), BF16, "pairs0", 26880)[:]
+        c_grouped[3] = [pairs[k][:, : 2 * P] for k in range(2)]
         group(3)
         dt2 = placed([P, SLOTS], F32, "dt2", 24832)
         fetch(dt2[:], 2, 0, SLOTS)
+        round_lane(0, 0)
         multiply(3, own([P, P], U32, "c_codes3"))
         dt3 = own([P, SLOTS], F32, "dt3")
         fetch(dt3[:], 3, 0, SLOTS)
@@ -309,7 +308,7 @@ def tile_attend_gdistm_t_pl_kernel(tc, hT, rT, G, hoffs, roffs, offs, out_0, out
 
         def weave(i, on_vector):
             k, lo = home(i)
-            src = pairs[k][:].rearrange("p u c e -> p (u c e)").bitcast(F32).rearrange("p (u c) -> p c u", u=2)
+            src = pairs[k].bitcast(F32).rearrange("p (u c) -> p c u", u=2)
             if on_vector:
                 nc.vector.tensor_copy(words(i), src[:, lo : lo + PIECE, :])
             else:

@@ -70,7 +70,8 @@ def tile_attend_gdistm_t_pl_kernel(tc, hT, rT, G, hoffs, roffs, offs, out_0, out
             placed([P, RELS], F32, "r_tab3", 53248),
         ]
         g_raw = own([P, PACK, SLOTS], F32, "g_raw")
-        window = [own([P, TAILS], F32, "window%d" % n) for n in range(2)]
+        window = [own([P, TAILS], F32, "window%d" % n) for n in range(PACK - 1)]
+        window.append(window[0])
 
         nc.sync.dma_start(r_tab[0][:], r_rows[:, LANES[0], :])
         nc.sync.dma_start(r_list[:], roffs)
@@ -94,7 +95,7 @@ def tile_attend_gdistm_t_pl_kernel(tc, hT, rT, G, hoffs, roffs, offs, out_0, out
         acc = [ps.tile([P, SLOTS], F32, name="acc%d" % n, tag="acc%d" % min(n, 2)) for n in range(PACK)]
         g_codes = own([P, SLOTS], U32, "g_codes")
         g_scales = own([P, SLOTS], U8, "g_scales")
-        c_grouped = {n: [own([P, P * PACK], BF16, "c_grouped%d" % n, "c_grouped%d" % n)[:]] for n in range(PACK - 1)}
+        c_grouped = {n: [own([P, P * PACK], BF16, "c_grouped%d" % n, "c_grouped%d" % min(n, 1))[:]] for n in range(PACK - 1)}
         pairs = {}
 
         def gather_r(n, r_got):
@@ -104,8 +105,7 @@ def tile_attend_gdistm_t_pl_kernel(tc, hT, rT, G, hoffs, roffs, offs, out_0, out
             nc.vector.tensor_tensor(c_rows, h_tab[n][:].indirect(h_list[:]), r_got, mult)
 
         def round_c(c_rows, c_pairs):
-            for u, c_half in enumerate(halves(c_pairs)):
-                round_c_half(c_rows, c_half, u)
+            nc.scalar.copy(c_pairs.rearrange("p (u q e) -> p u q e", u=2, e=2), c_rows.rearrange("p (q u e) -> p u q e", u=2, e=2))
 
         def round_c_half(c_rows, c_half, u):
             nc.scalar.copy(c_half.rearrange("p (q e) -> p q e", e=2), c_rows.rearrange("p (q u e) -> p u q e", u=2, e=2)[:, u])
@@ -153,7 +153,7 @@ def tile_attend_gdistm_t_pl_kernel(tc, hT, rT, G, hoffs, roffs, offs, out_0, out
         def store(n):
             nc.sync.dma_start(out_rows[:, LANES[n], :], window[n][:])
 
-        spans = ((768, 1280), (1280, 1792), (1792, 2048))
+        spans = ((768, 1024), (1024, 1280), (1280, 1536), (1536, 2048))
 
         def round_lane(n, k, lo=0, hi=None):
             first, last = spans[k]
@@ -175,7 +175,7 @@ def tile_attend_gdistm_t_pl_kernel(tc, hT, rT, G, hoffs, roffs, offs, out_0, out
 
         c_pair_shape = [P, R]
 
-        for n in range(2):
+        for n in range(PACK - 1):
             nc.vector.memset(window[n][:], 0.0)
         r_got0 = own([P, R], F32, "r_got0")
         gather_r(0, r_got0[:])
@@ -229,8 +229,6 @@ def tile_attend_gdistm_t_pl_kernel(tc, hT, rT, G, hoffs, roffs, offs, out_0, out
         gather_r(2, r_got12[:, R:])
         scatter(dt0a[:], 0, 0, half)
 
-        window.extend((placed([P, TAILS], F32, "window2", 43008), window[0]))
-        nc.gpsimd.memset(window[2][:], 0.0)
         c_rows1 = placed([P, R], F32, "c_rows1", 40960)
         gather_h(1, r_got12[:, :R], c_rows1[:])
         dt0b = placed([P, half], F32, "dt0b", 16384)
@@ -248,20 +246,21 @@ def tile_attend_gdistm_t_pl_kernel(tc, hT, rT, G, hoffs, roffs, offs, out_0, out
         turn(2, halves(c_pairs2))
         multiply(1, placed([P, P], U32, "c_codes1", 8192))
         group(2)
-        pairs[1] = own(pair_shape(1), BF16, "pairs1", "c_pairs2")[:]
-        round_lane(0, 1)
+        pairs[0] = own(pair_shape(0), BF16, "pairs0", "c_pairs2")[:]
+        round_lane(0, 0)
 
         h_got3 = placed([P, R], F32, "h_got3", 17920)
         nc.vector.tensor_copy(h_got3[:], h_tab[3][:].indirect(h_list[:]))
-        multiply(2, placed([P, P], U32, "c_codes2", 0))
+        multiply(2, own([P, P], U32, "c_codes2"))
         dt1 = placed([P, SLOTS], F32, "dt1", 1024)
         fetch(dt1[:], 1, 0, SLOTS)
-        pairs[2] = placed(pair_shape(2), BF16, "pairs2", 4096)[:]
-        round_lane(0, 2)
+        pairs[1] = placed(pair_shape(1), BF16, "pairs1", 4096)[:]
+        round_lane(0, 1)
         c_rows3 = own([P, R], F32, "c_rows3")
         nc.vector.tensor_tensor(c_rows3[:], r_tab[3][:].indirect(r_list[:]), h_got3[:], mult)
         scatter(dt1[:], 1, 0, SLOTS)
-        y_grouped = [placed([P, PIECE, PACK], BF16, "y_grouped%d" % i, at) for i, at in enumerate((53248, 55296, 17920))]
+        y_grouped = [placed([P, PIECE, PACK], BF16, "y_grouped%d" % i, at) for i, at in enumerate((52224, 56320, 17920))]
+        pairs[2] = placed(pair_shape(2), BF16, "pairs2", 54272)[:]
         y_grouped.extend(own([P, PIECE, PACK], BF16, "y_grouped%d" % i) for i in range(3, TAILS // PIECE))
         staged = own([P, P, 2], BF16, "staged")
         for i in range(3):
@@ -269,25 +268,26 @@ def tile_attend_gdistm_t_pl_kernel(tc, hT, rT, G, hoffs, roffs, offs, out_0, out
         c_halves3 = [own([P, 2 * P], BF16, "c_first3")[:], pairs[2][:, : 2 * P]]
         for u in range(2):
             round_c_half(c_rows3[:], c_halves3[u], u)
+        round_lane(0, 2)
         turn(3, c_halves3)
-        pairs[0] = placed(pair_shape(0), BF16, "pairs0", 26880)[:]
+        pairs[3] = placed(pair_shape(3), BF16, "pairs3", 26880)[:]
         c_grouped[3] = [pairs[k][:, : 2 * P] for k in range(2)]
         group(3)
         dt2 = placed([P, SLOTS], F32, "dt2", 24832)
         fetch(dt2[:], 2, 0, SLOTS)
-        round_lane(0, 0)
+        round_lane(0, 3)
         multiply(3, own([P, P], U32, "c_codes3"))
         dt3 = own([P, SLOTS], F32, "dt3")
         fetch(dt3[:], 3, 0, SLOTS)
         store(1)
-        for k in (2, 0, 1):
+        for k in (2, 3, 0, 1):
             round_lane(1, k)
         stage(1)
         for i in range(3):
             prefill(1, i, PIECE if i < 2 else P)
         scatter(dt2[:], 2, 0, SLOTS)
         store(2)
-        for k in range(3):
+        for k in range(len(spans)):
             round_lane(2, k)
         for i in range(3):
             prefill(2, i, PIECE if i < 2 else P)
@@ -303,7 +303,7 @@ def tile_attend_gdistm_t_pl_kernel(tc, hT, rT, G, hoffs, roffs, offs, out_0, out
             return y_grouped[i][:].rearrange("p c t -> p (c t)").bitcast(F32).rearrange("p (c u) -> p c u", u=2)
 
         def home(i):
-            k = max(k for k in range(3) if spans[k][0] <= i * PIECE)
+            k = max(k for k in range(len(spans)) if spans[k][0] <= i * PIECE)
             return k, i * PIECE - spans[k][0]
 
         def weave(i, on_vector):

@@ -95,7 +95,11 @@ def tile_attend_gdistm_t_pl_kernel(tc, hT, rT, G, hoffs, roffs, offs, out_0, out
         acc = [ps.tile([P, SLOTS], F32, name="acc%d" % n, tag="acc%d" % min(n, 2)) for n in range(PACK)]
         g_codes = own([P, SLOTS], U32, "g_codes")
         g_scales = own([P, SLOTS], U8, "g_scales")
-        c_grouped = {n: [own([P, P * PACK], BF16, "c_grouped%d" % n, "c_grouped%d" % min(n, 1))[:]] for n in range(PACK - 1)}
+        c_grouped = {
+            0: [own([P, P * PACK], BF16, "c_grouped0")[:]],
+            1: [placed([P, P * PACK], BF16, "c_grouped1", 61440)[:]],
+            2: [placed([P, P * PACK], BF16, "c_grouped2", 60928)[:]],
+        }
         pairs = {}
 
         def gather_r(n, r_got):
@@ -153,7 +157,7 @@ def tile_attend_gdistm_t_pl_kernel(tc, hT, rT, G, hoffs, roffs, offs, out_0, out
         def store(n):
             nc.sync.dma_start(out_rows[:, LANES[n], :], window[n][:])
 
-        spans = ((768, 1024), (1024, 1280), (1280, 1536), (1536, 2048))
+        spans = ((768, 1024), (1024, 1280), (1280, 2048))
 
         def round_lane(n, k, lo=0, hi=None):
             first, last = spans[k]
@@ -224,7 +228,7 @@ def tile_attend_gdistm_t_pl_kernel(tc, hT, rT, G, hoffs, roffs, offs, out_0, out
         product(0, c_codes0)
         r_got12 = own([P, 2 * R], F32, "r_got12", "c_grouped0")
         gather_r(1, r_got12[:, :R])
-        dt0a = own([P, half], F32, "dt0a", "r_tab1")
+        dt0a = own([P, half], F32, "dt0a")
         fetch(dt0a[:], 0, 0, half)
         gather_r(2, r_got12[:, R:])
         scatter(dt0a[:], 0, 0, half)
@@ -246,7 +250,7 @@ def tile_attend_gdistm_t_pl_kernel(tc, hT, rT, G, hoffs, roffs, offs, out_0, out
         turn(2, halves(c_pairs2))
         multiply(1, placed([P, P], U32, "c_codes1", 8192))
         group(2)
-        pairs[0] = own(pair_shape(0), BF16, "pairs0", "c_pairs2")[:]
+        pairs[0] = placed(pair_shape(0), BF16, "pairs0", 61952)[:]
         round_lane(0, 0)
 
         h_got3 = placed([P, R], F32, "h_got3", 17920)
@@ -259,28 +263,26 @@ def tile_attend_gdistm_t_pl_kernel(tc, hT, rT, G, hoffs, roffs, offs, out_0, out
         c_rows3 = own([P, R], F32, "c_rows3")
         nc.vector.tensor_tensor(c_rows3[:], r_tab[3][:].indirect(r_list[:]), h_got3[:], mult)
         scatter(dt1[:], 1, 0, SLOTS)
-        y_grouped = [placed([P, PIECE, PACK], BF16, "y_grouped%d" % i, at) for i, at in enumerate((52224, 56320, 17920))]
-        pairs[2] = placed(pair_shape(2), BF16, "pairs2", 54272)[:]
+        y_grouped = [placed([P, PIECE, PACK], BF16, "y_grouped%d" % i, at) for i, at in enumerate((53248, 55296, 17920))]
         y_grouped.extend(own([P, PIECE, PACK], BF16, "y_grouped%d" % i) for i in range(3, TAILS // PIECE))
         staged = own([P, P, 2], BF16, "staged")
         for i in range(3):
             prefill(0, i)
-        c_halves3 = [own([P, 2 * P], BF16, "c_first3")[:], pairs[2][:, : 2 * P]]
+        c_halves3 = [own([P, 2 * P], BF16, "c_first3")[:], pairs[0][:, : 2 * P]]
         for u in range(2):
             round_c_half(c_rows3[:], c_halves3[u], u)
-        round_lane(0, 2)
         turn(3, c_halves3)
-        pairs[3] = placed(pair_shape(3), BF16, "pairs3", 26880)[:]
-        c_grouped[3] = [pairs[k][:, : 2 * P] for k in range(2)]
+        pairs[2] = placed(pair_shape(2), BF16, "pairs2", 26880)[:]
+        c_grouped[3] = [pairs[k][:, : 2 * P] for k in (1, 2)]
         group(3)
         dt2 = placed([P, SLOTS], F32, "dt2", 24832)
         fetch(dt2[:], 2, 0, SLOTS)
-        round_lane(0, 3)
+        round_lane(0, 2)
         multiply(3, own([P, P], U32, "c_codes3"))
         dt3 = own([P, SLOTS], F32, "dt3")
         fetch(dt3[:], 3, 0, SLOTS)
         store(1)
-        for k in (2, 3, 0, 1):
+        for k in range(len(spans)):
             round_lane(1, k)
         stage(1)
         for i in range(3):
@@ -297,7 +299,7 @@ def tile_attend_gdistm_t_pl_kernel(tc, hT, rT, G, hoffs, roffs, offs, out_0, out
 
         y_codes = own([P, TAILS], U32, "y_codes")
         y_scales = own([P, CHUNK], U8, "y_scales")
-        stores = ((0, 512), (512, 1024), (1024, 1536), (1536, 1792), (1792, 2048))
+        stores = ((0, 768), (768, 1280), (1280, 1792), (1792, 2048))
 
         def words(i):
             return y_grouped[i][:].rearrange("p c t -> p (c t)").bitcast(F32).rearrange("p (c u) -> p c u", u=2)

@@ -17,6 +17,7 @@ PACK = 4
 D = 512
 R = 512
 SLOTS = 512
+HALF = SLOTS // 2
 HEADS = 2048
 RELS = 1024
 TAILS = 2048
@@ -25,19 +26,21 @@ PIECE = 256
 FLOPS = 2 * D * R * SLOTS
 
 LANES = (2, 0, 1, 3)
+SPLIT = 1024
+EARLY = 768
+STAGED = 32
 
 
 def tile_attend_gdistm_t_pl_kernel(tc, hT, rT, G, hoffs, roffs, offs, out_0, out_1, out_2):
     nc = tc.nc
     mult = mybir.AluOpType.mult
     add = mybir.AluOpType.add
-    half = SLOTS // 2
+    copy = mybir.ActivationFunctionType.Copy
     chunks = TAILS // CHUNK
 
     with ExitStack() as ctx:
         lists = ctx.enter_context(tc.tile_pool(name="lists", bufs=1))
         sb = ctx.enter_context(tc.tile_pool(name="sb", bufs=1))
-        reuse = ctx.enter_context(tc.tile_pool(name="reuse", bufs=1))
         ps = ctx.enter_context(tc.psum_pool(name="ps", bufs=1))
 
         h_list = lists.tile([P, R // 16], U16, name="h_list")
@@ -54,270 +57,190 @@ def tile_attend_gdistm_t_pl_kernel(tc, hT, rT, G, hoffs, roffs, offs, out_0, out
         def own(shape, dtype, name, tag=None):
             return sb.tile(shape, dtype, name=name, tag=tag or name, align_bytes=64)
 
-        def placed(shape, dtype, name, offset):
-            return reuse.tile(shape, dtype, name=name, offset=offset, align_bytes=64)
-
-        h_tab = [
-            own([P, HEADS], F32, "h_tab0"),
-            placed([P, HEADS], F32, "h_tab1", 16384),
-            own([P, HEADS], F32, "h_tab2"),
-            placed([P, HEADS], F32, "h_tab3", 0),
-        ]
-        r_tab = [
-            own([P, RELS], F32, "r_tab0"),
-            own([P, RELS], F32, "r_tab1"),
-            placed([P, RELS], F32, "r_tab2", 40960),
-            placed([P, RELS], F32, "r_tab3", 53248),
-        ]
+        h_tab = [own([P, HEADS], F32, "h_tab%d" % n) for n in range(PACK)]
+        r_tab = [own([P, RELS], F32, "r_tab%d" % n) for n in range(PACK)]
         g_raw = own([P, PACK, SLOTS], F32, "g_raw")
-        window = [own([P, TAILS], F32, "window%d" % n) for n in range(PACK - 1)]
-        window.append(window[0])
+        window = [own([P, TAILS], F32, "window%d" % n) for n in range(PACK)]
 
         nc.sync.dma_start(r_tab[0][:], r_rows[:, LANES[0], :])
         nc.sync.dma_start(r_list[:], roffs)
         nc.sync.dma_start(h_list[:], hoffs)
         nc.sync.dma_start(h_tab[0][:], h_rows[:, LANES[0], :])
         nc.sync.dma_start(g_raw[:], g_rows)
-        for n in (1, 2):
-            nc.sync.dma_start(r_tab[n][:], r_rows[:, LANES[n], :])
+        nc.sync.dma_start(r_tab[1][:], r_rows[:, LANES[1], :])
         nc.sync.dma_start(t_list[:], offs)
-        nc.sync.dma_start(h_tab[2][:, : HEADS // 2], h_rows[:, LANES[2], : HEADS // 2])
         nc.sync.dma_start(h_tab[1][:], h_rows[:, LANES[1], :])
-        nc.sync.dma_start(h_tab[2][:, HEADS // 2 :], h_rows[:, LANES[2], HEADS // 2 :])
-        nc.sync.dma_start(h_tab[3][:], h_rows[:, LANES[3], :])
-        nc.sync.dma_start(r_tab[3][:], r_rows[:, LANES[3], :])
+        for n in (2, 3):
+            nc.sync.dma_start(r_tab[n][:], r_rows[:, LANES[n], :])
+            nc.sync.dma_start(h_tab[n][:], h_rows[:, LANES[n], :])
 
-        ident = placed([P, P], F32, "ident", 26624)
+        ident = own([P, P], F32, "ident")
         make_identity(nc, ident[:])
+        nc.vector.memset(window[0][:, : TAILS // 2 + 1], 0.0)
+        nc.vector.memset(window[0][:, TAILS // 2 + 1 :], 0.0)
+        nc.vector.memset(window[1][:, : TAILS // 2 - 7], 0.0)
+        nc.vector.memset(window[1][:, TAILS // 2 - 7 : TAILS // 2], 0.0)
+        nc.gpsimd.memset(window[1][:, TAILS // 2 :], 0.0)
+        for n in (2, 3):
+            nc.gpsimd.memset(window[n][:], 0.0)
+
+        pairs = own([P, PACK * TAILS], BF16, "pairs")
+
+        def pair_words(lo, hi):
+            return pairs[:].rearrange("p (u c e) -> p u c e", u=2, e=2)[:, :, lo:hi, :]
+
+        def in_upper_words(col, count):
+            first = 2 * TAILS + 2 * col
+            return pairs[:, first : first + count]
 
         c_scales = [own([P, P], U8, "c_scales%d" % n) for n in range(PACK)]
-        turned = [ps.tile([P, 2, P], F32, name="turned%d" % n) for n in range(PACK)]
-        acc = [ps.tile([P, SLOTS], F32, name="acc%d" % n, tag="acc%d" % min(n, 2)) for n in range(PACK)]
+        c_codes = [own([P, P], U32, "c_codes%d" % n) for n in range(PACK)]
+        turned = [ps.tile([P, 2, P], F32, name="turned%d" % n, tag="turned%d" % (n % 2)) for n in range(PACK)]
         g_codes = own([P, SLOTS], U32, "g_codes")
         g_scales = own([P, SLOTS], U8, "g_scales")
-        c_grouped = {
-            0: [own([P, P * PACK], BF16, "c_grouped0")[:]],
-            1: [placed([P, P * PACK], BF16, "c_grouped1", 61440)[:]],
-            2: [placed([P, P * PACK], BF16, "c_grouped2", 60928)[:]],
-        }
-        pairs = {}
+        c_rows = [own([P, R], F32, "c_rows%d" % n)[:] for n in range(PACK)]
+        c_pairs = [own([P, R], BF16, "c_pairs%d" % n)[:] for n in range(PACK - 1)] + [in_upper_words(384, R)]
+        c_grouped = {0: g_raw[:, 0, :HALF].bitcast(BF16), 3: in_upper_words(-P, R)}
+        r_got = {0: own([P, R], F32, "r_got0")[:], 2: own([P, R], F32, "r_got2")[:], 3: in_upper_words(640, 2 * R).bitcast(F32)}
+        dt = [own([P, SLOTS], F32, "dt%d" % n)[:] for n in range(PACK)]
 
-        def gather_r(n, r_got):
-            nc.vector.tensor_copy(r_got, r_tab[n][:].indirect(r_list[:]))
+        def gather_r(n):
+            nc.vector.tensor_copy(r_got[n], r_tab[n][:].indirect(r_list[:]))
 
-        def gather_h(n, r_got, c_rows):
-            nc.vector.tensor_tensor(c_rows, h_tab[n][:].indirect(h_list[:]), r_got, mult)
+        def gather_h(n, lo=0, hi=R):
+            nc.vector.tensor_tensor(c_rows[n][:, lo:hi], h_tab[n][:].indirect(h_list[:, lo // 16 : hi // 16]), r_got[n][:, lo:hi], mult)
 
-        def round_c(c_rows, c_pairs):
-            nc.scalar.copy(c_pairs.rearrange("p (u q e) -> p u q e", u=2, e=2), c_rows.rearrange("p (q u e) -> p u q e", u=2, e=2))
-
-        def round_c_half(c_rows, c_half, u):
-            nc.scalar.copy(c_half.rearrange("p (q e) -> p q e", e=2), c_rows.rearrange("p (q u e) -> p u q e", u=2, e=2)[:, u])
-
-        def halves(c_pairs):
-            return [c_pairs[:, u * 2 * P : (u + 1) * 2 * P] for u in range(2)]
-
-        def turn(n, c_halves):
-            for u in range(2):
-                nc.tensor.transpose(turned[n][:, u, :], c_halves[u].bitcast(F32), ident[:])
-
-        def group(n):
-            width = P // len(c_grouped[n])
-            for a, part in enumerate(c_grouped[n]):
-                dst = part.bitcast(F32).rearrange("q (p u) -> q p u", u=2)
-                nc.scalar.copy(dst, turned[n][:, :, a * width : (a + 1) * width].rearrange("q u p -> q p u"))
-
-        def multiply(n, c_codes):
-            quantize_c(n, c_codes)
-            product(n, c_codes)
-
-        def quantize_c(n, c_codes):
-            width = P // len(c_grouped[n])
-            for a, part in enumerate(c_grouped[n]):
-                cols = slice(a * width, (a + 1) * width)
-                nc.vector.quantize_mx(out=c_codes[:, cols].bitcast(E4M3), scales=c_scales[n][:, cols], in_=part)
-
-        def product(n, c_codes):
-            nc.tensor.matmul_mx(
-                out=acc[n][:],
-                lhsT=c_codes[:].bitcast(E4M3),
-                lhsT_scale=c_scales[n][:],
-                rhs=g_codes[:].bitcast(E5M2),
-                rhs_scale=g_scales[:],
-                start=True,
-                stop=True,
-            )
-
-        def fetch(dt, n, lo, hi):
-            nc.scalar.copy(dt, acc[n][:, lo:hi])
-
-        def scatter(dt, n, lo, hi):
-            nc.vector.tensor_copy(window[n][:].indirect(t_list[:, lo // 16 : hi // 16]), dt)
-
-        def store(n):
-            nc.sync.dma_start(out_rows[:, LANES[n], :], window[n][:])
-
-        spans = ((768, 1024), (1024, 1280), (1280, 2048))
-
-        def round_lane(n, k, lo=0, hi=None):
-            first, last = spans[k]
-            hi = last - first if hi is None else hi
-            dst = pairs[k].rearrange("p (u c e) -> p u c e", u=2, e=2)[:, LANES[n] // 2, lo:hi, LANES[n] % 2]
-            nc.scalar.copy(dst, window[n][:, first + lo : first + hi])
-
-        def pair_shape(k):
-            return [P, PACK * (spans[k][1] - spans[k][0])]
+        def c_views(n, lo=0, hi=R):
+            dst = c_pairs[n].rearrange("p (u q e) -> p u q e", u=2, e=2)[:, :, lo // PACK : hi // PACK, :]
+            return dst, c_rows[n][:, lo:hi].rearrange("p (q u e) -> p u q e", u=2, e=2)
 
         def pool_round(dst, src):
             nc.gpsimd.tensor_scalar(dst, src, 1.0, -0.0, mult, add)
 
-        def prefill(n, i, hi=PIECE):
-            pool_round(y_grouped[i][:, :hi, LANES[n]], window[n][:, i * PIECE : i * PIECE + hi])
+        def turn(n):
+            for u in range(2):
+                nc.tensor.transpose(turned[n][:, u, :], c_pairs[n][:, u * 2 * P : (u + 1) * 2 * P].bitcast(F32), ident[:])
 
-        def stage(n):
-            pool_round(staged[:, :, LANES[n]], window[n][:, 3 * PIECE - P : 3 * PIECE])
+        def group(n):
+            dst = c_grouped[n].bitcast(F32).rearrange("q (p u) -> q p u", u=2)
+            nc.vector.tensor_copy(dst, turned[n][:].rearrange("q u p -> q p u"))
 
-        c_pair_shape = [P, R]
+        def quantize_c(n):
+            nc.vector.quantize_mx(out=c_codes[n][:].bitcast(E4M3), scales=c_scales[n][:], in_=c_grouped[n])
 
-        for n in range(PACK - 1):
-            nc.vector.memset(window[n][:], 0.0)
-        r_got0 = own([P, R], F32, "r_got0")
-        gather_r(0, r_got0[:])
-        c_rows0 = own([P, R], F32, "c_rows0")
-        c_pairs0 = own(c_pair_shape, BF16, "c_pairs0")
-        for a in range(2):
-            part = slice(a * R // 2, (a + 1) * R // 2)
-            nc.vector.tensor_tensor(c_rows0[:, part], h_tab[0][:].indirect(h_list[:, a * R // 32 : (a + 1) * R // 32]), r_got0[:, part], mult)
-            dst = c_pairs0[:].rearrange("p (u q e) -> p u q e", u=2, e=2)[:, :, a * P // 2 : (a + 1) * P // 2, :]
-            src = c_rows0[:, part].rearrange("p (q u e) -> p u q e", u=2, e=2)
-            if a == 0:
-                nc.scalar.copy(dst, src)
-            else:
-                for u in range(2):
-                    nc.scalar.copy(dst[:, u], src[:, u])
+        def product(n, lo, hi):
+            acc = ps.tile([P, hi - lo], F32, name="acc%d_%d" % (n, lo))
+            nc.tensor.matmul_mx(
+                out=acc[:],
+                lhsT=c_codes[n][:].bitcast(E4M3),
+                lhsT_scale=c_scales[n][:],
+                rhs=g_codes[:, lo:hi].bitcast(E5M2),
+                rhs_scale=g_scales[:, lo:hi],
+                start=True,
+                stop=True,
+            )
+            return acc
 
-        g_parts = ((0, 256), (256, 384), (384, 512))
-        g_grouped = [own([P, hi - lo, PACK], BF16, "g_grouped%d" % lo, "h_tab0" if lo == 384 else None) for lo, hi in g_parts]
+        def scatter_on_scalar(n, lo):
+            target = window[n][:].indirect(t_list[:, lo // 16 : (lo + HALF) // 16])
+            nc.scalar.activation(target, dt[n][:, lo : lo + HALF], copy)
 
-        def group_g(i):
-            lo, hi = g_parts[i]
-            dst = g_grouped[i][:].rearrange("q (c i) t -> q c t i", i=4)
-            src = g_raw[:, :, lo:hi].rearrange("q t (c i) -> q c t i", i=4)
-            if i < 2:
-                nc.vector.tensor_copy(dst, src)
-            else:
-                nc.scalar.copy(dst, src)
+        def store(n):
+            nc.sync.dma_start(out_rows[:, LANES[n], :], window[n][:])
 
-        def quantize_g(i):
-            lo, hi = g_parts[i]
+        def lane_views(n, lo, hi):
+            return pair_words(lo, hi)[:, LANES[n] // 2, :, LANES[n] % 2], window[n][:, lo:hi]
+
+        gather_r(0)
+        gather_h(0, 0, R // 2)
+        nc.scalar.copy(*c_views(0, 0, R // 2))
+        gather_h(0, R // 2, R)
+        nc.vector.tensor_copy(*c_views(0, R // 2, R))
+        turn(0)
+
+        g_grouped = [own([P, HALF, PACK], BF16, "g_grouped%d" % a) for a in range(2)]
+
+        def g_views(a, lo, hi):
+            dst = g_grouped[a][:, lo:hi, :].rearrange("q (c i) t -> q c t i", i=4)
+            return dst, g_raw[:, :, a * HALF + lo : a * HALF + hi].rearrange("q t (c i) -> q c t i", i=4)
+
+        def quantize_g(a):
+            cols = slice(a * HALF, (a + 1) * HALF)
             nc.vector.quantize_mx(
-                out=g_codes[:, lo:hi].bitcast(E5M2),
-                scales=g_scales[:, lo:hi],
-                in_=g_grouped[i][:].rearrange("q c t -> q (c t)"),
+                out=g_codes[:, cols].bitcast(E5M2),
+                scales=g_scales[:, cols],
+                in_=g_grouped[a][:].rearrange("q c t -> q (c t)"),
             )
 
-        turn(0, halves(c_pairs0))
-        for i in range(3):
-            group_g(i)
+        for a in range(2):
+            nc.scalar.copy(*g_views(a, 0, P))
+        for a in range(2):
+            nc.vector.tensor_copy(*g_views(a, P, HALF))
         group(0)
         quantize_g(0)
-        c_codes0 = own([P, P], U32, "c_codes0")
-        quantize_c(0, c_codes0)
+        quantize_c(0)
         quantize_g(1)
-        quantize_g(2)
-        product(0, c_codes0)
-        r_got12 = own([P, 2 * R], F32, "r_got12", "c_grouped0")
-        gather_r(1, r_got12[:, :R])
-        dt0a = own([P, half], F32, "dt0a")
-        fetch(dt0a[:], 0, 0, half)
-        gather_r(2, r_got12[:, R:])
-        scatter(dt0a[:], 0, 0, half)
-
-        c_rows1 = placed([P, R], F32, "c_rows1", 40960)
-        gather_h(1, r_got12[:, :R], c_rows1[:])
-        dt0b = placed([P, half], F32, "dt0b", 16384)
-        fetch(dt0b[:], 0, half, SLOTS)
-        c_pairs1 = placed(c_pair_shape, BF16, "c_pairs1", 17408)
-        round_c(c_rows1[:], c_pairs1[:])
-        c_rows2 = own([P, R], F32, "c_rows2")
-        gather_h(2, r_got12[:, R:], c_rows2[:])
-        scatter(dt0b[:], 0, half, SLOTS)
+        for lo in (0, HALF):
+            acc = product(0, lo, lo + HALF)
+            nc.scalar.copy(dt[0][:, lo : lo + HALF], acc[:])
+        for lo in (0, HALF):
+            scatter_on_scalar(0, lo)
         store(0)
-        turn(1, halves(c_pairs1))
-        c_pairs2 = own(c_pair_shape, BF16, "c_pairs2")
-        round_c(c_rows2[:], c_pairs2[:])
-        group(1)
-        turn(2, halves(c_pairs2))
-        multiply(1, placed([P, P], U32, "c_codes1", 8192))
-        group(2)
-        pairs[0] = placed(pair_shape(0), BF16, "pairs0", 61952)[:]
-        round_lane(0, 0)
+        nc.scalar.copy(*lane_views(0, TAILS - EARLY, TAILS))
 
-        h_got3 = placed([P, R], F32, "h_got3", 17920)
-        nc.vector.tensor_copy(h_got3[:], h_tab[3][:].indirect(h_list[:]))
-        multiply(2, own([P, P], U32, "c_codes2"))
-        dt1 = placed([P, SLOTS], F32, "dt1", 1024)
-        fetch(dt1[:], 1, 0, SLOTS)
-        pairs[1] = placed(pair_shape(1), BF16, "pairs1", 4096)[:]
-        round_lane(0, 1)
-        c_rows3 = own([P, R], F32, "c_rows3")
-        nc.vector.tensor_tensor(c_rows3[:], r_tab[3][:].indirect(r_list[:]), h_got3[:], mult)
-        scatter(dt1[:], 1, 0, SLOTS)
-        y_grouped = [placed([P, PIECE, PACK], BF16, "y_grouped%d" % i, at) for i, at in enumerate((53248, 55296, 17920))]
-        y_grouped.extend(own([P, PIECE, PACK], BF16, "y_grouped%d" % i) for i in range(3, TAILS // PIECE))
-        staged = own([P, P, 2], BF16, "staged")
-        for i in range(3):
-            prefill(0, i)
-        c_halves3 = [own([P, 2 * P], BF16, "c_first3")[:], pairs[0][:, : 2 * P]]
-        for u in range(2):
-            round_c_half(c_rows3[:], c_halves3[u], u)
-        turn(3, c_halves3)
-        pairs[2] = placed(pair_shape(2), BF16, "pairs2", 26880)[:]
-        c_grouped[3] = [pairs[k][:, : 2 * P] for k in (1, 2)]
+        r_got[1] = own([P, R], F32, "r_got1", "g_grouped1")[:]
+        gather_r(1)
+        for n in (1, 2):
+            gather_h(n)
+            pool_round(*c_views(n))
+            gather_r(n + 1)
+            turn(n)
+            if n == 2:
+                gather_h(3)
+            c_grouped[n] = own([P, R], BF16, "c_grouped%d" % n, ("r_tab2", "h_tab3")[n - 1])[:]
+            group(n)
+            if n == 2:
+                nc.vector.tensor_copy(*c_views(3))
+            quantize_c(n)
+            acc = product(n, 0, SLOTS)
+            for lo in (0, HALF):
+                nc.scalar.copy(dt[n][:, lo : lo + HALF], acc[:, lo : lo + HALF])
+            for lo in (0, HALF):
+                scatter_on_scalar(n, lo)
+            store(n)
+
+        def early_lane(lo, hi):
+            nc.vector.tensor_copy(*lane_views(0, lo, hi))
+
+        early_lane(640, TAILS - EARLY)
+        turn(3)
         group(3)
-        dt2 = placed([P, SLOTS], F32, "dt2", 24832)
-        fetch(dt2[:], 2, 0, SLOTS)
-        round_lane(0, 2)
-        multiply(3, own([P, P], U32, "c_codes3"))
-        dt3 = own([P, SLOTS], F32, "dt3")
-        fetch(dt3[:], 3, 0, SLOTS)
-        store(1)
-        for k in range(len(spans)):
-            round_lane(1, k)
-        stage(1)
-        for i in range(3):
-            prefill(1, i, PIECE if i < 2 else P)
-        scatter(dt2[:], 2, 0, SLOTS)
-        store(2)
-        for k in range(len(spans)):
-            round_lane(2, k)
-        for i in range(3):
-            prefill(2, i, PIECE if i < 2 else P)
-        stage(2)
-        scatter(dt3[:], 3, 0, SLOTS)
+        early_lane(384, 640)
+        quantize_c(3)
+        early_lane(0, 384)
+        for lo in (0, HALF):
+            acc = product(3, lo, lo + HALF)
+            nc.vector.tensor_copy(dt[3][:, lo : lo + HALF], acc[:])
+        for lo in (0, HALF):
+            nc.vector.tensor_copy(window[3][:].indirect(t_list[:, lo // 16 : (lo + HALF) // 16]), dt[3][:, lo : lo + HALF])
         store(3)
+        last = TAILS - STAGED
+        pool_round(*lane_views(1, 0, last))
+        staged = lane_views(2, last - STAGED, last)[0]
+        pool_round(staged, window[1][:, last:])
+        nc.scalar.copy(lane_views(1, last, TAILS)[0], staged)
+        nc.scalar.copy(*lane_views(2, SPLIT, TAILS))
+        pool_round(*lane_views(2, 0, SPLIT))
 
+        y_grouped = [own([P, PIECE, PACK], BF16, "y_grouped%d" % i) for i in range(TAILS // PIECE)]
         y_codes = own([P, TAILS], U32, "y_codes")
         y_scales = own([P, CHUNK], U8, "y_scales")
+        order = range(TAILS // PIECE)
         stores = ((0, 768), (768, 1280), (1280, 1792), (1792, 2048))
 
-        def words(i):
-            return y_grouped[i][:].rearrange("p c t -> p (c t)").bitcast(F32).rearrange("p (c u) -> p c u", u=2)
-
-        def home(i):
-            k = max(k for k in range(len(spans)) if spans[k][0] <= i * PIECE)
-            return k, i * PIECE - spans[k][0]
-
-        def weave(i, on_vector):
-            k, lo = home(i)
-            src = pairs[k].bitcast(F32).rearrange("p (u c) -> p c u", u=2)
-            if on_vector:
-                nc.vector.tensor_copy(words(i), src[:, lo : lo + PIECE, :])
-            else:
-                nc.scalar.copy(words(i), src[:, lo : lo + PIECE, :])
-
-        def finish(i):
-            nc.vector.tensor_copy(y_grouped[i][:, :, LANES[3]], window[3][:, i * PIECE : (i + 1) * PIECE])
+        def weave_views(i):
+            dst = y_grouped[i][:].rearrange("p c t -> p (c t)").bitcast(F32).rearrange("p (c u) -> p c u", u=2)
+            return dst, pairs[:].bitcast(F32).rearrange("p (u c) -> p c u", u=2)[:, i * PIECE : (i + 1) * PIECE, :]
 
         def quantize_planes(i):
             a, b = i * PIECE, (i + 1) * PIECE
@@ -331,22 +254,17 @@ def tile_attend_gdistm_t_pl_kernel(tc, hT, rT, G, hoffs, roffs, offs, out_0, out
                 if last == b:
                     nc.sync.dma_start(out_words[:, first:last], y_codes[:, first:last].bitcast(I32))
 
-        nc.vector.tensor_copy(words(2)[:, P:, 0], staged[:].rearrange("p c e -> p (c e)").bitcast(F32))
-        for i in range(3, TAILS // PIECE):
-            k, lo = home(i)
-            round_lane(3, k, lo, lo + PIECE)
-        finish(0)
-        finish(1)
-        quantize_planes(0)
-        finish(2)
-        quantize_planes(1)
-        weave(3, True)
-        quantize_planes(2)
-        weave(4, True)
-        for i in range(5, TAILS // PIECE):
-            weave(i, False)
-        for i in range(3, TAILS // PIECE):
-            quantize_planes(i)
+        nc.vector.tensor_copy(*lane_views(3, order[0] * PIECE, (order[0] + 1) * PIECE))
+        for i in order[1:]:
+            nc.scalar.copy(*lane_views(3, i * PIECE, (i + 1) * PIECE))
+        nc.vector.tensor_copy(*weave_views(order[0]))
+        for j in range(1, 6):
+            nc.vector.tensor_copy(*weave_views(order[j]))
+            quantize_planes(order[j - 1])
+        for j in (6, 7):
+            nc.scalar.copy(*weave_views(order[j]))
+        for j in (5, 6, 7):
+            quantize_planes(order[j])
         scale_rows = out_scales.rearrange("f (k c) -> k f c", k=chunks)
         for q in range(4):
             queue = nc.sync if q < 2 else nc.scalar

@@ -26,9 +26,8 @@ PIECE = 256
 FLOPS = 2 * D * R * SLOTS
 
 LANES = (2, 0, 1, 3)
-SPLIT = 1024
-EARLY = 768
-STAGED = 32
+SPLIT = 1280
+EARLY = 1280
 
 
 def tile_attend_gdistm_t_pl_kernel(tc, hT, rT, G, hoffs, roffs, offs, out_0, out_1, out_2):
@@ -41,6 +40,7 @@ def tile_attend_gdistm_t_pl_kernel(tc, hT, rT, G, hoffs, roffs, offs, out_0, out
     with ExitStack() as ctx:
         lists = ctx.enter_context(tc.tile_pool(name="lists", bufs=1))
         sb = ctx.enter_context(tc.tile_pool(name="sb", bufs=1))
+        reuse = ctx.enter_context(tc.tile_pool(name="reuse", bufs=1))
         ps = ctx.enter_context(tc.psum_pool(name="ps", bufs=1))
 
         h_list = lists.tile([P, R // 16], U16, name="h_list")
@@ -49,7 +49,7 @@ def tile_attend_gdistm_t_pl_kernel(tc, hT, rT, G, hoffs, roffs, offs, out_0, out
 
         h_rows = hT.rearrange("(p t) c -> p t c", t=PACK)
         r_rows = rT.rearrange("(p t) c -> p t c", t=PACK)
-        g_rows = G.rearrange("(q t) i -> q t i", t=PACK)
+        g_rows = G.rearrange("(q t) i -> q (t i)", t=PACK)
         out_rows = out_0.rearrange("(p t) c -> p t c", t=PACK)
         out_words = out_1[0].rearrange("p c t -> p (c t)").bitcast(I32)
         out_scales = out_2[0].bitcast(I32)
@@ -57,9 +57,12 @@ def tile_attend_gdistm_t_pl_kernel(tc, hT, rT, G, hoffs, roffs, offs, out_0, out
         def own(shape, dtype, name, tag=None):
             return sb.tile(shape, dtype, name=name, tag=tag or name, align_bytes=64)
 
+        def placed(shape, dtype, name, offset):
+            return reuse.tile(shape, dtype, name=name, offset=offset, align_bytes=64)
+
         h_tab = [own([P, HEADS], F32, "h_tab%d" % n) for n in range(PACK)]
         r_tab = [own([P, RELS], F32, "r_tab%d" % n) for n in range(PACK)]
-        g_raw = own([P, PACK, SLOTS], F32, "g_raw")
+        g_raw = own([P, PACK * SLOTS], F32, "g_raw")
         window = [own([P, TAILS], F32, "window%d" % n) for n in range(PACK)]
 
         nc.sync.dma_start(r_tab[0][:], r_rows[:, LANES[0], :])
@@ -94,25 +97,34 @@ def tile_attend_gdistm_t_pl_kernel(tc, hT, rT, G, hoffs, roffs, offs, out_0, out
             return pairs[:, first : first + count]
 
         c_scales = [own([P, P], U8, "c_scales%d" % n) for n in range(PACK)]
-        c_codes = [own([P, P], U32, "c_codes%d" % n) for n in range(PACK)]
+        c_codes = {n: own([P, P], U32, "c_codes%d" % n) for n in range(PACK)}
         turned = [ps.tile([P, 2, P], F32, name="turned%d" % n, tag="turned%d" % (n % 2)) for n in range(PACK)]
         g_codes = own([P, SLOTS], U32, "g_codes")
         g_scales = own([P, SLOTS], U8, "g_scales")
-        c_rows = [own([P, R], F32, "c_rows%d" % n)[:] for n in range(PACK)]
-        c_pairs = [own([P, R], BF16, "c_pairs%d" % n)[:] for n in range(PACK - 1)] + [in_upper_words(384, R)]
-        c_grouped = {0: g_raw[:, 0, :HALF].bitcast(BF16), 3: in_upper_words(-P, R)}
-        r_got = {0: own([P, R], F32, "r_got0")[:], 2: own([P, R], F32, "r_got2")[:], 3: in_upper_words(640, 2 * R).bitcast(F32)}
-        dt = [own([P, SLOTS], F32, "dt%d" % n)[:] for n in range(PACK)]
+        c_whole = [own([P, R], F32, "c_rows%d" % n)[:] for n in range(PACK - 1)]
+        c_rows = {(n, a): c_whole[n][:, a * R // 2 : (a + 1) * R // 2] for n in range(PACK - 1) for a in range(2)}
+        c_rows.update({(3, 0): in_upper_words(CHUNK, R).bitcast(F32), (3, 1): pairs[:, 2 * SPLIT : 2 * SPLIT + R].bitcast(F32)})
+        c_pairs = [own([P, R], BF16, "c_pairs%d" % n)[:] for n in range(PACK)]
+        c_grouped = {0: g_raw[:, :HALF].bitcast(BF16)}
+        last_grouped = [in_upper_words(0, R // 2), pairs[:, : R // 2]]
+        r_got = {(n, a): own([P, R // 2], F32, "r_got%d_%d" % (n, a))[:] for n in (0, 2, 3) for a in range(2)}
+        dt = {(n, lo): own([P, HALF], F32, "dt%d_%d" % (n, lo))[:] for n in (0, 1, 3) for lo in (0, HALF)}
+
+        def half_list(entries, a):
+            return entries[:, a * R // 32 : (a + 1) * R // 32]
 
         def gather_r(n):
-            nc.vector.tensor_copy(r_got[n], r_tab[n][:].indirect(r_list[:]))
+            for a in range(2):
+                nc.vector.tensor_copy(r_got[n, a], r_tab[n][:].indirect(half_list(r_list, a)))
 
-        def gather_h(n, lo=0, hi=R):
-            nc.vector.tensor_tensor(c_rows[n][:, lo:hi], h_tab[n][:].indirect(h_list[:, lo // 16 : hi // 16]), r_got[n][:, lo:hi], mult)
+        def gather_h(n, a):
+            nc.vector.tensor_tensor(c_rows[n, a], h_tab[n][:].indirect(half_list(h_list, a)), r_got[n, a], mult)
 
-        def c_views(n, lo=0, hi=R):
-            dst = c_pairs[n].rearrange("p (u q e) -> p u q e", u=2, e=2)[:, :, lo // PACK : hi // PACK, :]
-            return dst, c_rows[n][:, lo:hi].rearrange("p (q u e) -> p u q e", u=2, e=2)
+        def c_views(n, a=None):
+            dst = c_pairs[n].rearrange("p (u q e) -> p u q e", u=2, e=2)
+            if a is None:
+                return dst, c_whole[n].rearrange("p (q u e) -> p u q e", u=2, e=2)
+            return dst[:, :, a * P // 2 : (a + 1) * P // 2, :], c_rows[n, a].rearrange("p (q u e) -> p u q e", u=2, e=2)
 
         def pool_round(dst, src):
             nc.gpsimd.tensor_scalar(dst, src, 1.0, -0.0, mult, add)
@@ -121,12 +133,15 @@ def tile_attend_gdistm_t_pl_kernel(tc, hT, rT, G, hoffs, roffs, offs, out_0, out
             for u in range(2):
                 nc.tensor.transpose(turned[n][:, u, :], c_pairs[n][:, u * 2 * P : (u + 1) * 2 * P].bitcast(F32), ident[:])
 
-        def group(n):
-            dst = c_grouped[n].bitcast(F32).rearrange("q (p u) -> q p u", u=2)
-            nc.vector.tensor_copy(dst, turned[n][:].rearrange("q u p -> q p u"))
+        def grouped(n, lo, hi):
+            return last_grouped[2 * lo // P] if n == 3 else c_grouped[n][:, PACK * lo : PACK * hi]
 
-        def quantize_c(n):
-            nc.vector.quantize_mx(out=c_codes[n][:].bitcast(E4M3), scales=c_scales[n][:], in_=c_grouped[n])
+        def group_views(n, lo=0, hi=P):
+            dst = grouped(n, lo, hi).bitcast(F32).rearrange("q (p u) -> q p u", u=2)
+            return dst, turned[n][:, :, lo:hi].rearrange("q u p -> q p u")
+
+        def quantize_c(n, lo=0, hi=P):
+            nc.vector.quantize_mx(out=c_codes[n][:, lo:hi].bitcast(E4M3), scales=c_scales[n][:, lo:hi], in_=grouped(n, lo, hi))
 
         def product(n, lo, hi):
             acc = ps.tile([P, hi - lo], F32, name="acc%d_%d" % (n, lo))
@@ -143,7 +158,7 @@ def tile_attend_gdistm_t_pl_kernel(tc, hT, rT, G, hoffs, roffs, offs, out_0, out
 
         def scatter_on_scalar(n, lo):
             target = window[n][:].indirect(t_list[:, lo // 16 : (lo + HALF) // 16])
-            nc.scalar.activation(target, dt[n][:, lo : lo + HALF], copy)
+            nc.scalar.activation(target, dt[n, lo], copy)
 
         def store(n):
             nc.sync.dma_start(out_rows[:, LANES[n], :], window[n][:])
@@ -152,17 +167,18 @@ def tile_attend_gdistm_t_pl_kernel(tc, hT, rT, G, hoffs, roffs, offs, out_0, out
             return pair_words(lo, hi)[:, LANES[n] // 2, :, LANES[n] % 2], window[n][:, lo:hi]
 
         gather_r(0)
-        gather_h(0, 0, R // 2)
-        nc.scalar.copy(*c_views(0, 0, R // 2))
-        gather_h(0, R // 2, R)
-        nc.vector.tensor_copy(*c_views(0, R // 2, R))
+        gather_h(0, 0)
+        nc.scalar.copy(*c_views(0, 0))
+        gather_h(0, 1)
+        nc.vector.tensor_copy(*c_views(0, 1))
         turn(0)
 
-        g_grouped = [own([P, HALF, PACK], BF16, "g_grouped%d" % a) for a in range(2)]
+        g_grouped = [own([P, HALF, PACK], BF16, "g_grouped0"), placed([P, HALF, PACK], BF16, "g_grouped1", 4096)]
 
-        def g_views(a, lo, hi):
-            dst = g_grouped[a][:, lo:hi, :].rearrange("q (c i) t -> q c t i", i=4)
-            return dst, g_raw[:, :, a * HALF + lo : a * HALF + hi].rearrange("q t (c i) -> q c t i", i=4)
+        def g_views(a):
+            dst = g_grouped[a][:].rearrange("q (c i) t -> q c t i", i=4)
+            rows = g_raw[:].rearrange("q (t c) -> q t c", t=PACK)
+            return dst, rows[:, :, a * HALF : (a + 1) * HALF].rearrange("q t (c i) -> q c t i", i=4)
 
         def quantize_g(a):
             cols = slice(a * HALF, (a + 1) * HALF)
@@ -172,78 +188,83 @@ def tile_attend_gdistm_t_pl_kernel(tc, hT, rT, G, hoffs, roffs, offs, out_0, out
                 in_=g_grouped[a][:].rearrange("q c t -> q (c t)"),
             )
 
-        for a in range(2):
-            nc.scalar.copy(*g_views(a, 0, P))
-        for a in range(2):
-            nc.vector.tensor_copy(*g_views(a, P, HALF))
-        group(0)
+        nc.scalar.copy(*g_views(1))
+        nc.vector.tensor_copy(*g_views(0))
+        nc.vector.tensor_copy(*group_views(0))
         quantize_g(0)
         quantize_c(0)
         quantize_g(1)
         for lo in (0, HALF):
             acc = product(0, lo, lo + HALF)
-            nc.scalar.copy(dt[0][:, lo : lo + HALF], acc[:])
+            nc.scalar.copy(dt[0, lo], acc[:])
         for lo in (0, HALF):
             scatter_on_scalar(0, lo)
         store(0)
         nc.scalar.copy(*lane_views(0, TAILS - EARLY, TAILS))
 
-        r_got[1] = own([P, R], F32, "r_got1", "g_grouped1")[:]
+        for a in range(2):
+            r_got[1, a] = placed([P, R // 2], F32, "r_got1_%d" % a, 4096 + 1024 * a)[:]
         gather_r(1)
         for n in (1, 2):
-            gather_h(n)
-            pool_round(*c_views(n))
+            for a in range(2):
+                gather_h(n, a)
+            for a in range(2):
+                nc.vector.tensor_copy(*c_views(n, a))
             gather_r(n + 1)
             turn(n)
-            if n == 2:
-                gather_h(3)
-            c_grouped[n] = own([P, R], BF16, "c_grouped%d" % n, ("r_tab2", "h_tab3")[n - 1])[:]
-            group(n)
-            if n == 2:
-                nc.vector.tensor_copy(*c_views(3))
-            quantize_c(n)
+            c_grouped[n] = own([P, R], BF16, "c_grouped%d" % n, "r_tab%d" % (n + 1))[:]
+            for lo in (0, P // 2):
+                nc.vector.tensor_copy(*group_views(n, lo, lo + P // 2))
+            for lo in (0, P // 2):
+                quantize_c(n, lo, lo + P // 2)
             acc = product(n, 0, SLOTS)
-            for lo in (0, HALF):
-                nc.scalar.copy(dt[n][:, lo : lo + HALF], acc[:, lo : lo + HALF])
-            for lo in (0, HALF):
-                scatter_on_scalar(n, lo)
-            store(n)
+            if n == 1:
+                for lo in (0, HALF):
+                    nc.scalar.copy(dt[1, lo], acc[:, lo : lo + HALF])
+                for lo in (0, HALF):
+                    scatter_on_scalar(1, lo)
+                store(1)
+        for a in range(2):
+            gather_h(3, a)
+        for a in range(2):
+            nc.vector.tensor_copy(*c_views(3, a))
+        dt[2, 0] = own([P, HALF], F32, "dt2_0", "h_tab3")[:]
+        dt[2, HALF] = c_rows[3, 1]
+        for lo in (0, HALF):
+            nc.vector.tensor_copy(dt[2, lo], acc[:, lo : lo + HALF])
+        for lo in (0, HALF):
+            scatter_on_scalar(2, lo)
+        store(2)
 
-        def early_lane(lo, hi):
-            nc.vector.tensor_copy(*lane_views(0, lo, hi))
-
-        early_lane(640, TAILS - EARLY)
+        nc.vector.tensor_copy(*lane_views(0, CHUNK, TAILS - EARLY))
         turn(3)
-        group(3)
-        early_lane(384, 640)
-        quantize_c(3)
-        early_lane(0, 384)
+        for lo in (0, P // 2):
+            nc.vector.tensor_copy(*group_views(3, lo, lo + P // 2))
+        for lo in (0, P // 2):
+            quantize_c(3, lo, lo + P // 2)
+        nc.vector.tensor_copy(*lane_views(0, 0, CHUNK))
         for lo in (0, HALF):
             acc = product(3, lo, lo + HALF)
-            nc.vector.tensor_copy(dt[3][:, lo : lo + HALF], acc[:])
+            nc.vector.tensor_copy(dt[3, lo], acc[:])
         for lo in (0, HALF):
-            nc.vector.tensor_copy(window[3][:].indirect(t_list[:, lo // 16 : (lo + HALF) // 16]), dt[3][:, lo : lo + HALF])
+            nc.vector.tensor_copy(window[3][:].indirect(t_list[:, lo // 16 : (lo + HALF) // 16]), dt[3, lo])
         store(3)
-        last = TAILS - STAGED
-        pool_round(*lane_views(1, 0, last))
-        staged = lane_views(2, last - STAGED, last)[0]
-        pool_round(staged, window[1][:, last:])
-        nc.scalar.copy(lane_views(1, last, TAILS)[0], staged)
-        nc.scalar.copy(*lane_views(2, SPLIT, TAILS))
-        pool_round(*lane_views(2, 0, SPLIT))
+        for n in (1, 2):
+            pool_round(*lane_views(n, 0, SPLIT))
+            nc.scalar.copy(*lane_views(n, SPLIT, TAILS))
 
-        y_grouped = [own([P, PIECE, PACK], BF16, "y_grouped%d" % i) for i in range(TAILS // PIECE)]
+        edges = (0, 256, 512, 1024, 1536, 1792, 2048)
+        y_grouped = [own([P, edges[i + 1] - edges[i], PACK], BF16, "y_grouped%d" % i) for i in range(6)]
         y_codes = own([P, TAILS], U32, "y_codes")
         y_scales = own([P, CHUNK], U8, "y_scales")
-        order = range(TAILS // PIECE)
-        stores = ((0, 768), (768, 1280), (1280, 1792), (1792, 2048))
+        stores = ((0, 512), (512, 1024), (1024, 1536), (1536, 1792), (1792, 2048))
 
         def weave_views(i):
             dst = y_grouped[i][:].rearrange("p c t -> p (c t)").bitcast(F32).rearrange("p (c u) -> p c u", u=2)
-            return dst, pairs[:].bitcast(F32).rearrange("p (u c) -> p c u", u=2)[:, i * PIECE : (i + 1) * PIECE, :]
+            return dst, pairs[:].bitcast(F32).rearrange("p (u c) -> p c u", u=2)[:, edges[i] : edges[i + 1], :]
 
         def quantize_planes(i):
-            a, b = i * PIECE, (i + 1) * PIECE
+            a, b = edges[i], edges[i + 1]
             k = a // CHUNK
             nc.vector.quantize_mx(
                 out=y_codes[:, a:b].bitcast(E4M3),
@@ -254,17 +275,20 @@ def tile_attend_gdistm_t_pl_kernel(tc, hT, rT, G, hoffs, roffs, offs, out_0, out
                 if last == b:
                     nc.sync.dma_start(out_words[:, first:last], y_codes[:, first:last].bitcast(I32))
 
-        nc.vector.tensor_copy(*lane_views(3, order[0] * PIECE, (order[0] + 1) * PIECE))
-        for i in order[1:]:
-            nc.scalar.copy(*lane_views(3, i * PIECE, (i + 1) * PIECE))
-        nc.vector.tensor_copy(*weave_views(order[0]))
-        for j in range(1, 6):
-            nc.vector.tensor_copy(*weave_views(order[j]))
-            quantize_planes(order[j - 1])
-        for j in (6, 7):
-            nc.scalar.copy(*weave_views(order[j]))
-        for j in (5, 6, 7):
-            quantize_planes(order[j])
+        nc.vector.tensor_copy(*lane_views(3, edges[0], edges[1]))
+        for i in range(1, 6):
+            nc.scalar.copy(*lane_views(3, edges[i], edges[i + 1]))
+        for i in (0, 1):
+            nc.vector.tensor_copy(*weave_views(i))
+        for i in (0, 1):
+            quantize_planes(i)
+        for i in (2, 3):
+            nc.vector.tensor_copy(*weave_views(i))
+        quantize_planes(2)
+        nc.vector.tensor_copy(*weave_views(4))
+        nc.scalar.copy(*weave_views(5))
+        for i in range(3, 6):
+            quantize_planes(i)
         scale_rows = out_scales.rearrange("f (k c) -> k f c", k=chunks)
         for q in range(4):
             queue = nc.sync if q < 2 else nc.scalar

@@ -26,8 +26,9 @@ PIECE = 256
 FLOPS = 2 * D * R * SLOTS
 
 LANES = (2, 0, 1, 3)
-SPLIT = 1280
-EARLY = 1280
+SPLIT = 1152
+EARLY = 512
+IN_WAITS = 1280
 
 
 def tile_attend_gdistm_t_pl_kernel(tc, hT, rT, G, hoffs, roffs, offs, out_0, out_1, out_2):
@@ -101,14 +102,16 @@ def tile_attend_gdistm_t_pl_kernel(tc, hT, rT, G, hoffs, roffs, offs, out_0, out
         turned = [ps.tile([P, 2, P], F32, name="turned%d" % n, tag="turned%d" % (n % 2)) for n in range(PACK)]
         g_codes = own([P, SLOTS], U32, "g_codes")
         g_scales = own([P, SLOTS], U8, "g_scales")
-        c_whole = [own([P, R], F32, "c_rows%d" % n)[:] for n in range(PACK - 1)]
-        c_rows = {(n, a): c_whole[n][:, a * R // 2 : (a + 1) * R // 2] for n in range(PACK - 1) for a in range(2)}
-        c_rows.update({(3, 0): in_upper_words(CHUNK, R).bitcast(F32), (3, 1): pairs[:, 2 * SPLIT : 2 * SPLIT + R].bitcast(F32)})
+        c_rows = {(n, a): own([P, R // 2], F32, "c_rows%d_%d" % (n, a))[:] for n in range(PACK) for a in range(2)}
         c_pairs = [own([P, R], BF16, "c_pairs%d" % n)[:] for n in range(PACK)]
         c_grouped = {0: g_raw[:, :HALF].bitcast(BF16)}
         last_grouped = [in_upper_words(0, R // 2), pairs[:, : R // 2]]
-        r_got = {(n, a): own([P, R // 2], F32, "r_got%d_%d" % (n, a))[:] for n in (0, 2, 3) for a in range(2)}
-        dt = {(n, lo): own([P, HALF], F32, "dt%d_%d" % (n, lo))[:] for n in (0, 1, 3) for lo in (0, HALF)}
+        r_got = {(n, a): own([P, R // 2], F32, "r_got%d_%d" % (n, a))[:] for n, a in ((0, 0), (0, 1), (2, 0), (2, 1), (3, 0))}
+        r_got[3, 1] = in_upper_words(CHUNK, R).bitcast(F32)
+        dt = {(n, lo): own([P, HALF], F32, "dt%d_%d" % (n, lo))[:] for n in (0, 1) for lo in (0, HALF)}
+        late = TAILS - PIECE
+        dt.update({(2, 0): in_upper_words(IN_WAITS, R).bitcast(F32), (2, HALF): pairs[:, 2 * SPLIT : 2 * SPLIT + R].bitcast(F32)})
+        dt.update({(3, 0): own([P, HALF], F32, "dt3_0")[:], (3, HALF): pairs[:, 2 * late : 2 * TAILS].bitcast(F32)})
 
         def half_list(entries, a):
             return entries[:, a * R // 32 : (a + 1) * R // 32]
@@ -120,10 +123,8 @@ def tile_attend_gdistm_t_pl_kernel(tc, hT, rT, G, hoffs, roffs, offs, out_0, out
         def gather_h(n, a):
             nc.vector.tensor_tensor(c_rows[n, a], h_tab[n][:].indirect(half_list(h_list, a)), r_got[n, a], mult)
 
-        def c_views(n, a=None):
+        def c_views(n, a):
             dst = c_pairs[n].rearrange("p (u q e) -> p u q e", u=2, e=2)
-            if a is None:
-                return dst, c_whole[n].rearrange("p (q u e) -> p u q e", u=2, e=2)
             return dst[:, :, a * P // 2 : (a + 1) * P // 2, :], c_rows[n, a].rearrange("p (q u e) -> p u q e", u=2, e=2)
 
         def pool_round(dst, src):
@@ -144,7 +145,7 @@ def tile_attend_gdistm_t_pl_kernel(tc, hT, rT, G, hoffs, roffs, offs, out_0, out
             nc.vector.quantize_mx(out=c_codes[n][:, lo:hi].bitcast(E4M3), scales=c_scales[n][:, lo:hi], in_=grouped(n, lo, hi))
 
         def product(n, lo, hi):
-            acc = ps.tile([P, hi - lo], F32, name="acc%d_%d" % (n, lo))
+            acc = ps.tile([P, hi - lo], F32, name="acc%d_%d" % (n, lo), tag="acc%d_%d" % (n % 2, lo))
             nc.tensor.matmul_mx(
                 out=acc[:],
                 lhsT=c_codes[n][:].bitcast(E4M3),
@@ -217,26 +218,18 @@ def tile_attend_gdistm_t_pl_kernel(tc, hT, rT, G, hoffs, roffs, offs, out_0, out
                 nc.vector.tensor_copy(*group_views(n, lo, lo + P // 2))
             for lo in (0, P // 2):
                 quantize_c(n, lo, lo + P // 2)
-            acc = product(n, 0, SLOTS)
-            if n == 1:
-                for lo in (0, HALF):
-                    nc.scalar.copy(dt[1, lo], acc[:, lo : lo + HALF])
-                for lo in (0, HALF):
-                    scatter_on_scalar(1, lo)
-                store(1)
+            acc = {lo: product(n, lo, lo + HALF) for lo in (0, HALF)}
+            for lo in (0, HALF):
+                nc.scalar.copy(dt[n, lo], acc[lo][:])
+            for lo in (0, HALF):
+                scatter_on_scalar(n, lo)
+            store(n)
         for a in range(2):
             gather_h(3, a)
         for a in range(2):
             nc.vector.tensor_copy(*c_views(3, a))
-        dt[2, 0] = own([P, HALF], F32, "dt2_0", "h_tab3")[:]
-        dt[2, HALF] = c_rows[3, 1]
-        for lo in (0, HALF):
-            nc.vector.tensor_copy(dt[2, lo], acc[:, lo : lo + HALF])
-        for lo in (0, HALF):
-            scatter_on_scalar(2, lo)
-        store(2)
 
-        nc.vector.tensor_copy(*lane_views(0, CHUNK, TAILS - EARLY))
+        nc.vector.tensor_copy(*lane_views(0, CHUNK, IN_WAITS))
         turn(3)
         for lo in (0, P // 2):
             nc.vector.tensor_copy(*group_views(3, lo, lo + P // 2))
@@ -249,9 +242,10 @@ def tile_attend_gdistm_t_pl_kernel(tc, hT, rT, G, hoffs, roffs, offs, out_0, out
         for lo in (0, HALF):
             nc.vector.tensor_copy(window[3][:].indirect(t_list[:, lo // 16 : (lo + HALF) // 16]), dt[3, lo])
         store(3)
+        nc.scalar.copy(*lane_views(0, IN_WAITS, TAILS - EARLY))
         for n in (1, 2):
             pool_round(*lane_views(n, 0, SPLIT))
-            nc.scalar.copy(*lane_views(n, SPLIT, TAILS))
+            nc.scalar.copy(*lane_views(n, SPLIT, late))
 
         edges = (0, 256, 512, 1024, 1536, 1792, 2048)
         y_grouped = [own([P, edges[i + 1] - edges[i], PACK], BF16, "y_grouped%d" % i) for i in range(6)]
@@ -276,8 +270,10 @@ def tile_attend_gdistm_t_pl_kernel(tc, hT, rT, G, hoffs, roffs, offs, out_0, out
                     nc.sync.dma_start(out_words[:, first:last], y_codes[:, first:last].bitcast(I32))
 
         nc.vector.tensor_copy(*lane_views(3, edges[0], edges[1]))
-        for i in range(1, 6):
+        for i in range(1, 5):
             nc.scalar.copy(*lane_views(3, edges[i], edges[i + 1]))
+        for n in (1, 2, 3):
+            nc.scalar.copy(*lane_views(n, late, TAILS))
         for i in (0, 1):
             nc.vector.tensor_copy(*weave_views(i))
         for i in (0, 1):
@@ -286,8 +282,9 @@ def tile_attend_gdistm_t_pl_kernel(tc, hT, rT, G, hoffs, roffs, offs, out_0, out
             nc.vector.tensor_copy(*weave_views(i))
         quantize_planes(2)
         nc.vector.tensor_copy(*weave_views(4))
-        nc.scalar.copy(*weave_views(5))
-        for i in range(3, 6):
+        quantize_planes(3)
+        nc.vector.tensor_copy(*weave_views(5))
+        for i in (4, 5):
             quantize_planes(i)
         scale_rows = out_scales.rearrange("f (k c) -> k f c", k=chunks)
         for q in range(4):

@@ -26,9 +26,9 @@ PIECE = 256
 FLOPS = 2 * D * R * SLOTS
 
 LANES = (2, 0, 1, 3)
-SPLIT = 1152
+SPLIT = 1280
 EARLY = 512
-IN_WAITS = 1280
+IN_WAITS = 1024
 
 
 def tile_attend_gdistm_t_pl_kernel(tc, hT, rT, G, hoffs, roffs, offs, out_0, out_1, out_2):
@@ -102,30 +102,31 @@ def tile_attend_gdistm_t_pl_kernel(tc, hT, rT, G, hoffs, roffs, offs, out_0, out
         turned = [ps.tile([P, 2, P], F32, name="turned%d" % n, tag="turned%d" % (n % 2)) for n in range(PACK)]
         g_codes = own([P, SLOTS], U32, "g_codes")
         g_scales = own([P, SLOTS], U8, "g_scales")
-        c_rows = {(n, a): own([P, R // 2], F32, "c_rows%d_%d" % (n, a))[:] for n in range(PACK) for a in range(2)}
+        c_rows = [own([P, R], F32, "c_rows%d" % n)[:] for n in range(PACK)]
         c_pairs = [own([P, R], BF16, "c_pairs%d" % n)[:] for n in range(PACK)]
         c_grouped = {0: g_raw[:, :HALF].bitcast(BF16)}
         last_grouped = [in_upper_words(0, R // 2), pairs[:, : R // 2]]
-        r_got = {(n, a): own([P, R // 2], F32, "r_got%d_%d" % (n, a))[:] for n, a in ((0, 0), (0, 1), (2, 0), (2, 1), (3, 0))}
-        r_got[3, 1] = in_upper_words(CHUNK, R).bitcast(F32)
+        r_got = {n: own([P, R], F32, "r_got%d" % n)[:] for n in (0, 2)}
+        r_got[3] = in_upper_words(CHUNK, 2 * R).bitcast(F32)
         dt = {(n, lo): own([P, HALF], F32, "dt%d_%d" % (n, lo))[:] for n in (0, 1) for lo in (0, HALF)}
         late = TAILS - PIECE
         dt.update({(2, 0): in_upper_words(IN_WAITS, R).bitcast(F32), (2, HALF): pairs[:, 2 * SPLIT : 2 * SPLIT + R].bitcast(F32)})
         dt.update({(3, 0): own([P, HALF], F32, "dt3_0")[:], (3, HALF): pairs[:, 2 * late : 2 * TAILS].bitcast(F32)})
 
-        def half_list(entries, a):
-            return entries[:, a * R // 32 : (a + 1) * R // 32]
-
         def gather_r(n):
-            for a in range(2):
-                nc.vector.tensor_copy(r_got[n, a], r_tab[n][:].indirect(half_list(r_list, a)))
+            nc.vector.tensor_copy(r_got[n], r_tab[n][:].indirect(r_list[:]))
 
-        def gather_h(n, a):
-            nc.vector.tensor_tensor(c_rows[n, a], h_tab[n][:].indirect(half_list(h_list, a)), r_got[n, a], mult)
+        def gather_h(n, lo=0, hi=R):
+            nc.vector.tensor_tensor(c_rows[n][:, lo:hi], h_tab[n][:].indirect(h_list[:, lo // 16 : hi // 16]), r_got[n][:, lo:hi], mult)
 
-        def c_views(n, a):
-            dst = c_pairs[n].rearrange("p (u q e) -> p u q e", u=2, e=2)
-            return dst[:, :, a * P // 2 : (a + 1) * P // 2, :], c_rows[n, a].rearrange("p (q u e) -> p u q e", u=2, e=2)
+        def c_views(n, lo=0, hi=R):
+            dst = c_pairs[n].rearrange("p (u q e) -> p u q e", u=2, e=2)[:, :, lo // PACK : hi // PACK, :]
+            return dst, c_rows[n][:, lo:hi].rearrange("p (q u e) -> p u q e", u=2, e=2)
+
+        def round_c(n):
+            dst, src = c_views(n)
+            for u in range(2):
+                nc.vector.tensor_copy(dst[:, u], src[:, u])
 
         def pool_round(dst, src):
             nc.gpsimd.tensor_scalar(dst, src, 1.0, -0.0, mult, add)
@@ -168,10 +169,10 @@ def tile_attend_gdistm_t_pl_kernel(tc, hT, rT, G, hoffs, roffs, offs, out_0, out
             return pair_words(lo, hi)[:, LANES[n] // 2, :, LANES[n] % 2], window[n][:, lo:hi]
 
         gather_r(0)
-        gather_h(0, 0)
-        nc.scalar.copy(*c_views(0, 0))
-        gather_h(0, 1)
-        nc.vector.tensor_copy(*c_views(0, 1))
+        gather_h(0, 0, R // 2)
+        nc.scalar.copy(*c_views(0, 0, R // 2))
+        gather_h(0, R // 2, R)
+        nc.vector.tensor_copy(*c_views(0, R // 2, R))
         turn(0)
 
         g_grouped = [own([P, HALF, PACK], BF16, "g_grouped0"), placed([P, HALF, PACK], BF16, "g_grouped1", 4096)]
@@ -203,14 +204,11 @@ def tile_attend_gdistm_t_pl_kernel(tc, hT, rT, G, hoffs, roffs, offs, out_0, out
         store(0)
         nc.scalar.copy(*lane_views(0, TAILS - EARLY, TAILS))
 
-        for a in range(2):
-            r_got[1, a] = placed([P, R // 2], F32, "r_got1_%d" % a, 4096 + 1024 * a)[:]
+        r_got[1] = placed([P, R], F32, "r_got1", 4096)[:]
         gather_r(1)
         for n in (1, 2):
-            for a in range(2):
-                gather_h(n, a)
-            for a in range(2):
-                nc.vector.tensor_copy(*c_views(n, a))
+            gather_h(n)
+            round_c(n)
             gather_r(n + 1)
             turn(n)
             c_grouped[n] = own([P, R], BF16, "c_grouped%d" % n, "r_tab%d" % (n + 1))[:]
@@ -224,10 +222,8 @@ def tile_attend_gdistm_t_pl_kernel(tc, hT, rT, G, hoffs, roffs, offs, out_0, out
             for lo in (0, HALF):
                 scatter_on_scalar(n, lo)
             store(n)
-        for a in range(2):
-            gather_h(3, a)
-        for a in range(2):
-            nc.vector.tensor_copy(*c_views(3, a))
+        gather_h(3)
+        round_c(3)
 
         nc.vector.tensor_copy(*lane_views(0, CHUNK, IN_WAITS))
         turn(3)

@@ -26,9 +26,8 @@ PIECE = 256
 FLOPS = 2 * D * R * SLOTS
 
 LANES = (2, 0, 1, 3)
-SPLIT = 1280
-EARLY = 512
-IN_WAITS = 1024
+SPLIT = 864
+EARLY = 1024
 
 
 def tile_attend_gdistm_t_pl_kernel(tc, hT, rT, G, hoffs, roffs, offs, out_0, out_1, out_2):
@@ -105,12 +104,11 @@ def tile_attend_gdistm_t_pl_kernel(tc, hT, rT, G, hoffs, roffs, offs, out_0, out
         c_rows = [own([P, R], F32, "c_rows%d" % n)[:] for n in range(PACK)]
         c_pairs = [own([P, R], BF16, "c_pairs%d" % n)[:] for n in range(PACK)]
         c_grouped = {0: g_raw[:, :HALF].bitcast(BF16)}
-        last_grouped = [in_upper_words(0, R // 2), pairs[:, : R // 2]]
+        last_grouped = [in_upper_words(0, R // 2), pairs[:, 2 * SPLIT - P : 2 * SPLIT + P]]
         r_got = {n: own([P, R], F32, "r_got%d" % n)[:] for n in (0, 2)}
         r_got[3] = in_upper_words(CHUNK, 2 * R).bitcast(F32)
-        dt = {(n, lo): own([P, HALF], F32, "dt%d_%d" % (n, lo))[:] for n in (0, 1) for lo in (0, HALF)}
+        dt = {(n, lo): own([P, HALF], F32, "dt%d_%d" % (n, lo))[:] for n in range(PACK - 1) for lo in (0, HALF)}
         late = TAILS - PIECE
-        dt.update({(2, 0): in_upper_words(IN_WAITS, R).bitcast(F32), (2, HALF): pairs[:, 2 * SPLIT : 2 * SPLIT + R].bitcast(F32)})
         dt.update({(3, 0): own([P, HALF], F32, "dt3_0")[:], (3, HALF): pairs[:, 2 * late : 2 * TAILS].bitcast(F32)})
 
         def gather_r(n):
@@ -205,27 +203,39 @@ def tile_attend_gdistm_t_pl_kernel(tc, hT, rT, G, hoffs, roffs, offs, out_0, out
         nc.scalar.copy(*lane_views(0, TAILS - EARLY, TAILS))
 
         r_got[1] = placed([P, R], F32, "r_got1", 4096)[:]
-        gather_r(1)
-        for n in (1, 2):
-            gather_h(n)
-            round_c(n)
-            gather_r(n + 1)
-            turn(n)
-            c_grouped[n] = own([P, R], BF16, "c_grouped%d" % n, "r_tab%d" % (n + 1))[:]
-            for lo in (0, P // 2):
-                nc.vector.tensor_copy(*group_views(n, lo, lo + P // 2))
-            for lo in (0, P // 2):
-                quantize_c(n, lo, lo + P // 2)
+        def fetch_and_scatter(n):
             acc = {lo: product(n, lo, lo + HALF) for lo in (0, HALF)}
             for lo in (0, HALF):
                 nc.scalar.copy(dt[n, lo], acc[lo][:])
             for lo in (0, HALF):
                 scatter_on_scalar(n, lo)
             store(n)
-        gather_h(3)
-        round_c(3)
 
-        nc.vector.tensor_copy(*lane_views(0, CHUNK, IN_WAITS))
+        gather_r(1)
+        gather_h(1)
+        round_c(1)
+        gather_r(2)
+        turn(1)
+        c_grouped[1] = own([P, R], BF16, "c_grouped1", "r_tab2")[:]
+        for lo in (0, P // 2):
+            nc.vector.tensor_copy(*group_views(1, lo, lo + P // 2))
+        for lo in (0, P // 2):
+            quantize_c(1, lo, lo + P // 2)
+        fetch_and_scatter(1)
+
+        gather_h(2)
+        round_c(2)
+        gather_r(3)
+        turn(2)
+        for lo in (0, R // 2):
+            gather_h(3, lo, lo + R // 2)
+        c_grouped[2] = in_upper_words(CHUNK, R)
+        nc.vector.tensor_copy(*group_views(2))
+        round_c(3)
+        quantize_c(2)
+        fetch_and_scatter(2)
+
+        nc.vector.tensor_copy(*lane_views(0, CHUNK, TAILS - EARLY))
         turn(3)
         for lo in (0, P // 2):
             nc.vector.tensor_copy(*group_views(3, lo, lo + P // 2))
@@ -238,10 +248,15 @@ def tile_attend_gdistm_t_pl_kernel(tc, hT, rT, G, hoffs, roffs, offs, out_0, out
         for lo in (0, HALF):
             nc.vector.tensor_copy(window[3][:].indirect(t_list[:, lo // 16 : (lo + HALF) // 16]), dt[3, lo])
         store(3)
-        nc.scalar.copy(*lane_views(0, IN_WAITS, TAILS - EARLY))
-        for n in (1, 2):
-            pool_round(*lane_views(n, 0, SPLIT))
-            nc.scalar.copy(*lane_views(n, SPLIT, late))
+        passed = late - 48
+        staged = pair_words(SPLIT, SPLIT + 3 * 384)[:, :, :, 1].rearrange("p u (j m) -> p u j m", j=3)[:, :, :, :8]
+        dst, src = (view.rearrange("p (u j m) -> p u j m", u=2, j=3) for view in lane_views(1, passed, late))
+        pool_round(*lane_views(1, SPLIT, passed))
+        pool_round(staged, src)
+        pool_round(*lane_views(1, 0, SPLIT))
+        nc.scalar.copy(dst, staged)
+        nc.scalar.copy(*lane_views(2, SPLIT, late))
+        pool_round(*lane_views(2, 0, SPLIT))
 
         edges = (0, 256, 512, 1024, 1536, 1792, 2048)
         y_grouped = [own([P, edges[i + 1] - edges[i], PACK], BF16, "y_grouped%d" % i) for i in range(6)]
@@ -265,8 +280,9 @@ def tile_attend_gdistm_t_pl_kernel(tc, hT, rT, G, hoffs, roffs, offs, out_0, out
                 if last == b:
                     nc.sync.dma_start(out_words[:, first:last], y_codes[:, first:last].bitcast(I32))
 
-        nc.vector.tensor_copy(*lane_views(3, edges[0], edges[1]))
-        for i in range(1, 5):
+        for i in (0, 1):
+            nc.vector.tensor_copy(*lane_views(3, edges[i], edges[i + 1]))
+        for i in range(2, 5):
             nc.scalar.copy(*lane_views(3, edges[i], edges[i + 1]))
         for n in (1, 2, 3):
             nc.scalar.copy(*lane_views(n, late, TAILS))
@@ -279,7 +295,7 @@ def tile_attend_gdistm_t_pl_kernel(tc, hT, rT, G, hoffs, roffs, offs, out_0, out
         quantize_planes(2)
         nc.vector.tensor_copy(*weave_views(4))
         quantize_planes(3)
-        nc.vector.tensor_copy(*weave_views(5))
+        nc.scalar.copy(*weave_views(5))
         for i in (4, 5):
             quantize_planes(i)
         scale_rows = out_scales.rearrange("f (k c) -> k f c", k=chunks)

@@ -25,9 +25,8 @@ CHUNK = 512
 PIECE = 256
 FLOPS = 2 * D * R * SLOTS
 
-LANES = (2, 0, 1, 3)
-SPLIT = 864
-EARLY = 1024
+LANES = (0, 1, 2, 3)
+FIRST_LANE = (0, 384, 1024, 1792, 2048)
 
 
 def tile_attend_gdistm_t_pl_kernel(tc, hT, rT, G, hoffs, roffs, offs, out_0, out_1, out_2):
@@ -92,8 +91,8 @@ def tile_attend_gdistm_t_pl_kernel(tc, hT, rT, G, hoffs, roffs, offs, out_0, out
         def pair_words(lo, hi):
             return pairs[:].rearrange("p (u c e) -> p u c e", u=2, e=2)[:, :, lo:hi, :]
 
-        def in_upper_words(col, count):
-            first = 2 * TAILS + 2 * col
+        def in_words(u, col, count):
+            first = 2 * (u * TAILS + col)
             return pairs[:, first : first + count]
 
         c_scales = [own([P, P], U8, "c_scales%d" % n) for n in range(PACK)]
@@ -101,15 +100,14 @@ def tile_attend_gdistm_t_pl_kernel(tc, hT, rT, G, hoffs, roffs, offs, out_0, out
         turned = [ps.tile([P, 2, P], F32, name="turned%d" % n, tag="turned%d" % (n % 2)) for n in range(PACK)]
         g_codes = own([P, SLOTS], U32, "g_codes")
         g_scales = own([P, SLOTS], U8, "g_scales")
-        c_rows = [own([P, R], F32, "c_rows%d" % n)[:] for n in range(PACK)]
+        c_rows = [own([P, R], F32, "c_rows%d" % n)[:] if n != 2 else in_words(0, 0, 2 * R).bitcast(F32) for n in range(PACK)]
         c_pairs = [own([P, R], BF16, "c_pairs%d" % n)[:] for n in range(PACK)]
         c_grouped = {0: g_raw[:, :HALF].bitcast(BF16)}
-        last_grouped = [in_upper_words(0, R // 2), pairs[:, 2 * SPLIT - P : 2 * SPLIT + P]]
+        last_grouped = [own([P, R // 2], BF16, "last_grouped")[:], in_words(0, FIRST_LANE[2], R // 2)]
         r_got = {n: own([P, R], F32, "r_got%d" % n)[:] for n in (0, 2)}
-        r_got[3] = in_upper_words(CHUNK, 2 * R).bitcast(F32)
+        r_got[3] = in_words(0, CHUNK, 2 * R).bitcast(F32)
         dt = {(n, lo): own([P, HALF], F32, "dt%d_%d" % (n, lo))[:] for n in range(PACK - 1) for lo in (0, HALF)}
-        late = TAILS - PIECE
-        dt.update({(3, 0): own([P, HALF], F32, "dt3_0")[:], (3, HALF): pairs[:, 2 * late : 2 * TAILS].bitcast(F32)})
+        dt.update({(3, 0): in_words(1, 0, R).bitcast(F32), (3, HALF): in_words(1, 3 * CHUNK - P, R).bitcast(F32)})
 
         def gather_r(n):
             nc.vector.tensor_copy(r_got[n], r_tab[n][:].indirect(r_list[:]))
@@ -200,7 +198,7 @@ def tile_attend_gdistm_t_pl_kernel(tc, hT, rT, G, hoffs, roffs, offs, out_0, out
         for lo in (0, HALF):
             scatter_on_scalar(0, lo)
         store(0)
-        nc.scalar.copy(*lane_views(0, TAILS - EARLY, TAILS))
+        nc.scalar.copy(*lane_views(0, *FIRST_LANE[3:5]))
 
         r_got[1] = placed([P, R], F32, "r_got1", 4096)[:]
         def fetch_and_scatter(n):
@@ -225,38 +223,31 @@ def tile_attend_gdistm_t_pl_kernel(tc, hT, rT, G, hoffs, roffs, offs, out_0, out
 
         gather_h(2)
         round_c(2)
+        pool_round(*lane_views(0, *FIRST_LANE[0:2]))
         gather_r(3)
         turn(2)
         for lo in (0, R // 2):
             gather_h(3, lo, lo + R // 2)
-        c_grouped[2] = in_upper_words(CHUNK, R)
+        c_grouped[2] = in_words(0, CHUNK, R)
         nc.vector.tensor_copy(*group_views(2))
         round_c(3)
         quantize_c(2)
         fetch_and_scatter(2)
 
-        nc.vector.tensor_copy(*lane_views(0, CHUNK, TAILS - EARLY))
+        nc.vector.tensor_copy(*lane_views(0, *FIRST_LANE[1:3]))
         turn(3)
         for lo in (0, P // 2):
             nc.vector.tensor_copy(*group_views(3, lo, lo + P // 2))
         for lo in (0, P // 2):
             quantize_c(3, lo, lo + P // 2)
-        nc.vector.tensor_copy(*lane_views(0, 0, CHUNK))
+        pool_round(*lane_views(0, *FIRST_LANE[2:4]))
+        pool_round(*lane_views(1, 0, TAILS))
         for lo in (0, HALF):
             acc = product(3, lo, lo + HALF)
             nc.vector.tensor_copy(dt[3, lo], acc[:])
         for lo in (0, HALF):
             nc.vector.tensor_copy(window[3][:].indirect(t_list[:, lo // 16 : (lo + HALF) // 16]), dt[3, lo])
         store(3)
-        passed = late - 48
-        staged = pair_words(SPLIT, SPLIT + 3 * 384)[:, :, :, 1].rearrange("p u (j m) -> p u j m", j=3)[:, :, :, :8]
-        dst, src = (view.rearrange("p (u j m) -> p u j m", u=2, j=3) for view in lane_views(1, passed, late))
-        pool_round(*lane_views(1, SPLIT, passed))
-        pool_round(staged, src)
-        pool_round(*lane_views(1, 0, SPLIT))
-        nc.scalar.copy(dst, staged)
-        nc.scalar.copy(*lane_views(2, SPLIT, late))
-        pool_round(*lane_views(2, 0, SPLIT))
 
         edges = (0, 256, 512, 1024, 1536, 1792, 2048)
         y_grouped = [own([P, edges[i + 1] - edges[i], PACK], BF16, "y_grouped%d" % i) for i in range(6)]
@@ -280,22 +271,25 @@ def tile_attend_gdistm_t_pl_kernel(tc, hT, rT, G, hoffs, roffs, offs, out_0, out
                 if last == b:
                     nc.sync.dma_start(out_words[:, first:last], y_codes[:, first:last].bitcast(I32))
 
+        nc.vector.tensor_copy(*lane_views(2, 0, CHUNK))
         for i in (0, 1):
             nc.vector.tensor_copy(*lane_views(3, edges[i], edges[i + 1]))
-        for i in range(2, 5):
+        for i in (2, 3):
+            for n in (2, 3):
+                nc.scalar.copy(*lane_views(n, edges[i], edges[i + 1]))
+        nc.scalar.copy(*lane_views(2, edges[4], edges[6]))
+        for i in (4, 5):
             nc.scalar.copy(*lane_views(3, edges[i], edges[i + 1]))
-        for n in (1, 2, 3):
-            nc.scalar.copy(*lane_views(n, late, TAILS))
         for i in (0, 1):
             nc.vector.tensor_copy(*weave_views(i))
         for i in (0, 1):
             quantize_planes(i)
-        for i in (2, 3):
-            nc.vector.tensor_copy(*weave_views(i))
+        nc.vector.tensor_copy(*weave_views(2))
         quantize_planes(2)
-        nc.vector.tensor_copy(*weave_views(4))
+        nc.vector.tensor_copy(*weave_views(3))
         quantize_planes(3)
-        nc.scalar.copy(*weave_views(5))
+        for i in (4, 5):
+            nc.vector.tensor_copy(*weave_views(i))
         for i in (4, 5):
             quantize_planes(i)
         scale_rows = out_scales.rearrange("f (k c) -> k f c", k=chunks)

@@ -26,7 +26,8 @@ PIECE = 256
 FLOPS = 2 * D * R * SLOTS
 
 LANES = (0, 1, 2, 3)
-FIRST_LANE = (0, 384, 1024, 1792, 2048)
+FIRST_LANE = (0, 512, 1152, 1408, 2016)
+THIRD_LANE = 1280
 
 
 def tile_attend_gdistm_t_pl_kernel(tc, hT, rT, G, hoffs, roffs, offs, out_0, out_1, out_2):
@@ -106,8 +107,9 @@ def tile_attend_gdistm_t_pl_kernel(tc, hT, rT, G, hoffs, roffs, offs, out_0, out
         last_grouped = [own([P, R // 2], BF16, "last_grouped")[:], in_words(0, FIRST_LANE[2], R // 2)]
         r_got = {n: own([P, R], F32, "r_got%d" % n)[:] for n in (0, 2)}
         r_got[3] = in_words(0, CHUNK, 2 * R).bitcast(F32)
-        dt = {(n, lo): own([P, HALF], F32, "dt%d_%d" % (n, lo))[:] for n in range(PACK - 1) for lo in (0, HALF)}
-        dt.update({(3, 0): in_words(1, 0, R).bitcast(F32), (3, HALF): in_words(1, 3 * CHUNK - P, R).bitcast(F32)})
+        dt = {(n, lo): own([P, HALF], F32, "dt%d_%d" % (n, lo))[:] for n, lo in ((0, 0), (0, HALF), (1, 0), (1, HALF), (3, 0))}
+        dt.update({(2, HALF): in_words(0, FIRST_LANE[4], R).bitcast(F32), (3, HALF): in_words(1, 3 * CHUNK - P, R).bitcast(F32)})
+        staged = pair_words(CHUNK, 3 * CHUNK)[:, 1, :, 1].rearrange("p (j m) -> p j m", j=2)[:, :, : TAILS - FIRST_LANE[4]]
 
         def gather_r(n):
             nc.vector.tensor_copy(r_got[n], r_tab[n][:].indirect(r_list[:]))
@@ -220,6 +222,9 @@ def tile_attend_gdistm_t_pl_kernel(tc, hT, rT, G, hoffs, roffs, offs, out_0, out
         for lo in (0, P // 2):
             quantize_c(1, lo, lo + P // 2)
         fetch_and_scatter(1)
+        nc.scalar.copy(*lane_views(1, *FIRST_LANE[3:5]))
+        for n in (0, 1):
+            nc.scalar.copy(staged[:, n, :], window[n][:, FIRST_LANE[4] :])
 
         gather_h(2)
         round_c(2)
@@ -232,22 +237,25 @@ def tile_attend_gdistm_t_pl_kernel(tc, hT, rT, G, hoffs, roffs, offs, out_0, out
         nc.vector.tensor_copy(*group_views(2))
         round_c(3)
         quantize_c(2)
-        fetch_and_scatter(2)
 
         nc.vector.tensor_copy(*lane_views(0, *FIRST_LANE[1:3]))
         turn(3)
+        acc = {lo: product(2, lo, lo + HALF) for lo in (0, HALF)}
         for lo in (0, P // 2):
             nc.vector.tensor_copy(*group_views(3, lo, lo + P // 2))
         for lo in (0, P // 2):
             quantize_c(3, lo, lo + P // 2)
         pool_round(*lane_views(0, *FIRST_LANE[2:4]))
-        pool_round(*lane_views(1, 0, TAILS))
+        pool_round(*lane_views(1, 0, FIRST_LANE[3]))
+        dt[2, 0] = own([P, HALF], F32, "dt2_0", "last_grouped")[:]
+        nc.vector.tensor_copy(dt[2, 0], acc[0][:])
+        nc.scalar.copy(dt[2, HALF], acc[HALF][:])
         for lo in (0, HALF):
-            acc = product(3, lo, lo + HALF)
-            nc.vector.tensor_copy(dt[3, lo], acc[:])
-        for lo in (0, HALF):
-            nc.vector.tensor_copy(window[3][:].indirect(t_list[:, lo // 16 : (lo + HALF) // 16]), dt[3, lo])
-        store(3)
+            nc.vector.tensor_copy(window[2][:].indirect(t_list[:, lo // 16 : (lo + HALF) // 16]), dt[2, lo])
+        store(2)
+        fetch_and_scatter(3)
+        nc.vector.tensor_copy(*lane_views(2, 0, THIRD_LANE))
+        nc.vector.tensor_copy(pair_words(FIRST_LANE[4], TAILS)[:, 0].rearrange("p c e -> p e c"), staged)
 
         edges = (0, 256, 512, 1024, 1536, 1792, 2048)
         y_grouped = [own([P, edges[i + 1] - edges[i], PACK], BF16, "y_grouped%d" % i) for i in range(6)]
@@ -271,12 +279,11 @@ def tile_attend_gdistm_t_pl_kernel(tc, hT, rT, G, hoffs, roffs, offs, out_0, out
                 if last == b:
                     nc.sync.dma_start(out_words[:, first:last], y_codes[:, first:last].bitcast(I32))
 
-        nc.vector.tensor_copy(*lane_views(2, 0, CHUNK))
         for i in (0, 1):
             nc.vector.tensor_copy(*lane_views(3, edges[i], edges[i + 1]))
-        for i in (2, 3):
-            for n in (2, 3):
-                nc.scalar.copy(*lane_views(n, edges[i], edges[i + 1]))
+        nc.scalar.copy(*lane_views(3, edges[2], edges[3]))
+        nc.scalar.copy(*lane_views(2, THIRD_LANE, edges[4]))
+        nc.scalar.copy(*lane_views(3, edges[3], edges[4]))
         nc.scalar.copy(*lane_views(2, edges[4], edges[6]))
         for i in (4, 5):
             nc.scalar.copy(*lane_views(3, edges[i], edges[i + 1]))
@@ -284,10 +291,10 @@ def tile_attend_gdistm_t_pl_kernel(tc, hT, rT, G, hoffs, roffs, offs, out_0, out
             nc.vector.tensor_copy(*weave_views(i))
         for i in (0, 1):
             quantize_planes(i)
-        nc.vector.tensor_copy(*weave_views(2))
-        quantize_planes(2)
-        nc.vector.tensor_copy(*weave_views(3))
-        quantize_planes(3)
+        for i in (2, 3):
+            nc.vector.tensor_copy(*weave_views(i))
+        for i in (2, 3):
+            quantize_planes(i)
         for i in (4, 5):
             nc.vector.tensor_copy(*weave_views(i))
         for i in (4, 5):

@@ -26,7 +26,7 @@ PIECE = 256
 FLOPS = 2 * D * R * SLOTS
 
 LANES = (0, 1, 2, 3)
-FIRST_LANE = (0, 512, 1152, 1408, 2016)
+FIRST_LANE = (0, 512, 1152, 1280, 2016)
 THIRD_LANE = 1280
 
 
@@ -40,7 +40,6 @@ def tile_attend_gdistm_t_pl_kernel(tc, hT, rT, G, hoffs, roffs, offs, out_0, out
     with ExitStack() as ctx:
         lists = ctx.enter_context(tc.tile_pool(name="lists", bufs=1))
         sb = ctx.enter_context(tc.tile_pool(name="sb", bufs=1))
-        reuse = ctx.enter_context(tc.tile_pool(name="reuse", bufs=1))
         ps = ctx.enter_context(tc.psum_pool(name="ps", bufs=1))
 
         h_list = lists.tile([P, R // 16], U16, name="h_list")
@@ -56,9 +55,6 @@ def tile_attend_gdistm_t_pl_kernel(tc, hT, rT, G, hoffs, roffs, offs, out_0, out
 
         def own(shape, dtype, name, tag=None):
             return sb.tile(shape, dtype, name=name, tag=tag or name, align_bytes=64)
-
-        def placed(shape, dtype, name, offset):
-            return reuse.tile(shape, dtype, name=name, offset=offset, align_bytes=64)
 
         h_tab = [own([P, HEADS], F32, "h_tab%d" % n) for n in range(PACK)]
         r_tab = [own([P, RELS], F32, "r_tab%d" % n) for n in range(PACK)]
@@ -105,9 +101,9 @@ def tile_attend_gdistm_t_pl_kernel(tc, hT, rT, G, hoffs, roffs, offs, out_0, out
         c_pairs = [own([P, R], BF16, "c_pairs%d" % n)[:] for n in range(PACK)]
         c_grouped = {0: g_raw[:, :HALF].bitcast(BF16)}
         last_grouped = [own([P, R // 2], BF16, "last_grouped")[:], in_words(0, FIRST_LANE[2], R // 2)]
-        r_got = {n: own([P, R], F32, "r_got%d" % n)[:] for n in (0, 2)}
+        r_got = {n: own([P, R], F32, "r_got%d" % n)[:] for n in range(PACK - 1)}
         r_got[3] = in_words(0, CHUNK, 2 * R).bitcast(F32)
-        dt = {(n, lo): own([P, HALF], F32, "dt%d_%d" % (n, lo))[:] for n, lo in ((0, 0), (0, HALF), (1, 0), (1, HALF), (3, 0))}
+        dt = {(n, lo): own([P, HALF], F32, "dt%d_%d" % (n, lo))[:] for n, lo in ((1, 0), (1, HALF), (3, 0))}
         dt.update({(2, HALF): in_words(0, FIRST_LANE[4], R).bitcast(F32), (3, HALF): in_words(1, 3 * CHUNK - P, R).bitcast(F32)})
         staged = pair_words(CHUNK, 3 * CHUNK)[:, 1, :, 1].rearrange("p (j m) -> p j m", j=2)[:, :, : TAILS - FIRST_LANE[4]]
 
@@ -173,7 +169,7 @@ def tile_attend_gdistm_t_pl_kernel(tc, hT, rT, G, hoffs, roffs, offs, out_0, out
         nc.vector.tensor_copy(*c_views(0, R // 2, R))
         turn(0)
 
-        g_grouped = [own([P, HALF, PACK], BF16, "g_grouped0"), placed([P, HALF, PACK], BF16, "g_grouped1", 4096)]
+        g_grouped = [own([P, HALF, PACK], BF16, "g_grouped%d" % a) for a in range(2)]
 
         def g_views(a):
             dst = g_grouped[a][:].rearrange("q (c i) t -> q c t i", i=4)
@@ -194,6 +190,9 @@ def tile_attend_gdistm_t_pl_kernel(tc, hT, rT, G, hoffs, roffs, offs, out_0, out
         quantize_g(0)
         quantize_c(0)
         quantize_g(1)
+        nc.scalar.activation(r_got[1], r_tab[1][:].indirect(r_list[:]), copy)
+        first_dt = own([P, SLOTS], F32, "first_dt", "r_tab1")
+        dt.update({(0, lo): first_dt[:, lo : lo + HALF] for lo in (0, HALF)})
         for lo in (0, HALF):
             acc = product(0, lo, lo + HALF)
             nc.scalar.copy(dt[0, lo], acc[:])
@@ -202,7 +201,6 @@ def tile_attend_gdistm_t_pl_kernel(tc, hT, rT, G, hoffs, roffs, offs, out_0, out
         store(0)
         nc.scalar.copy(*lane_views(0, *FIRST_LANE[3:5]))
 
-        r_got[1] = placed([P, R], F32, "r_got1", 4096)[:]
         def fetch_and_scatter(n):
             acc = {lo: product(n, lo, lo + HALF) for lo in (0, HALF)}
             for lo in (0, HALF):
@@ -211,23 +209,20 @@ def tile_attend_gdistm_t_pl_kernel(tc, hT, rT, G, hoffs, roffs, offs, out_0, out
                 scatter_on_scalar(n, lo)
             store(n)
 
-        gather_r(1)
         gather_h(1)
         round_c(1)
         gather_r(2)
         turn(1)
-        c_grouped[1] = own([P, R], BF16, "c_grouped1", "r_tab2")[:]
-        for lo in (0, P // 2):
-            nc.vector.tensor_copy(*group_views(1, lo, lo + P // 2))
-        for lo in (0, P // 2):
-            quantize_c(1, lo, lo + P // 2)
+        for lo in (0, R // 2):
+            gather_h(2, lo, lo + R // 2)
+        c_grouped[1] = r_got[2][:, : R // 2].bitcast(BF16)
+        nc.vector.tensor_copy(*group_views(1))
+        round_c(2)
+        quantize_c(1)
         fetch_and_scatter(1)
-        nc.scalar.copy(*lane_views(1, *FIRST_LANE[3:5]))
         for n in (0, 1):
             nc.scalar.copy(staged[:, n, :], window[n][:, FIRST_LANE[4] :])
 
-        gather_h(2)
-        round_c(2)
         pool_round(*lane_views(0, *FIRST_LANE[0:2]))
         gather_r(3)
         turn(2)
@@ -246,7 +241,7 @@ def tile_attend_gdistm_t_pl_kernel(tc, hT, rT, G, hoffs, roffs, offs, out_0, out
         for lo in (0, P // 2):
             quantize_c(3, lo, lo + P // 2)
         pool_round(*lane_views(0, *FIRST_LANE[2:4]))
-        pool_round(*lane_views(1, 0, FIRST_LANE[3]))
+        pool_round(*lane_views(1, 0, FIRST_LANE[4]))
         dt[2, 0] = own([P, HALF], F32, "dt2_0", "last_grouped")[:]
         nc.vector.tensor_copy(dt[2, 0], acc[0][:])
         nc.scalar.copy(dt[2, HALF], acc[HALF][:])
@@ -295,8 +290,8 @@ def tile_attend_gdistm_t_pl_kernel(tc, hT, rT, G, hoffs, roffs, offs, out_0, out
             nc.vector.tensor_copy(*weave_views(i))
         for i in (2, 3):
             quantize_planes(i)
-        for i in (4, 5):
-            nc.vector.tensor_copy(*weave_views(i))
+        nc.vector.tensor_copy(*weave_views(4))
+        nc.scalar.copy(*weave_views(5))
         for i in (4, 5):
             quantize_planes(i)
         scale_rows = out_scales.rearrange("f (k c) -> k f c", k=chunks)

@@ -26,7 +26,7 @@ PIECE = 256
 FLOPS = 2 * D * R * SLOTS
 
 LANES = (0, 1, 2, 3)
-FIRST_LANE = (0, 512, 1152, 1280, 2016)
+FIRST_LANE = (0, 256, 768, 896, 2016)
 THIRD_LANE = 1280
 
 
@@ -83,10 +83,11 @@ def tile_attend_gdistm_t_pl_kernel(tc, hT, rT, G, hoffs, roffs, offs, out_0, out
         for n in (2, 3):
             nc.gpsimd.memset(window[n][:], 0.0)
 
-        pairs = own([P, PACK * TAILS], BF16, "pairs")
+        pair_tile = own([P, R + PACK * TAILS], BF16, "pair_tile")
+        pairs = pair_tile[:, R:]
 
         def pair_words(lo, hi):
-            return pairs[:].rearrange("p (u c e) -> p u c e", u=2, e=2)[:, :, lo:hi, :]
+            return pairs.rearrange("p (u c e) -> p u c e", u=2, e=2)[:, :, lo:hi, :]
 
         def in_words(u, col, count):
             first = 2 * (u * TAILS + col)
@@ -97,12 +98,12 @@ def tile_attend_gdistm_t_pl_kernel(tc, hT, rT, G, hoffs, roffs, offs, out_0, out
         turned = [ps.tile([P, 2, P], F32, name="turned%d" % n, tag="turned%d" % (n % 2)) for n in range(PACK)]
         g_codes = own([P, SLOTS], U32, "g_codes")
         g_scales = own([P, SLOTS], U8, "g_scales")
-        c_rows = [own([P, R], F32, "c_rows%d" % n)[:] if n != 2 else in_words(0, 0, 2 * R).bitcast(F32) for n in range(PACK)]
+        c_rows = [own([P, R], F32, "c_rows%d" % n)[:] if n != 2 else in_words(0, FIRST_LANE[1], 2 * R).bitcast(F32) for n in range(PACK)]
         c_pairs = [own([P, R], BF16, "c_pairs%d" % n)[:] for n in range(PACK)]
         c_grouped = {0: g_raw[:, :HALF].bitcast(BF16)}
         last_grouped = [own([P, R // 2], BF16, "last_grouped")[:], in_words(0, FIRST_LANE[2], R // 2)]
         r_got = {n: own([P, R], F32, "r_got%d" % n)[:] for n in range(PACK - 1)}
-        r_got[3] = in_words(0, CHUNK, 2 * R).bitcast(F32)
+        r_got[3] = pair_tile[:, : 2 * R].bitcast(F32)
         dt = {(n, lo): own([P, HALF], F32, "dt%d_%d" % (n, lo))[:] for n, lo in ((1, 0), (1, HALF), (3, 0))}
         dt.update({(2, HALF): in_words(0, FIRST_LANE[4], R).bitcast(F32), (3, HALF): in_words(1, 3 * CHUNK - P, R).bitcast(F32)})
         staged = pair_words(CHUNK, 3 * CHUNK)[:, 1, :, 1].rearrange("p (j m) -> p j m", j=2)[:, :, : TAILS - FIRST_LANE[4]]
@@ -223,17 +224,17 @@ def tile_attend_gdistm_t_pl_kernel(tc, hT, rT, G, hoffs, roffs, offs, out_0, out
         for n in (0, 1):
             nc.scalar.copy(staged[:, n, :], window[n][:, FIRST_LANE[4] :])
 
-        pool_round(*lane_views(0, *FIRST_LANE[0:2]))
+        pool_round(*lane_views(0, *FIRST_LANE[1:3]))
         gather_r(3)
         turn(2)
         for lo in (0, R // 2):
             gather_h(3, lo, lo + R // 2)
-        c_grouped[2] = in_words(0, CHUNK, R)
+        c_grouped[2] = pair_tile[:, :R]
         nc.vector.tensor_copy(*group_views(2))
         round_c(3)
         quantize_c(2)
 
-        nc.vector.tensor_copy(*lane_views(0, *FIRST_LANE[1:3]))
+        nc.vector.tensor_copy(*lane_views(0, *FIRST_LANE[0:2]))
         turn(3)
         acc = {lo: product(2, lo, lo + HALF) for lo in (0, HALF)}
         for lo in (0, P // 2):
@@ -260,7 +261,7 @@ def tile_attend_gdistm_t_pl_kernel(tc, hT, rT, G, hoffs, roffs, offs, out_0, out
 
         def weave_views(i):
             dst = y_grouped[i][:].rearrange("p c t -> p (c t)").bitcast(F32).rearrange("p (c u) -> p c u", u=2)
-            return dst, pairs[:].bitcast(F32).rearrange("p (u c) -> p c u", u=2)[:, edges[i] : edges[i + 1], :]
+            return dst, pairs.bitcast(F32).rearrange("p (u c) -> p c u", u=2)[:, edges[i] : edges[i + 1], :]
 
         def quantize_planes(i):
             a, b = edges[i], edges[i + 1]

@@ -239,19 +239,20 @@ def tile_attend_gdistm_t_pl_kernel(tc, hT, rT, G, hoffs, roffs, offs, out_0, out
         acc = {lo: product(2, lo, lo + HALF) for lo in (0, HALF)}
         for lo in (0, P // 2):
             nc.vector.tensor_copy(*group_views(3, lo, lo + P // 2))
+        dt[2, 0] = own([P, HALF], F32, "dt2_0", "c_pairs3")[:]
+        nc.vector.tensor_copy(dt[2, 0], acc[0][:])
         for lo in (0, P // 2):
             quantize_c(3, lo, lo + P // 2)
         pool_round(*lane_views(0, *FIRST_LANE[2:4]))
         pool_round(*lane_views(1, 0, FIRST_LANE[4]))
-        dt[2, 0] = own([P, HALF], F32, "dt2_0", "last_grouped")[:]
-        nc.vector.tensor_copy(dt[2, 0], acc[0][:])
         nc.scalar.copy(dt[2, HALF], acc[HALF][:])
         for lo in (0, HALF):
             nc.vector.tensor_copy(window[2][:].indirect(t_list[:, lo // 16 : (lo + HALF) // 16]), dt[2, lo])
         store(2)
         fetch_and_scatter(3)
-        nc.vector.tensor_copy(*lane_views(2, 0, THIRD_LANE))
+        nc.vector.tensor_copy(*lane_views(2, CHUNK, THIRD_LANE))
         nc.vector.tensor_copy(pair_words(FIRST_LANE[4], TAILS)[:, 0].rearrange("p c e -> p e c"), staged)
+        nc.vector.tensor_copy(*lane_views(2, 0, CHUNK))
 
         edges = (0, 256, 512, 1024, 1536, 1792, 2048)
         y_grouped = [own([P, edges[i + 1] - edges[i], PACK], BF16, "y_grouped%d" % i) for i in range(6)]

@@ -27,7 +27,7 @@ FLOPS = 2 * D * R * SLOTS
 
 LANES = (0, 1, 2, 3)
 FIRST_LANE = (0, 256, 768, 896, 2016)
-THIRD_LANE = 1280
+THIRD_LANE = 1536
 
 
 def tile_attend_gdistm_t_pl_kernel(tc, hT, rT, G, hoffs, roffs, offs, out_0, out_1, out_2):
@@ -105,7 +105,7 @@ def tile_attend_gdistm_t_pl_kernel(tc, hT, rT, G, hoffs, roffs, offs, out_0, out
         r_got = {n: own([P, R], F32, "r_got%d" % n)[:] for n in range(PACK - 1)}
         r_got[3] = pair_tile[:, : 2 * R].bitcast(F32)
         dt = {(n, lo): own([P, HALF], F32, "dt%d_%d" % (n, lo))[:] for n, lo in ((1, 0), (1, HALF), (3, 0))}
-        dt.update({(2, HALF): in_words(0, FIRST_LANE[4], R).bitcast(F32), (3, HALF): in_words(1, 3 * CHUNK - P, R).bitcast(F32)})
+        dt.update({(2, HALF): in_words(0, FIRST_LANE[4], R).bitcast(F32), (3, HALF): in_words(1, THIRD_LANE, R).bitcast(F32)})
         staged = pair_words(CHUNK, 3 * CHUNK)[:, 1, :, 1].rearrange("p (j m) -> p j m", j=2)[:, :, : TAILS - FIRST_LANE[4]]
 
         def gather_r(n):
@@ -279,7 +279,6 @@ def tile_attend_gdistm_t_pl_kernel(tc, hT, rT, G, hoffs, roffs, offs, out_0, out
         for i in (0, 1):
             nc.vector.tensor_copy(*lane_views(3, edges[i], edges[i + 1]))
         nc.scalar.copy(*lane_views(3, edges[2], edges[3]))
-        nc.scalar.copy(*lane_views(2, THIRD_LANE, edges[4]))
         nc.scalar.copy(*lane_views(3, edges[3], edges[4]))
         nc.scalar.copy(*lane_views(2, edges[4], edges[6]))
         for i in (4, 5):

@@ -22,12 +22,14 @@ HEADS = 2048
 RELS = 1024
 TAILS = 2048
 CHUNK = 512
-PIECE = 256
 FLOPS = 2 * D * R * SLOTS
 
-LANES = (0, 1, 2, 3)
-FIRST_LANE = (0, 256, 768, 896, 2016)
-THIRD_LANE = 1536
+LANE0 = (0, 128, 640, 1120, 1760, 2048)
+LANE1 = 992
+MIDDLE = TAILS // 2
+PASSED = 48
+PIECES = (0, 256, 512, 1024, 1536, 1792, 2048)
+WORD_STORES = (0, 512, 1024, 1536, 1792, 2048)
 
 
 def tile_attend_gdistm_t_pl_kernel(tc, hT, rT, G, hoffs, roffs, offs, out_0, out_1, out_2):
@@ -35,7 +37,6 @@ def tile_attend_gdistm_t_pl_kernel(tc, hT, rT, G, hoffs, roffs, offs, out_0, out
     mult = mybir.AluOpType.mult
     add = mybir.AluOpType.add
     copy = mybir.ActivationFunctionType.Copy
-    chunks = TAILS // CHUNK
 
     with ExitStack() as ctx:
         lists = ctx.enter_context(tc.tile_pool(name="lists", bufs=1))
@@ -61,17 +62,17 @@ def tile_attend_gdistm_t_pl_kernel(tc, hT, rT, G, hoffs, roffs, offs, out_0, out
         g_raw = own([P, PACK * SLOTS], F32, "g_raw")
         window = [own([P, TAILS], F32, "window%d" % n) for n in range(PACK)]
 
-        nc.sync.dma_start(r_tab[0][:], r_rows[:, LANES[0], :])
+        nc.sync.dma_start(r_tab[0][:], r_rows[:, 0, :])
         nc.sync.dma_start(r_list[:], roffs)
         nc.sync.dma_start(h_list[:], hoffs)
-        nc.sync.dma_start(h_tab[0][:], h_rows[:, LANES[0], :])
+        nc.sync.dma_start(h_tab[0][:], h_rows[:, 0, :])
         nc.sync.dma_start(g_raw[:], g_rows)
-        nc.sync.dma_start(r_tab[1][:], r_rows[:, LANES[1], :])
+        nc.sync.dma_start(r_tab[1][:], r_rows[:, 1, :])
         nc.sync.dma_start(t_list[:], offs)
-        nc.sync.dma_start(h_tab[1][:], h_rows[:, LANES[1], :])
+        nc.sync.dma_start(h_tab[1][:], h_rows[:, 1, :])
         for n in (2, 3):
-            nc.sync.dma_start(r_tab[n][:], r_rows[:, LANES[n], :])
-            nc.sync.dma_start(h_tab[n][:], h_rows[:, LANES[n], :])
+            nc.sync.dma_start(r_tab[n][:], r_rows[:, n, :])
+            nc.sync.dma_start(h_tab[n][:], h_rows[:, n, :])
 
         ident = own([P, P], F32, "ident")
         make_identity(nc, ident[:])
@@ -83,99 +84,95 @@ def tile_attend_gdistm_t_pl_kernel(tc, hT, rT, G, hoffs, roffs, offs, out_0, out
         for n in (2, 3):
             nc.gpsimd.memset(window[n][:], 0.0)
 
-        pair_tile = own([P, R + PACK * TAILS], BF16, "pair_tile")
-        pairs = pair_tile[:, R:]
+        pairs = own([P, PACK * TAILS], BF16, "pairs")[:]
 
         def pair_words(lo, hi):
             return pairs.rearrange("p (u c e) -> p u c e", u=2, e=2)[:, :, lo:hi, :]
 
-        def in_words(u, col, count):
-            first = 2 * (u * TAILS + col)
-            return pairs[:, first : first + count]
+        def in_pairs(col, words, dtype):
+            return pairs[:, 2 * col : 2 * (col + words)].bitcast(dtype)
 
+        halves = (0, 1)
         c_scales = [own([P, P], U8, "c_scales%d" % n) for n in range(PACK)]
-        c_codes = {n: own([P, P], U32, "c_codes%d" % n) for n in range(PACK)}
+        c_codes = [own([P, P], U32, "c_codes%d" % n) for n in range(PACK)]
         turned = [ps.tile([P, 2, P], F32, name="turned%d" % n, tag="turned%d" % (n % 2)) for n in range(PACK)]
         g_codes = own([P, SLOTS], U32, "g_codes")
         g_scales = own([P, SLOTS], U8, "g_scales")
-        c_rows = [own([P, R], F32, "c_rows%d" % n)[:] if n != 2 else in_words(0, FIRST_LANE[1], 2 * R).bitcast(F32) for n in range(PACK)]
+        g_grouped = [own([P, HALF, PACK], BF16, "g_grouped%d" % a) for a in halves]
+        c_rows = [in_pairs(LANE0[3], R, F32) if n == 2 else own([P, R], F32, "c_rows%d" % n)[:] for n in range(PACK)]
         c_pairs = [own([P, R], BF16, "c_pairs%d" % n)[:] for n in range(PACK)]
-        c_grouped = {0: g_raw[:, :HALF].bitcast(BF16)}
-        last_grouped = [own([P, R // 2], BF16, "last_grouped")[:], in_words(0, FIRST_LANE[2], R // 2)]
-        r_got = {n: own([P, R], F32, "r_got%d" % n)[:] for n in range(PACK - 1)}
-        r_got[3] = pair_tile[:, : 2 * R].bitcast(F32)
-        dt = {(n, lo): own([P, HALF], F32, "dt%d_%d" % (n, lo))[:] for n, lo in ((1, 0), (1, HALF), (3, 0))}
-        dt.update({(2, HALF): in_words(0, FIRST_LANE[4], R).bitcast(F32), (3, HALF): in_words(1, THIRD_LANE, R).bitcast(F32)})
-        staged = pair_words(CHUNK, 3 * CHUNK)[:, 1, :, 1].rearrange("p (j m) -> p j m", j=2)[:, :, : TAILS - FIRST_LANE[4]]
+        c_grouped = {(n, a): own([P, R // 2], BF16, "c_grouped%d_%d" % (n, a))[:] for n in (1, 2) for a in halves}
+        c_grouped[3, 0] = in_pairs(LANE0[0], R // 4, BF16)
+        c_grouped[3, 1] = in_pairs(TAILS - R // 8, R // 4, BF16)
+        first_grouped = own([P, R], BF16, "first_grouped")[:]
+        r_got = {n: own([P, R], F32, "r_got%d" % n)[:] for n in (0, 2)}
+        r_got[3] = in_pairs(LANE0[1], R, F32)
+        dt = {(n, a): own([P, HALF], F32, "dt%d_%d" % (n, a))[:] for n in range(PACK - 1) for a in halves}
+        last_dt = own([P, SLOTS], F32, "last_dt")
+        passing = pair_words(0, CHUNK)[:, 1, :, 1].rearrange("p (j m) -> p j m", j=2)[:, :, : PASSED // 2]
 
         def gather_r(n):
             nc.vector.tensor_copy(r_got[n], r_tab[n][:].indirect(r_list[:]))
 
-        def gather_h(n, lo=0, hi=R):
-            nc.vector.tensor_tensor(c_rows[n][:, lo:hi], h_tab[n][:].indirect(h_list[:, lo // 16 : hi // 16]), r_got[n][:, lo:hi], mult)
+        def gather_h(n, a):
+            cols = slice(a * R // 2, (a + 1) * R // 2)
+            nc.vector.tensor_tensor(c_rows[n][:, cols], h_tab[n][:].indirect(h_list[:, cols.start // 16 : cols.stop // 16]), r_got[n][:, cols], mult)
 
-        def c_views(n, lo=0, hi=R):
+        def c_views(n, a):
+            lo, hi = a * R // 2, (a + 1) * R // 2
             dst = c_pairs[n].rearrange("p (u q e) -> p u q e", u=2, e=2)[:, :, lo // PACK : hi // PACK, :]
             return dst, c_rows[n][:, lo:hi].rearrange("p (q u e) -> p u q e", u=2, e=2)
-
-        def round_c(n):
-            dst, src = c_views(n)
-            for u in range(2):
-                nc.vector.tensor_copy(dst[:, u], src[:, u])
-
-        def pool_round(dst, src):
-            nc.gpsimd.tensor_scalar(dst, src, 1.0, -0.0, mult, add)
 
         def turn(n):
             for u in range(2):
                 nc.tensor.transpose(turned[n][:, u, :], c_pairs[n][:, u * 2 * P : (u + 1) * 2 * P].bitcast(F32), ident[:])
 
-        def grouped(n, lo, hi):
-            return last_grouped[2 * lo // P] if n == 3 else c_grouped[n][:, PACK * lo : PACK * hi]
+        def group(grouped, n, lo, hi):
+            dst = grouped.bitcast(F32).rearrange("q (p u) -> q p u", u=2)
+            nc.vector.tensor_copy(dst, turned[n][:, :, lo:hi].rearrange("q u p -> q p u"))
 
-        def group_views(n, lo=0, hi=P):
-            dst = grouped(n, lo, hi).bitcast(F32).rearrange("q (p u) -> q p u", u=2)
-            return dst, turned[n][:, :, lo:hi].rearrange("q u p -> q p u")
+        def quantize_c(grouped, n, lo, hi):
+            nc.vector.quantize_mx(out=c_codes[n][:, lo:hi].bitcast(E4M3), scales=c_scales[n][:, lo:hi], in_=grouped)
 
-        def quantize_c(n, lo=0, hi=P):
-            nc.vector.quantize_mx(out=c_codes[n][:, lo:hi].bitcast(E4M3), scales=c_scales[n][:, lo:hi], in_=grouped(n, lo, hi))
-
-        def product(n, lo, hi):
-            acc = ps.tile([P, hi - lo], F32, name="acc%d_%d" % (n, lo), tag="acc%d_%d" % (n % 2, lo))
+        def product(n, a):
+            cols = slice(a * HALF, (a + 1) * HALF)
+            acc = ps.tile([P, HALF], F32, name="acc%d_%d" % (n, a), tag="acc%d_%d" % (n % 2, a))
             nc.tensor.matmul_mx(
                 out=acc[:],
                 lhsT=c_codes[n][:].bitcast(E4M3),
                 lhsT_scale=c_scales[n][:],
-                rhs=g_codes[:, lo:hi].bitcast(E5M2),
-                rhs_scale=g_scales[:, lo:hi],
+                rhs=g_codes[:, cols].bitcast(E5M2),
+                rhs_scale=g_scales[:, cols],
                 start=True,
                 stop=True,
             )
             return acc
 
-        def scatter_on_scalar(n, lo):
-            target = window[n][:].indirect(t_list[:, lo // 16 : (lo + HALF) // 16])
-            nc.scalar.activation(target, dt[n, lo], copy)
+        def places(n, a):
+            return window[n][:].indirect(t_list[:, a * HALF // 16 : (a + 1) * HALF // 16])
 
         def store(n):
-            nc.sync.dma_start(out_rows[:, LANES[n], :], window[n][:])
+            nc.sync.dma_start(out_rows[:, n, :], window[n][:])
+
+        def scalar_step(n):
+            acc = [product(n, a) for a in halves]
+            for a in halves:
+                nc.scalar.copy(dt[n, a], acc[a][:])
+            for a in halves:
+                nc.scalar.activation(places(n, a), dt[n, a], copy)
+            store(n)
 
         def lane_views(n, lo, hi):
-            return pair_words(lo, hi)[:, LANES[n] // 2, :, LANES[n] % 2], window[n][:, lo:hi]
+            return pair_words(lo, hi)[:, n // 2, :, n % 2], window[n][:, lo:hi]
 
-        gather_r(0)
-        gather_h(0, 0, R // 2)
-        nc.scalar.copy(*c_views(0, 0, R // 2))
-        gather_h(0, R // 2, R)
-        nc.vector.tensor_copy(*c_views(0, R // 2, R))
-        turn(0)
+        def pool_round(dst, src):
+            nc.gpsimd.tensor_scalar(dst, src, 1.0, -0.0, mult, add)
 
-        g_grouped = [own([P, HALF, PACK], BF16, "g_grouped%d" % a) for a in range(2)]
-
-        def g_views(a):
-            dst = g_grouped[a][:].rearrange("q (c i) t -> q c t i", i=4)
+        def g_views(a, b):
+            dst = g_grouped[a][:, b * P : (b + 1) * P, :].rearrange("q (c i) t -> q c t i", i=4)
             rows = g_raw[:].rearrange("q (t c) -> q t c", t=PACK)
-            return dst, rows[:, :, a * HALF : (a + 1) * HALF].rearrange("q t (c i) -> q c t i", i=4)
+            first = a * HALF + b * P
+            return dst, rows[:, :, first : first + P].rearrange("q t (c i) -> q c t i", i=4)
 
         def quantize_g(a):
             cols = slice(a * HALF, (a + 1) * HALF)
@@ -185,117 +182,94 @@ def tile_attend_gdistm_t_pl_kernel(tc, hT, rT, G, hoffs, roffs, offs, out_0, out
                 in_=g_grouped[a][:].rearrange("q c t -> q (c t)"),
             )
 
-        nc.scalar.copy(*g_views(1))
-        nc.vector.tensor_copy(*g_views(0))
-        nc.vector.tensor_copy(*group_views(0))
+        def heads(n):
+            for a in halves:
+                gather_h(n, a)
+            for a in halves:
+                nc.vector.tensor_copy(*c_views(n, a))
+            turn(n)
+
+        def operand(n):
+            for a in halves:
+                group(c_grouped[n, a], n, a * P // 2, (a + 1) * P // 2)
+            for a in halves:
+                quantize_c(c_grouped[n, a], n, a * P // 2, (a + 1) * P // 2)
+
+        gather_r(0)
+        gather_h(0, 0)
+        nc.scalar.copy(*c_views(0, 0))
+        gather_h(0, 1)
+        nc.vector.tensor_copy(*c_views(0, 1))
+        turn(0)
+        for a in halves:
+            nc.vector.tensor_copy(*g_views(a, 0))
+            nc.scalar.copy(*g_views(a, 1))
+        group(first_grouped, 0, 0, P)
         quantize_g(0)
-        quantize_c(0)
+        quantize_c(first_grouped, 0, 0, P)
         quantize_g(1)
-        nc.scalar.activation(r_got[1], r_tab[1][:].indirect(r_list[:]), copy)
-        first_dt = own([P, SLOTS], F32, "first_dt", "r_tab1")
-        dt.update({(0, lo): first_dt[:, lo : lo + HALF] for lo in (0, HALF)})
-        for lo in (0, HALF):
-            acc = product(0, lo, lo + HALF)
-            nc.scalar.copy(dt[0, lo], acc[:])
-        for lo in (0, HALF):
-            scatter_on_scalar(0, lo)
-        store(0)
-        nc.scalar.copy(*lane_views(0, *FIRST_LANE[3:5]))
+        r_got[1] = own([P, R], F32, "r_got1", "g_grouped0")[:]
+        gather_r(1)
+        scalar_step(0)
+        nc.scalar.copy(*lane_views(0, LANE0[2], LANE0[3]))
 
-        def fetch_and_scatter(n):
-            acc = {lo: product(n, lo, lo + HALF) for lo in (0, HALF)}
-            for lo in (0, HALF):
-                nc.scalar.copy(dt[n, lo], acc[lo][:])
-            for lo in (0, HALF):
-                scatter_on_scalar(n, lo)
-            store(n)
+        for n in (1, 2):
+            heads(n)
+            gather_r(n + 1)
+            operand(n)
+            scalar_step(n)
+        pool_round(*lane_views(0, LANE0[3], LANE0[4]))
+        nc.scalar.copy(*lane_views(2, MIDDLE, TAILS))
 
-        gather_h(1)
-        round_c(1)
-        gather_r(2)
-        turn(1)
-        for lo in (0, R // 2):
-            gather_h(2, lo, lo + R // 2)
-        c_grouped[1] = r_got[2][:, : R // 2].bitcast(BF16)
-        nc.vector.tensor_copy(*group_views(1))
-        round_c(2)
-        quantize_c(1)
-        fetch_and_scatter(1)
-        for n in (0, 1):
-            nc.scalar.copy(staged[:, n, :], window[n][:, FIRST_LANE[4] :])
+        heads(3)
+        nc.vector.tensor_copy(*lane_views(0, LANE0[1], LANE0[2]))
+        operand(3)
+        nc.vector.tensor_copy(*lane_views(0, LANE0[0], LANE0[1]))
+        nc.vector.tensor_copy(*lane_views(1, 0, LANE1))
+        pool_round(*lane_views(0, LANE0[4], TAILS))
+        pool_round(*lane_views(1, LANE1, TAILS))
+        pool_round(*lane_views(2, 0, MIDDLE - PASSED))
+        pool_round(passing, window[2][:, MIDDLE - PASSED : MIDDLE].rearrange("p (j m) -> p j m", j=2))
+        acc = [product(3, a) for a in halves]
+        for a in halves:
+            nc.vector.tensor_copy(last_dt[:, a * HALF : (a + 1) * HALF], acc[a][:])
+        nc.vector.tensor_copy(window[3][:].indirect(t_list[:]), last_dt[:])
+        store(3)
+        nc.vector.tensor_copy(pair_words(MIDDLE - PASSED, MIDDLE)[:, 1, :, 0].rearrange("p (j m) -> p j m", j=2), passing)
 
-        pool_round(*lane_views(0, *FIRST_LANE[1:3]))
-        gather_r(3)
-        turn(2)
-        for lo in (0, R // 2):
-            gather_h(3, lo, lo + R // 2)
-        c_grouped[2] = pair_tile[:, :R]
-        nc.vector.tensor_copy(*group_views(2))
-        round_c(3)
-        quantize_c(2)
-
-        nc.vector.tensor_copy(*lane_views(0, *FIRST_LANE[0:2]))
-        turn(3)
-        acc = {lo: product(2, lo, lo + HALF) for lo in (0, HALF)}
-        for lo in (0, P // 2):
-            nc.vector.tensor_copy(*group_views(3, lo, lo + P // 2))
-        dt[2, 0] = own([P, HALF], F32, "dt2_0", "c_pairs3")[:]
-        nc.vector.tensor_copy(dt[2, 0], acc[0][:])
-        for lo in (0, P // 2):
-            quantize_c(3, lo, lo + P // 2)
-        pool_round(*lane_views(0, *FIRST_LANE[2:4]))
-        pool_round(*lane_views(1, 0, FIRST_LANE[4]))
-        nc.scalar.copy(dt[2, HALF], acc[HALF][:])
-        for lo in (0, HALF):
-            nc.vector.tensor_copy(window[2][:].indirect(t_list[:, lo // 16 : (lo + HALF) // 16]), dt[2, lo])
-        store(2)
-        fetch_and_scatter(3)
-        nc.vector.tensor_copy(*lane_views(2, CHUNK, THIRD_LANE))
-        nc.vector.tensor_copy(pair_words(FIRST_LANE[4], TAILS)[:, 0].rearrange("p c e -> p e c"), staged)
-        nc.vector.tensor_copy(*lane_views(2, 0, CHUNK))
-
-        edges = (0, 256, 512, 1024, 1536, 1792, 2048)
-        y_grouped = [own([P, edges[i + 1] - edges[i], PACK], BF16, "y_grouped%d" % i) for i in range(6)]
+        y_grouped = [own([P, PIECES[i + 1] - PIECES[i], PACK], BF16, "y_grouped%d" % i) for i in range(6)]
         y_codes = own([P, TAILS], U32, "y_codes")
-        y_scales = own([P, CHUNK], U8, "y_scales")
-        stores = ((0, 512), (512, 1024), (1024, 1536), (1536, 1792), (1792, 2048))
+        y_scales = own([P, MIDDLE], U8, "y_scales")
 
         def weave_views(i):
             dst = y_grouped[i][:].rearrange("p c t -> p (c t)").bitcast(F32).rearrange("p (c u) -> p c u", u=2)
-            return dst, pairs.bitcast(F32).rearrange("p (u c) -> p c u", u=2)[:, edges[i] : edges[i + 1], :]
+            return dst, pairs.bitcast(F32).rearrange("p (u c) -> p c u", u=2)[:, PIECES[i] : PIECES[i + 1], :]
 
         def quantize_planes(i):
-            a, b = edges[i], edges[i + 1]
-            k = a // CHUNK
+            a, b = PIECES[i], PIECES[i + 1]
+            k = a // MIDDLE
             nc.vector.quantize_mx(
                 out=y_codes[:, a:b].bitcast(E4M3),
-                scales=y_scales[4 * k :, a - k * CHUNK : b - k * CHUNK],
+                scales=y_scales[4 * k :, a - k * MIDDLE : b - k * MIDDLE],
                 in_=y_grouped[i][:].rearrange("p c t -> p (c t)"),
             )
-            for first, last in stores:
-                if last == b:
-                    nc.sync.dma_start(out_words[:, first:last], y_codes[:, first:last].bitcast(I32))
+            if b in WORD_STORES:
+                first = WORD_STORES[WORD_STORES.index(b) - 1]
+                nc.sync.dma_start(out_words[:, first:b], y_codes[:, first:b].bitcast(I32))
 
-        for i in (0, 1):
-            nc.vector.tensor_copy(*lane_views(3, edges[i], edges[i + 1]))
-        nc.scalar.copy(*lane_views(3, edges[2], edges[3]))
-        nc.scalar.copy(*lane_views(3, edges[3], edges[4]))
-        nc.scalar.copy(*lane_views(2, edges[4], edges[6]))
-        for i in (4, 5):
-            nc.scalar.copy(*lane_views(3, edges[i], edges[i + 1]))
+        nc.vector.tensor_copy(*lane_views(3, 0, PIECES[1]))
+        nc.vector.tensor_copy(*lane_views(3, PIECES[1], MIDDLE))
+        nc.scalar.copy(*lane_views(3, MIDDLE, PIECES[4]))
+        nc.scalar.copy(*lane_views(3, PIECES[4], TAILS))
+        for i in (3, 4, 5):
+            nc.scalar.copy(*weave_views(i))
         for i in (0, 1):
             nc.vector.tensor_copy(*weave_views(i))
-        for i in (0, 1):
+        quantize_planes(0)
+        nc.vector.tensor_copy(*weave_views(2))
+        for i in range(1, 6):
             quantize_planes(i)
-        for i in (2, 3):
-            nc.vector.tensor_copy(*weave_views(i))
-        for i in (2, 3):
-            quantize_planes(i)
-        nc.vector.tensor_copy(*weave_views(4))
-        nc.scalar.copy(*weave_views(5))
-        for i in (4, 5):
-            quantize_planes(i)
-        scale_rows = out_scales.rearrange("f (k c) -> k f c", k=chunks)
+        scale_rows = out_scales.rearrange("f (k c) -> k f c", k=2)
         for q in range(4):
             queue = nc.sync if q < 2 else nc.scalar
-            queue.dma_start(scale_rows[:, 4 * q : 4 * q + 4, :], y_scales[32 * q : 32 * q + 16, :].bitcast(I32))
+            queue.dma_start(scale_rows[:, 4 * q : 4 * q + 4, :], y_scales[32 * q : 32 * q + 8, :].bitcast(I32))

@@ -24,10 +24,12 @@ TAILS = 2048
 CHUNK = 512
 FLOPS = 2 * D * R * SLOTS
 
-LANE0 = (0, 128, 640, 1120, 1760, 2048)
-LANE1 = 992
+LANE0 = (0, 128, 768, 1248, 1984, 2048)
+LANE1 = 864
+LATE_CUT = 896
+QUERY_CUT = 384
 MIDDLE = TAILS // 2
-PASSED = 48
+PASSED = TAILS - LANE0[4]
 PIECES = (0, 256, 512, 1024, 1536, 1792, 2048)
 WORD_STORES = (0, 512, 1024, 1536, 1792, 2048)
 
@@ -114,12 +116,11 @@ def tile_attend_gdistm_t_pl_kernel(tc, hT, rT, G, hoffs, roffs, offs, out_0, out
         def gather_r(n):
             nc.vector.tensor_copy(r_got[n], r_tab[n][:].indirect(r_list[:]))
 
-        def gather_h(n, a):
-            cols = slice(a * R // 2, (a + 1) * R // 2)
+        def gather_h(n, cols):
             nc.vector.tensor_tensor(c_rows[n][:, cols], h_tab[n][:].indirect(h_list[:, cols.start // 16 : cols.stop // 16]), r_got[n][:, cols], mult)
 
-        def c_views(n, a):
-            lo, hi = a * R // 2, (a + 1) * R // 2
+        def c_views(n, cols):
+            lo, hi = cols.start, cols.stop
             dst = c_pairs[n].rearrange("p (u q e) -> p u q e", u=2, e=2)[:, :, lo // PACK : hi // PACK, :]
             return dst, c_rows[n][:, lo:hi].rearrange("p (q u e) -> p u q e", u=2, e=2)
 
@@ -134,9 +135,9 @@ def tile_attend_gdistm_t_pl_kernel(tc, hT, rT, G, hoffs, roffs, offs, out_0, out
         def quantize_c(grouped, n, lo, hi):
             nc.vector.quantize_mx(out=c_codes[n][:, lo:hi].bitcast(E4M3), scales=c_scales[n][:, lo:hi], in_=grouped)
 
-        def product(n, a):
-            cols = slice(a * HALF, (a + 1) * HALF)
-            acc = ps.tile([P, HALF], F32, name="acc%d_%d" % (n, a), tag="acc%d_%d" % (n % 2, a))
+        def product(n, a, width=HALF):
+            cols = slice(a * width, (a + 1) * width)
+            acc = ps.tile([P, width], F32, name="acc%d_%d" % (n, a), tag="acc%d" % ((2 * n + a) % 4))
             nc.tensor.matmul_mx(
                 out=acc[:],
                 lhsT=c_codes[n][:].bitcast(E4M3),
@@ -183,10 +184,11 @@ def tile_attend_gdistm_t_pl_kernel(tc, hT, rT, G, hoffs, roffs, offs, out_0, out
             )
 
         def heads(n):
-            for a in halves:
-                gather_h(n, a)
-            for a in halves:
-                nc.vector.tensor_copy(*c_views(n, a))
+            parts = (slice(0, QUERY_CUT), slice(QUERY_CUT, R))
+            for cols in parts:
+                gather_h(n, cols)
+            for cols in parts:
+                nc.vector.tensor_copy(*c_views(n, cols))
             turn(n)
 
         def operand(n):
@@ -196,10 +198,10 @@ def tile_attend_gdistm_t_pl_kernel(tc, hT, rT, G, hoffs, roffs, offs, out_0, out
                 quantize_c(c_grouped[n, a], n, a * P // 2, (a + 1) * P // 2)
 
         gather_r(0)
-        gather_h(0, 0)
-        nc.scalar.copy(*c_views(0, 0))
-        gather_h(0, 1)
-        nc.vector.tensor_copy(*c_views(0, 1))
+        gather_h(0, slice(0, R // 2))
+        nc.scalar.copy(*c_views(0, slice(0, R // 2)))
+        gather_h(0, slice(R // 2, R))
+        nc.vector.tensor_copy(*c_views(0, slice(R // 2, R)))
         turn(0)
         for a in halves:
             nc.vector.tensor_copy(*g_views(a, 0))
@@ -219,23 +221,22 @@ def tile_attend_gdistm_t_pl_kernel(tc, hT, rT, G, hoffs, roffs, offs, out_0, out
             operand(n)
             scalar_step(n)
         pool_round(*lane_views(0, LANE0[3], LANE0[4]))
-        nc.scalar.copy(*lane_views(2, MIDDLE, TAILS))
+        nc.scalar.copy(*lane_views(2, LATE_CUT, TAILS))
 
         heads(3)
         nc.vector.tensor_copy(*lane_views(0, LANE0[1], LANE0[2]))
         operand(3)
         nc.vector.tensor_copy(*lane_views(0, LANE0[0], LANE0[1]))
         nc.vector.tensor_copy(*lane_views(1, 0, LANE1))
-        pool_round(*lane_views(0, LANE0[4], TAILS))
         pool_round(*lane_views(1, LANE1, TAILS))
-        pool_round(*lane_views(2, 0, MIDDLE - PASSED))
-        pool_round(passing, window[2][:, MIDDLE - PASSED : MIDDLE].rearrange("p (j m) -> p j m", j=2))
-        acc = [product(3, a) for a in halves]
-        for a in halves:
-            nc.vector.tensor_copy(last_dt[:, a * HALF : (a + 1) * HALF], acc[a][:])
+        pool_round(*lane_views(2, 0, LATE_CUT))
+        pool_round(passing, window[0][:, LANE0[4] :].rearrange("p (j m) -> p j m", j=2))
+        acc = [product(3, a, P) for a in range(PACK)]
+        for a in range(PACK):
+            nc.vector.tensor_copy(last_dt[:, a * P : (a + 1) * P], acc[a][:])
         nc.vector.tensor_copy(window[3][:].indirect(t_list[:]), last_dt[:])
         store(3)
-        nc.vector.tensor_copy(pair_words(MIDDLE - PASSED, MIDDLE)[:, 1, :, 0].rearrange("p (j m) -> p j m", j=2), passing)
+        nc.vector.tensor_copy(pair_words(LANE0[4], TAILS)[:, 0, :, 0].rearrange("p (j m) -> p j m", j=2), passing)
 
         y_grouped = [own([P, PIECES[i + 1] - PIECES[i], PACK], BF16, "y_grouped%d" % i) for i in range(6)]
         y_codes = own([P, TAILS], U32, "y_codes")
@@ -258,8 +259,8 @@ def tile_attend_gdistm_t_pl_kernel(tc, hT, rT, G, hoffs, roffs, offs, out_0, out
                 nc.sync.dma_start(out_words[:, first:b], y_codes[:, first:b].bitcast(I32))
 
         nc.vector.tensor_copy(*lane_views(3, 0, PIECES[1]))
-        nc.vector.tensor_copy(*lane_views(3, PIECES[1], MIDDLE))
-        nc.scalar.copy(*lane_views(3, MIDDLE, PIECES[4]))
+        nc.vector.tensor_copy(*lane_views(3, PIECES[1], LATE_CUT))
+        nc.scalar.copy(*lane_views(3, LATE_CUT, PIECES[4]))
         nc.scalar.copy(*lane_views(3, PIECES[4], TAILS))
         for i in (3, 4, 5):
             nc.scalar.copy(*weave_views(i))

@@ -24,12 +24,12 @@ TAILS = 2048
 CHUNK = 512
 FLOPS = 2 * D * R * SLOTS
 
-LANE0 = (0, 128, 768, 1248, 1984, 2048)
-LANE1 = 864
+LANE0 = (0, 160, 352, 832, 1536, 1984)
+LANE1 = LANE0[3]
 LATE_CUT = 896
 QUERY_CUT = 384
 MIDDLE = TAILS // 2
-PASSED = TAILS - LANE0[4]
+PASSED = TAILS - LANE0[5]
 PIECES = (0, 256, 512, 1024, 1536, 1792, 2048)
 WORD_STORES = (0, 512, 1024, 1536, 1792, 2048)
 
@@ -86,7 +86,8 @@ def tile_attend_gdistm_t_pl_kernel(tc, hT, rT, G, hoffs, roffs, offs, out_0, out
         for n in (2, 3):
             nc.gpsimd.memset(window[n][:], 0.0)
 
-        pairs = own([P, PACK * TAILS], BF16, "pairs")[:]
+        pair_tile = own([P, 2 * QUERY_CUT + PACK * TAILS], BF16, "pair_tile")
+        pairs = pair_tile[:, 2 * QUERY_CUT :]
 
         def pair_words(lo, hi):
             return pairs.rearrange("p (u c e) -> p u c e", u=2, e=2)[:, :, lo:hi, :]
@@ -101,15 +102,15 @@ def tile_attend_gdistm_t_pl_kernel(tc, hT, rT, G, hoffs, roffs, offs, out_0, out
         g_codes = own([P, SLOTS], U32, "g_codes")
         g_scales = own([P, SLOTS], U8, "g_scales")
         g_grouped = [own([P, HALF, PACK], BF16, "g_grouped%d" % a) for a in halves]
-        c_rows = [in_pairs(LANE0[3], R, F32) if n == 2 else own([P, R], F32, "c_rows%d" % n)[:] for n in range(PACK)]
+        c_rows = [in_pairs(LANE0[n + 1], R, F32) if n >= 2 else own([P, R], F32, "c_rows%d" % n)[:] for n in range(PACK)]
         c_pairs = [own([P, R], BF16, "c_pairs%d" % n)[:] for n in range(PACK)]
         c_grouped = {(n, a): own([P, R // 2], BF16, "c_grouped%d_%d" % (n, a))[:] for n in (1, 2) for a in halves}
         c_grouped[3, 0] = in_pairs(LANE0[0], R // 4, BF16)
         c_grouped[3, 1] = in_pairs(TAILS - R // 8, R // 4, BF16)
         first_grouped = own([P, R], BF16, "first_grouped")[:]
         r_got = {n: own([P, R], F32, "r_got%d" % n)[:] for n in (0, 2)}
-        r_got[3] = in_pairs(LANE0[1], R, F32)
-        dt = {(n, a): own([P, HALF], F32, "dt%d_%d" % (n, a))[:] for n in range(PACK - 1) for a in halves}
+        r_got[3] = pair_tile[:, 2 * (LANE0[2] - P) : 2 * (LANE0[2] - P + R)].bitcast(F32)
+        dt = {(n, a): own([P, HALF], F32, "dt%d_%d" % (n, a))[:] for n in range(2) for a in halves}
         last_dt = own([P, SLOTS], F32, "last_dt")
         passing = pair_words(0, CHUNK)[:, 1, :, 1].rearrange("p (j m) -> p j m", j=2)[:, :, : PASSED // 2]
 
@@ -219,24 +220,33 @@ def tile_attend_gdistm_t_pl_kernel(tc, hT, rT, G, hoffs, roffs, offs, out_0, out
             heads(n)
             gather_r(n + 1)
             operand(n)
-            scalar_step(n)
+            if n == 1:
+                scalar_step(n)
         pool_round(*lane_views(0, LANE0[3], LANE0[4]))
-        nc.scalar.copy(*lane_views(2, LATE_CUT, TAILS))
 
         heads(3)
         nc.vector.tensor_copy(*lane_views(0, LANE0[1], LANE0[2]))
+        pool_round(*lane_views(0, LANE0[4], LANE0[5]))
+        third_dt = own([P, SLOTS], F32, "third_dt", "h_tab3")
+        for a in halves:
+            acc = product(2, a)
+            nc.vector.tensor_copy(third_dt[:, a * HALF : (a + 1) * HALF], acc[:])
+        for a in halves:
+            nc.scalar.activation(places(2, a), third_dt[:, a * HALF : (a + 1) * HALF], copy)
+        store(2)
+        nc.scalar.copy(*lane_views(2, LATE_CUT, TAILS))
         operand(3)
         nc.vector.tensor_copy(*lane_views(0, LANE0[0], LANE0[1]))
         nc.vector.tensor_copy(*lane_views(1, 0, LANE1))
         pool_round(*lane_views(1, LANE1, TAILS))
         pool_round(*lane_views(2, 0, LATE_CUT))
-        pool_round(passing, window[0][:, LANE0[4] :].rearrange("p (j m) -> p j m", j=2))
+        pool_round(passing, window[0][:, LANE0[5] :].rearrange("p (j m) -> p j m", j=2))
         acc = [product(3, a, P) for a in range(PACK)]
         for a in range(PACK):
             nc.vector.tensor_copy(last_dt[:, a * P : (a + 1) * P], acc[a][:])
         nc.vector.tensor_copy(window[3][:].indirect(t_list[:]), last_dt[:])
         store(3)
-        nc.vector.tensor_copy(pair_words(LANE0[4], TAILS)[:, 0, :, 0].rearrange("p (j m) -> p j m", j=2), passing)
+        nc.vector.tensor_copy(pair_words(LANE0[5], TAILS)[:, 0, :, 0].rearrange("p (j m) -> p j m", j=2), passing)
 
         y_grouped = [own([P, PIECES[i + 1] - PIECES[i], PACK], BF16, "y_grouped%d" % i) for i in range(6)]
         y_codes = own([P, TAILS], U32, "y_codes")

@@ -30,7 +30,9 @@ LATE_CUT = 896
 QUERY_CUT = 384
 MIDDLE = TAILS // 2
 PASSED = TAILS - LANE0[5]
-PIECES = (0, 256, 512, 1024, 1536, 1792, 2048)
+PIECES = (0, 256, 512, 1024, 1536, 1792, 1920, 2048)
+VECTOR_WEAVES = (0, 256, 512, 1152)
+SCALAR_WEAVES = (1152, 1536, 1792, 1920, 2048)
 WORD_STORES = (0, 512, 1024, 1536, 1792, 2048)
 
 
@@ -248,13 +250,13 @@ def tile_attend_gdistm_t_pl_kernel(tc, hT, rT, G, hoffs, roffs, offs, out_0, out
         store(3)
         nc.vector.tensor_copy(pair_words(LANE0[5], TAILS)[:, 0, :, 0].rearrange("p (j m) -> p j m", j=2), passing)
 
-        y_grouped = [own([P, PIECES[i + 1] - PIECES[i], PACK], BF16, "y_grouped%d" % i) for i in range(6)]
+        y_grouped = own([P, PACK * TAILS], BF16, "y_grouped")
         y_codes = own([P, TAILS], U32, "y_codes")
         y_scales = own([P, MIDDLE], U8, "y_scales")
 
-        def weave_views(i):
-            dst = y_grouped[i][:].rearrange("p c t -> p (c t)").bitcast(F32).rearrange("p (c u) -> p c u", u=2)
-            return dst, pairs.bitcast(F32).rearrange("p (u c) -> p c u", u=2)[:, PIECES[i] : PIECES[i + 1], :]
+        def weave_views(lo, hi):
+            dst = y_grouped[:, PACK * lo : PACK * hi].bitcast(F32).rearrange("p (c u) -> p c u", u=2)
+            return dst, pairs.bitcast(F32).rearrange("p (u c) -> p c u", u=2)[:, lo:hi, :]
 
         def quantize_planes(i):
             a, b = PIECES[i], PIECES[i + 1]
@@ -262,7 +264,7 @@ def tile_attend_gdistm_t_pl_kernel(tc, hT, rT, G, hoffs, roffs, offs, out_0, out
             nc.vector.quantize_mx(
                 out=y_codes[:, a:b].bitcast(E4M3),
                 scales=y_scales[4 * k :, a - k * MIDDLE : b - k * MIDDLE],
-                in_=y_grouped[i][:].rearrange("p c t -> p (c t)"),
+                in_=y_grouped[:, PACK * a : PACK * b],
             )
             if b in WORD_STORES:
                 first = WORD_STORES[WORD_STORES.index(b) - 1]
@@ -272,13 +274,13 @@ def tile_attend_gdistm_t_pl_kernel(tc, hT, rT, G, hoffs, roffs, offs, out_0, out
         nc.vector.tensor_copy(*lane_views(3, PIECES[1], LATE_CUT))
         nc.scalar.copy(*lane_views(3, LATE_CUT, PIECES[4]))
         nc.scalar.copy(*lane_views(3, PIECES[4], TAILS))
-        for i in (3, 4, 5):
-            nc.scalar.copy(*weave_views(i))
+        for i in range(4):
+            nc.scalar.copy(*weave_views(*SCALAR_WEAVES[i : i + 2]))
         for i in (0, 1):
-            nc.vector.tensor_copy(*weave_views(i))
+            nc.vector.tensor_copy(*weave_views(*VECTOR_WEAVES[i : i + 2]))
         quantize_planes(0)
-        nc.vector.tensor_copy(*weave_views(2))
-        for i in range(1, 6):
+        nc.vector.tensor_copy(*weave_views(*VECTOR_WEAVES[2:]))
+        for i in range(1, 7):
             quantize_planes(i)
         scale_rows = out_scales.rearrange("f (k c) -> k f c", k=2)
         for q in range(4):

from contextlib import ExitStack

import concourse.mybir as mybir
from concourse.masks import make_identity

F32 = mybir.dt.float32
BF16 = mybir.dt.bfloat16
U32 = mybir.dt.uint32
I32 = mybir.dt.int32
U16 = mybir.dt.uint16
U8 = mybir.dt.uint8
E4M3 = mybir.dt.float8_e4m3fn_x4
E5M2 = mybir.dt.float8_e5m2_x4

P = 128
PACK = 4
D = 512
R = 512
SLOTS = 512
HALF = SLOTS // 2
HEADS = 2048
RELS = 1024
TAILS = 2048
CHUNK = 512
FLOPS = 2 * D * R * SLOTS

LANE0 = (0, 160, 352, 832, 1536, 1984)
LANE1 = LANE0[3]
LATE_CUT = 896
QUERY_CUT = 384
MIDDLE = TAILS // 2
PASSED = TAILS - LANE0[5]
PIECES = (0, 256, 512, 1024, 1536, 1792, 1920, 2048)
VECTOR_WEAVES = (0, 256, 512, 1152)
SCALAR_WEAVES = (1152, 1536, 1792, 1920, 2048)
WORD_STORES = (0, 512, 1024, 1536, 1792, 2048)


def tile_attend_gdistm_t_pl_kernel(tc, hT, rT, G, hoffs, roffs, offs, out_0, out_1, out_2):
    nc = tc.nc
    mult = mybir.AluOpType.mult
    add = mybir.AluOpType.add
    copy = mybir.ActivationFunctionType.Copy

    with ExitStack() as ctx:
        lists = ctx.enter_context(tc.tile_pool(name="lists", bufs=1))
        sb = ctx.enter_context(tc.tile_pool(name="sb", bufs=1))
        ps = ctx.enter_context(tc.psum_pool(name="ps", bufs=1))

        h_list = lists.tile([P, R // 16], U16, name="h_list")
        r_list = lists.tile([P, R // 16], U16, name="r_list")
        t_list = lists.tile([P, SLOTS // 16], U16, name="t_list")

        h_rows = hT.rearrange("(p t) c -> p t c", t=PACK)
        r_rows = rT.rearrange("(p t) c -> p t c", t=PACK)
        g_rows = G.rearrange("(q t) i -> q (t i)", t=PACK)
        out_rows = out_0.rearrange("(p t) c -> p t c", t=PACK)
        out_words = out_1[0].rearrange("p c t -> p (c t)").bitcast(I32)
        out_scales = out_2[0].bitcast(I32)

        def own(shape, dtype, name, tag=None):
            return sb.tile(shape, dtype, name=name, tag=tag or name, align_bytes=64)

        h_tab = [own([P, HEADS], F32, "h_tab%d" % n) for n in range(PACK)]
        r_tab = [own([P, RELS], F32, "r_tab%d" % n) for n in range(PACK)]
        g_raw = own([P, PACK * SLOTS], F32, "g_raw")
        window = [own([P, TAILS], F32, "window%d" % n) for n in range(PACK)]

        nc.sync.dma_start(r_tab[0][:], r_rows[:, 0, :])
        nc.sync.dma_start(r_list[:], roffs)
        nc.sync.dma_start(h_list[:], hoffs)
        nc.sync.dma_start(h_tab[0][:], h_rows[:, 0, :])
        nc.sync.dma_start(g_raw[:], g_rows)
        nc.sync.dma_start(r_tab[1][:], r_rows[:, 1, :])
        nc.sync.dma_start(t_list[:], offs)
        nc.sync.dma_start(h_tab[1][:], h_rows[:, 1, :])
        for n in (2, 3):
            nc.sync.dma_start(r_tab[n][:], r_rows[:, n, :])
            nc.sync.dma_start(h_tab[n][:], h_rows[:, n, :])

        ident = own([P, P], F32, "ident")
        make_identity(nc, ident[:])
        nc.vector.memset(window[0][:, : TAILS // 2 + 1], 0.0)
        nc.vector.memset(window[0][:, TAILS // 2 + 1 :], 0.0)
        nc.vector.memset(window[1][:, : TAILS // 2 - 7], 0.0)
        nc.vector.memset(window[1][:, TAILS // 2 - 7 : TAILS // 2], 0.0)
        nc.gpsimd.memset(window[1][:, TAILS // 2 :], 0.0)
        for n in (2, 3):
            nc.gpsimd.memset(window[n][:], 0.0)

        pair_tile = own([P, 2 * QUERY_CUT + PACK * TAILS], BF16, "pair_tile")
        pairs = pair_tile[:, 2 * QUERY_CUT :]

        def pair_words(lo, hi):
            return pairs.rearrange("p (u c e) -> p u c e", u=2, e=2)[:, :, lo:hi, :]

        def in_pairs(col, words, dtype):
            return pairs[:, 2 * col : 2 * (col + words)].bitcast(dtype)

        halves = (0, 1)
        c_scales = [own([P, P], U8, "c_scales%d" % n) for n in range(PACK)]
        c_codes = [own([P, P], U32, "c_codes%d" % n) for n in range(PACK)]
        turned = [ps.tile([P, 2, P], F32, name="turned%d" % n, tag="turned%d" % (n % 2)) for n in range(PACK)]
        g_codes = own([P, SLOTS], U32, "g_codes")
        g_scales = own([P, SLOTS], U8, "g_scales")
        g_grouped = [own([P, HALF, PACK], BF16, "g_grouped%d" % a) for a in halves]
        c_rows = [in_pairs(LANE0[n + 1], R, F32) if n >= 2 else own([P, R], F32, "c_rows%d" % n)[:] for n in range(PACK)]
        c_pairs = [own([P, R], BF16, "c_pairs%d" % n)[:] for n in range(PACK)]
        c_grouped = {(n, a): own([P, R // 2], BF16, "c_grouped%d_%d" % (n, a))[:] for n in (1, 2) for a in halves}
        c_grouped[3, 0] = in_pairs(LANE0[0], R // 4, BF16)
        c_grouped[3, 1] = in_pairs(TAILS - R // 8, R // 4, BF16)
        first_grouped = own([P, R], BF16, "first_grouped")[:]
        r_got = {n: own([P, R], F32, "r_got%d" % n)[:] for n in (0, 2)}
        r_got[3] = pair_tile[:, 2 * (LANE0[2] - P) : 2 * (LANE0[2] - P + R)].bitcast(F32)
        dt = {(n, a): own([P, HALF], F32, "dt%d_%d" % (n, a))[:] for n in range(2) for a in halves}
        last_dt = own([P, SLOTS], F32, "last_dt")
        passing = pair_words(0, CHUNK)[:, 1, :, 1].rearrange("p (j m) -> p j m", j=2)[:, :, : PASSED // 2]

        def gather_r(n):
            nc.vector.tensor_copy(r_got[n], r_tab[n][:].indirect(r_list[:]))

        def gather_h(n, cols):
            nc.vector.tensor_tensor(c_rows[n][:, cols], h_tab[n][:].indirect(h_list[:, cols.start // 16 : cols.stop // 16]), r_got[n][:, cols], mult)

        def c_views(n, cols):
            lo, hi = cols.start, cols.stop
            dst = c_pairs[n].rearrange("p (u q e) -> p u q e", u=2, e=2)[:, :, lo // PACK : hi // PACK, :]
            return dst, c_rows[n][:, lo:hi].rearrange("p (q u e) -> p u q e", u=2, e=2)

        def turn(n):
            for u in range(2):
                nc.tensor.transpose(turned[n][:, u, :], c_pairs[n][:, u * 2 * P : (u + 1) * 2 * P].bitcast(F32), ident[:])

        def group(grouped, n, lo, hi):
            dst = grouped.bitcast(F32).rearrange("q (p u) -> q p u", u=2)
            nc.vector.tensor_copy(dst, turned[n][:, :, lo:hi].rearrange("q u p -> q p u"))

        def quantize_c(grouped, n, lo, hi):
            nc.vector.quantize_mx(out=c_codes[n][:, lo:hi].bitcast(E4M3), scales=c_scales[n][:, lo:hi], in_=grouped)

        def product(n, a, width=HALF):
            cols = slice(a * width, (a + 1) * width)
            acc = ps.tile([P, width], F32, name="acc%d_%d" % (n, a), tag="acc%d" % ((2 * n + a) % 4))
            nc.tensor.matmul_mx(
                out=acc[:],
                lhsT=c_codes[n][:].bitcast(E4M3),
                lhsT_scale=c_scales[n][:],
                rhs=g_codes[:, cols].bitcast(E5M2),
                rhs_scale=g_scales[:, cols],
                start=True,
                stop=True,
            )
            return acc

        def places(n, a):
            return window[n][:].indirect(t_list[:, a * HALF // 16 : (a + 1) * HALF // 16])

        def store(n):
            nc.sync.dma_start(out_rows[:, n, :], window[n][:])

        def scalar_step(n):
            acc = [product(n, a) for a in halves]
            for a in halves:
                nc.scalar.copy(dt[n, a], acc[a][:])
            for a in halves:
                nc.scalar.activation(places(n, a), dt[n, a], copy)
            store(n)

        def lane_views(n, lo, hi):
            return pair_words(lo, hi)[:, n // 2, :, n % 2], window[n][:, lo:hi]

        def pool_round(dst, src):
            nc.gpsimd.tensor_scalar(dst, src, 1.0, -0.0, mult, add)

        def g_views(a, b):
            dst = g_grouped[a][:, b * P : (b + 1) * P, :].rearrange("q (c i) t -> q c t i", i=4)
            rows = g_raw[:].rearrange("q (t c) -> q t c", t=PACK)
            first = a * HALF + b * P
            return dst, rows[:, :, first : first + P].rearrange("q t (c i) -> q c t i", i=4)

        def quantize_g(a):
            cols = slice(a * HALF, (a + 1) * HALF)
            nc.vector.quantize_mx(
                out=g_codes[:, cols].bitcast(E5M2),
                scales=g_scales[:, cols],
                in_=g_grouped[a][:].rearrange("q c t -> q (c t)"),
            )

        def heads(n):
            parts = (slice(0, QUERY_CUT), slice(QUERY_CUT, R))
            for cols in parts:
                gather_h(n, cols)
            for cols in parts:
                nc.vector.tensor_copy(*c_views(n, cols))
            turn(n)

        def operand(n):
            for a in halves:
                group(c_grouped[n, a], n, a * P // 2, (a + 1) * P // 2)
            for a in halves:
                quantize_c(c_grouped[n, a], n, a * P // 2, (a + 1) * P // 2)

        gather_r(0)
        gather_h(0, slice(0, R // 2))
        nc.scalar.copy(*c_views(0, slice(0, R // 2)))
        gather_h(0, slice(R // 2, R))
        nc.vector.tensor_copy(*c_views(0, slice(R // 2, R)))
        turn(0)
        for a in halves:
            nc.vector.tensor_copy(*g_views(a, 0))
            nc.scalar.copy(*g_views(a, 1))
        group(first_grouped, 0, 0, P)
        quantize_g(0)
        quantize_c(first_grouped, 0, 0, P)
        quantize_g(1)
        r_got[1] = own([P, R], F32, "r_got1", "g_grouped0")[:]
        gather_r(1)
        scalar_step(0)
        nc.scalar.copy(*lane_views(0, LANE0[2], LANE0[3]))

        for n in (1, 2):
            heads(n)
            gather_r(n + 1)
            operand(n)
            if n == 1:
                scalar_step(n)
        pool_round(*lane_views(0, LANE0[3], LANE0[4]))

        heads(3)
        nc.vector.tensor_copy(*lane_views(0, LANE0[1], LANE0[2]))
        pool_round(*lane_views(0, LANE0[4], LANE0[5]))
        third_dt = own([P, SLOTS], F32, "third_dt", "h_tab3")
        for a in halves:
            acc = product(2, a)
            nc.vector.tensor_copy(third_dt[:, a * HALF : (a + 1) * HALF], acc[:])
        for a in halves:
            nc.scalar.activation(places(2, a), third_dt[:, a * HALF : (a + 1) * HALF], copy)
        store(2)
        nc.scalar.copy(*lane_views(2, LATE_CUT, TAILS))
        operand(3)
        nc.vector.tensor_copy(*lane_views(0, LANE0[0], LANE0[1]))
        nc.vector.tensor_copy(*lane_views(1, 0, LANE1))
        pool_round(*lane_views(1, LANE1, TAILS))
        pool_round(*lane_views(2, 0, LATE_CUT))
        pool_round(passing, window[0][:, LANE0[5] :].rearrange("p (j m) -> p j m", j=2))
        acc = [product(3, a, P) for a in range(PACK)]
        for a in range(PACK):
            nc.vector.tensor_copy(last_dt[:, a * P : (a + 1) * P], acc[a][:])
        nc.vector.tensor_copy(window[3][:].indirect(t_list[:]), last_dt[:])
        store(3)
        nc.vector.tensor_copy(pair_words(LANE0[5], TAILS)[:, 0, :, 0].rearrange("p (j m) -> p j m", j=2), passing)

        y_grouped = own([P, PACK * TAILS], BF16, "y_grouped")
        y_codes = own([P, TAILS], U32, "y_codes")
        y_scales = own([P, MIDDLE], U8, "y_scales")

        def weave_views(lo, hi):
            dst = y_grouped[:, PACK * lo : PACK * hi].bitcast(F32).rearrange("p (c u) -> p c u", u=2)
            return dst, pairs.bitcast(F32).rearrange("p (u c) -> p c u", u=2)[:, lo:hi, :]

        def quantize_planes(i):
            a, b = PIECES[i], PIECES[i + 1]
            k = a // MIDDLE
            nc.vector.quantize_mx(
                out=y_codes[:, a:b].bitcast(E4M3),
                scales=y_scales[4 * k :, a - k * MIDDLE : b - k * MIDDLE],
                in_=y_grouped[:, PACK * a : PACK * b],
            )
            if b in WORD_STORES:
                first = WORD_STORES[WORD_STORES.index(b) - 1]
                nc.sync.dma_start(out_words[:, first:b], y_codes[:, first:b].bitcast(I32))

        nc.vector.tensor_copy(*lane_views(3, 0, PIECES[1]))
        nc.vector.tensor_copy(*lane_views(3, PIECES[1], LATE_CUT))
        nc.scalar.copy(*lane_views(3, LATE_CUT, PIECES[4]))
        nc.scalar.copy(*lane_views(3, PIECES[4], TAILS))
        for i in range(4):
            nc.scalar.copy(*weave_views(*SCALAR_WEAVES[i : i + 2]))
        for i in (0, 1):
            nc.vector.tensor_copy(*weave_views(*VECTOR_WEAVES[i : i + 2]))
        quantize_planes(0)
        nc.vector.tensor_copy(*weave_views(*VECTOR_WEAVES[2:]))
        for i in range(1, 7):
            quantize_planes(i)
        scale_rows = out_scales.rearrange("f (k c) -> k f c", k=2)
        for q in range(4):
            queue = nc.sync if q < 2 else nc.scalar
            queue.dma_start(scale_rows[:, 4 * q : 4 * q + 4, :], y_scales[32 * q : 32 * q + 8, :].bitcast(I32))
